import numpy as np
import ml_dtypes


def mxq(x, axis, fmt="e4m3"):
    dtype, down = {"e4m3": (ml_dtypes.float8_e4m3fn, 7), "e5m2": (ml_dtypes.float8_e5m2, 14)}[fmt]
    v = np.moveaxis(np.asarray(x, np.float32).astype(ml_dtypes.bfloat16).astype(np.float64), axis, -1)
    blocks = v.reshape(v.shape[:-1] + (-1, 32))
    amax = np.abs(blocks).max(-1, keepdims=True)
    byte = np.maximum(np.where(amax > 0, np.frexp(amax)[1] - 1 + 127, 0) - down, 1)
    scale = np.exp2(byte - 127.0)
    codes = (blocks / scale).astype(np.float32).astype(dtype).astype(np.float64)
    return np.moveaxis((codes * scale).reshape(v.shape), -1, axis)


WIDE = False


def mx_kscale(k):
    if not WIDE:
        return np.ones(k)
    levels = np.array([10, -10, 5, -5, 0])
    if k % 512:
        return np.exp2(np.random.permutation(np.resize(levels, k // 32))).repeat(32)
    a = np.empty((k // 512, 16))
    for p in range(k // 512):
        a[p, :8] = np.random.permutation(np.resize(levels, 8))
        for g in range(8):
            far = levels[np.abs(levels - a[p, g]) >= 10]
            a[p, g + 8] = far[np.random.randint(len(far))]
    return np.exp2(a.ravel()).repeat(32)


def f64(x):
    return np.asarray(x).astype(np.float64)


def striped(idx):
    return np.tile(idx.reshape(-1, 16).T, (8, 1)).astype(np.uint16)


def unstriped(offs):
    return offs[:16].T.reshape(-1).astype(np.int64)


E2M1 = np.array([0.0, 0.5, 1.0, 1.5, 2.0, 3.0, 4.0, 6.0, -0.0, -0.5, -1.0, -1.5, -2.0, -3.0, -4.0, -6.0])


def pack_weight(w, fmt):
    k, n = w.shape
    w = f64(np.asarray(w, np.float32).astype(ml_dtypes.bfloat16)).reshape(k // 32, 32, n)
    amax = np.abs(w).max(1)
    if fmt == "e4m3":
        byte = np.frexp(amax)[1] - 1 + 127 - 7
    else:
        mant, ex = np.frexp(amax / 6.0)
        byte = np.where(mant > 0.5, ex, ex - 1) + 127
    byte = np.clip(np.where(amax > 0, byte, 1), 1, 254)
    scaled = (w * np.exp2(127.0 - byte)[:, None, :]).reshape(k, n).astype(np.float32)
    by_word = np.ascontiguousarray(scaled.reshape(k // 512, 128, 4, n).transpose(0, 1, 3, 2))
    if fmt == "e4m3":
        words = by_word.astype(ml_dtypes.float8_e4m3fn).view(np.uint8)
    else:
        c = by_word.astype(ml_dtypes.float4_e2m1fn).view(np.uint8) & 0xF
        words = (c[..., 0::2] | (c[..., 1::2] << 4)).reshape(k // 512, 128, 2 * n)
    return np.ascontiguousarray(words), np.ascontiguousarray(byte.astype(np.uint8).reshape(k // 512, 16, n))


def unpack_weight(words, scales, fmt):
    g, _, n = scales.shape
    words = np.ascontiguousarray(words).reshape(g, 128, n, -1)
    if fmt == "e4m3":
        vals = words.view(ml_dtypes.float8_e4m3fn).astype(np.float64)
    else:
        nib = np.empty((g, 128, n, 4), np.uint8)
        nib[..., 0::2] = words & 0xF
        nib[..., 1::2] = words >> 4
        vals = E2M1[nib]
    vals = vals * np.repeat(np.exp2(scales.astype(np.float64) - 127.0), 8, axis=1)[..., None]
    return vals.transpose(0, 1, 3, 2).reshape(g * 512, n)


def gelu(v):
    return 0.5 * v * (1.0 + np.tanh(np.sqrt(2.0 / np.pi) * (v + 0.044715 * v**3)))


K, H, N, T, S, T2 = 1024, 1024, 512, 2048, 1024, 2048

def setup_inputs():
    n = np.random.standard_normal
    s = mx_kscale(K)[:, None]
    u = mx_kscale(H)[:, None]
    tab_words, tab_scales = pack_weight(n((K, T)) * s, "e4m3")
    wg_words, wg_scales = pack_weight(n((K, H)) / np.sqrt(K) / s, "e2m1")
    return {
        "tab_words": tab_words, "tab_scales": tab_scales,
        "offs": striped(np.random.permutation(T)[:S]),
        "wv": (n((K, H)) / np.sqrt(K) / s * u.T).astype(np.float32),
        "bv": (0.5 * n(H) * u[:, 0]).astype(np.float32),
        "wg_words": wg_words, "wg_scales": wg_scales,
        "wp": (n((H, N)) / np.sqrt(H) / u).astype(np.float32),
        "wgo": np.exp(0.3 * n((128, S))).astype(np.float32),
        "offs2": striped(np.random.permutation(T2)[:S]),
    }

def reference(tab_words, tab_scales, offs, wv, bv, wg_words, wg_scales, wp, wgo, offs2):
    v = unpack_weight(tab_words, tab_scales, "e4m3")[:, unstriped(offs)]
    wg = unpack_weight(wg_words, wg_scales, "e2m1")
    vel = (mxq(f64(wv), 0, "e4m3").T @ v) + f64(bv)[:, None]
    grad = wg.T @ v
    h = vel * grad
    y = mxq(f64(wp), 0, "e4m3").T @ mxq(h, 0, "e4m3")
    out = np.zeros((N, T2))
    out[:, unstriped(offs2)] = np.tile(f64(wgo), (N // 128, 1)) * y
    return out

@@ -1,0 +1,258 @@
+from contextlib import ExitStack
+
+import concourse.mybir as mybir
+from concourse.masks import make_identity
+
+K, H, N, T, S, T2 = 1024, 1024, 512, 2048, 1024, 2048
+FLOPS = 2 * S * (2 * K * H + H * N)
+
+F32 = mybir.dt.float32
+BF16 = mybir.dt.bfloat16
+I32 = mybir.dt.int32
+U32 = mybir.dt.uint32
+U16 = mybir.dt.uint16
+U8 = mybir.dt.uint8
+FP8X4 = mybir.dt.float8_e4m3fn_x4
+FP4X4 = mybir.dt.float4_e2m1fn_x4
+MULT = mybir.AluOpType.mult
+IDENTITY = mybir.ActivationFunctionType.Identity
+
+P = 128
+PACK = 4
+PASS = P * PACK
+K_PASSES = K // PASS
+R_PASSES = H // PASS
+CHUNK = 512
+CHUNKS = S // CHUNK
+LIST_COLS = CHUNK // 16
+SUB = 128
+N_TILES = N // P
+ON_VECTOR = (("wp", 0), ("wp", 1))
+
+
+def tile_list_mesh_convective_terms_kernel(
+    tc, tab_words, tab_scales, offs, wv, bv, wg_words, wg_scales, wp, wgo, offs2, out
+):
+    nc = tc.nc
+    with ExitStack() as ctx:
+        keep = ctx.enter_context(tc.tile_pool(name="keep", bufs=1))
+        ring = ctx.enter_context(tc.tile_pool(name="ring", bufs=2))
+        psum = ctx.enter_context(tc.psum_pool(name="psum", bufs=1))
+
+        def held(shape, dtype, name):
+            return keep.tile(shape, dtype, name=name, align_bytes=64)
+
+        gather_list = held([P, S // 16], U16, "gather_list")
+        scatter_list = held([P, S // 16], U16, "scatter_list")
+        table = [held([P, T], I32, "table%d" % a) for a in range(K_PASSES)]
+        table_planes = held([P, K_PASSES, T], U8, "table_planes")
+        wg_raw = held([P, K_PASSES, 2 * H], U8, "wg_raw")
+        wg_planes_raw = held([P, K_PASSES, H], U8, "wg_planes_raw")
+
+        def staged(shape, name):
+            return ring.tile(shape, F32, name=name, tag="staged", bufs=3, align_bytes=64)
+
+        wv_raw, wp_raw = {}, {}
+        bias_rows = held([P, P], F32, "bias_rows")
+        identity = staged([P, P], "identity")
+        bias = held([P, R_PASSES * PACK], F32, "bias")
+        store = [held([P, T2], F32, "store%d" % m) for m in range(N_TILES)]
+
+        def words_of(planes):
+            return planes[:].rearrange("p a n -> p (a n)").bitcast(I32)
+
+        nc.vector.memset(words_of(table_planes), 0)
+        nc.gpsimd.memset(bias_rows[:], 0.0)
+        for b in range(R_PASSES):
+            nc.gpsimd.dma_start(
+                out=bias_rows[PACK * b : PACK * (b + 1), :].rearrange("t (q i) -> t q i", i=8),
+                in_=bv[b * PASS : (b + 1) * PASS].rearrange("(q t i) -> t q i", t=PACK, i=8),
+            )
+        make_identity(nc, identity[:])
+        nc.gpsimd.memset(words_of(wg_planes_raw), 0)
+        bias_ps = psum.tile([P, CHUNK], F32, name="bias_ps", tag="y", bufs=2)
+        nc.tensor.transpose(bias_ps[:, 0:P], bias_rows[:], identity[:])
+        nc.scalar.activation(out=bias[:], in_=bias_ps[:, 0 : R_PASSES * PACK], func=IDENTITY)
+
+        def load_planes(queue, planes, scales):
+            for q in range(4):
+                queue.dma_start(
+                    out=planes[32 * q : 32 * q + 4, :, :].bitcast(I32),
+                    in_=scales[:, 4 * q : 4 * q + 4, :].rearrange("a r n -> r a n").bitcast(I32),
+                )
+
+        def load_table(a):
+            nc.sync.dma_start(out=table[a][:], in_=tab_words[a].rearrange("p t i -> p (t i)").bitcast(I32))
+
+        def load_wv(b, a):
+            rows = wv[a * PASS : (a + 1) * PASS, b * PASS : (b + 1) * PASS]
+            wv_raw[b, a] = staged([P, PACK, PASS], "wv_raw%d%d" % (b, a))
+            nc.sync.dma_start(out=wv_raw[b, a][:], in_=rows.rearrange("(p j) c -> p j c", j=PACK))
+
+        def load_wp(b):
+            wp_raw[b] = staged([P, PACK, N], "wp_raw%d" % b)
+            rows = wp[b * PASS : (b + 1) * PASS, :].rearrange("(q t i) n -> t q i n", t=PACK, i=8)
+            for t in range(PACK):
+                nc.sync.dma_start(out=wp_raw[b][:, t, :], in_=rows[t])
+
+        nc.sync.dma_start(gather_list[:], offs)
+        nc.sync.dma_start(scatter_list[:], offs2)
+        load_table(0)
+        load_planes(nc.scalar, table_planes, tab_scales)
+        load_wv(0, 0)
+        load_table(1)
+        load_wv(0, 1)
+        nc.sync.dma_start(out=wg_raw[:].bitcast(I32), in_=wg_words.rearrange("a p n -> p a n").bitcast(I32))
+        load_planes(nc.gpsimd, wg_planes_raw, wg_scales)
+        load_wv(1, 0)
+        load_wv(1, 1)
+        load_wp(0)
+        load_wp(1)
+        masses = staged([P, S], "masses")
+        nc.sync.dma_start(out=masses[:], in_=wgo)
+
+        for m in range(N_TILES):
+            (nc.vector if m < 2 else nc.gpsimd).memset(store[m][:], 0.0)
+
+        v_codes, v_scales = {}, {}
+
+        def gather(c):
+            picks = gather_list[:, c * LIST_COLS : (c + 1) * LIST_COLS]
+            for a in range(K_PASSES):
+                v_codes[c, a] = held([P, CHUNK], U32, "v_codes%d%d" % (c, a))
+                v_scales[c, a] = held([P, CHUNK], U8, "v_scales%d%d" % (c, a))
+                nc.vector.tensor_copy(out=v_scales[c, a][:], in_=table_planes[:, a, :].indirect(picks))
+                nc.vector.tensor_copy(out=v_codes[c, a][:], in_=table[a][:].bitcast(U32).indirect(picks))
+
+        def cast(key, dst, src):
+            if key in ON_VECTOR:
+                nc.vector.tensor_copy(out=dst, in_=src)
+            else:
+                nc.scalar.copy(out=dst, in_=src)
+
+        def quantize(grouped, name):
+            codes = held([P, PASS], U32, name + "_codes")
+            scales = held([P, PASS], U8, name + "_scales")
+            nc.vector.quantize_mx(out=codes[:].bitcast(FP8X4), scales=scales[:], in_=grouped[:])
+            return codes, scales
+
+        wv_q, wp_q, h_q = {}, {}, {}
+
+        def prepare_wv(b):
+            for a in range(K_PASSES):
+                grouped = ring.tile([P, PASS * PACK], BF16, name="grouped", bufs=3, align_bytes=64)
+                cast(
+                    ("wv", b, a),
+                    grouped[:].rearrange("p (t q i j) -> p t q j i", t=PACK, i=8, j=PACK),
+                    wv_raw[b, a][:].rearrange("p j (q t i) -> p t q j i", t=PACK, i=8),
+                )
+                wv_q[b, a] = quantize(grouped, "wv%d%d" % (b, a))
+
+        def prepare_wp(b):
+            grouped = ring.tile([P, PASS * PACK], BF16, name="grouped", bufs=3, align_bytes=64)
+            cast(
+                ("wp", b),
+                grouped[:].rearrange("p (c i t) -> p c t i", t=PACK, i=4),
+                wp_raw[b][:].rearrange("p t (c i) -> p c t i", i=4),
+            )
+            wp_q[b] = quantize(grouped, "wp%d" % b)
+
+        wg_codes = held([P, K_PASSES * 2 * H], U8, "wg_codes")
+        wg_planes = held([P, K_PASSES * H], U8, "wg_planes")
+
+        def permute_wg():
+            nc.vector.tensor_copy(
+                out=wg_codes[:].bitcast(I32).rearrange("p (g t q w) -> p g t q w", t=PACK, q=16, w=4),
+                in_=words_of(wg_raw).rearrange("p (g q t w) -> p g t q w", t=PACK, q=16, w=4),
+            )
+            nc.vector.tensor_copy(
+                out=wg_planes[:].bitcast(I32).rearrange("p (g t q w) -> p g t q w", t=PACK, q=16, w=2),
+                in_=words_of(wg_planes_raw).rearrange("p (g q t w) -> p g t q w", t=PACK, q=16, w=2),
+            )
+
+        def convective(c, b):
+            vel = ring.tile([P, PACK, CHUNK], F32, name="vel")
+            for t in range(PACK):
+                vel_ps = psum.tile([P, CHUNK], F32, name="vel_ps", bufs=3)
+                cols = slice(t * P, (t + 1) * P)
+                for a in range(K_PASSES):
+                    codes, scales = wv_q[b, a]
+                    nc.tensor.matmul_mx(
+                        out=vel_ps[:],
+                        lhsT=codes[:, cols].bitcast(FP8X4),
+                        lhsT_scale=scales[:, cols],
+                        rhs=v_codes[c, a][:].bitcast(FP8X4),
+                        rhs_scale=v_scales[c, a][:],
+                        start=(a == 0),
+                        stop=(a == K_PASSES - 1),
+                    )
+                nc.scalar.activation(
+                    out=vel[:, t, :], in_=vel_ps[:], func=IDENTITY, bias=bias[:, PACK * b + t : PACK * b + t + 1], scale=1.0
+                )
+            h = ring.tile([P, CHUNK * PACK], BF16, name="h", align_bytes=64)
+            for s in range(CHUNK // SUB):
+                grad_ps = psum.tile([P, PACK, SUB], F32, name="grad_ps", bufs=3)
+                picks = slice(s * SUB, (s + 1) * SUB)
+                for t in range(PACK):
+                    for a in range(K_PASSES):
+                        col = a * H + b * PASS + t * P
+                        nc.tensor.matmul_mx(
+                            out=grad_ps[:, t, :],
+                            lhsT=wg_codes[:, 2 * col : 2 * (col + P)].bitcast(FP4X4),
+                            lhsT_scale=wg_planes[:, col : col + P],
+                            rhs=v_codes[c, a][:, picks].bitcast(FP8X4),
+                            rhs_scale=v_scales[c, a][:, picks],
+                            start=(a == 0),
+                            stop=(a == K_PASSES - 1),
+                        )
+                nc.vector.tensor_tensor(
+                    out=h[:, s * SUB * PACK : (s + 1) * SUB * PACK].rearrange("p (e i t) -> p e t i", t=PACK, i=4),
+                    in0=grad_ps[:].rearrange("p t (e i) -> p e t i", i=4),
+                    in1=vel[:, :, picks].rearrange("p t (e i) -> p e t i", i=4),
+                    op=MULT,
+                )
+            h_q[c, b] = quantize(h, "h%d%d" % (c, b))
+
+        y = {}
+
+        def project(c):
+            for m in range(N_TILES):
+                y_ps = psum.tile([P, CHUNK], F32, name="y_ps", tag="y", bufs=2)
+                cols = slice(m * P, (m + 1) * P)
+                for b in range(R_PASSES):
+                    nc.tensor.matmul_mx(
+                        out=y_ps[:],
+                        lhsT=wp_q[b][0][:, cols].bitcast(FP8X4),
+                        lhsT_scale=wp_q[b][1][:, cols],
+                        rhs=h_q[c, b][0][:].bitcast(FP8X4),
+                        rhs_scale=h_q[c, b][1][:],
+                        start=(b == 0),
+                        stop=(b == R_PASSES - 1),
+                    )
+                y[c, m] = held([P, CHUNK], F32, "y%d%d" % (c, m))
+                nc.scalar.copy(out=y[c, m][:], in_=y_ps[:])
+
+        def scatter(c):
+            places = scatter_list[:, c * LIST_COLS : (c + 1) * LIST_COLS]
+            for m in range(N_TILES):
+                nc.vector.tensor_tensor(
+                    out=store[m][:].indirect(places), in0=y[c, m][:], in1=masses[:, c * CHUNK : (c + 1) * CHUNK], op=MULT
+                )
+                if c == CHUNKS - 1:
+                    nc.sync.dma_start(out=out[m * P : (m + 1) * P, :], in_=store[m][:])
+
+        gather(0)
+        prepare_wv(0)
+        permute_wg()
+        convective(0, 0)
+        prepare_wv(1)
+        convective(0, 1)
+        prepare_wp(0)
+        prepare_wp(1)
+        project(0)
+        gather(1)
+        convective(1, 0)
+        convective(1, 1)
+        project(1)
+        scatter(0)
+        scatter(1)

@@ -49,12 +49,13 @@ def tile_list_mesh_convective_terms_kernel(
         wg_raw = held([P, K_PASSES, 2 * H], U8, "wg_raw")
         wg_planes_raw = held([P, K_PASSES, H], U8, "wg_planes_raw")
 
-        def staged(shape, name):
-            return ring.tile(shape, F32, name=name, tag="staged", bufs=3, align_bytes=64)
-
-        wv_raw, wp_raw = {}, {}
-        bias_rows = held([P, P], F32, "bias_rows")
-        identity = staged([P, P], "identity")
+        stage = [held([P, PACK * PASS], F32, "stage%d" % i) for i in range(3)]
+        planes_of = [x[:].rearrange("p (j c) -> p j c", j=PACK) for x in stage]
+        wv_raw = {(b, a): planes_of[(K_PASSES * b + a) % 3] for b in range(R_PASSES) for a in range(K_PASSES)}
+        wp_raw = [planes_of[1 + b] for b in range(R_PASSES)]
+        masses = stage[0][:, 0:S]
+        identity = held([P, P], F32, "identity")[:]
+        bias_rows = stage[2][:, 0:P]
         bias = held([P, R_PASSES * PACK], F32, "bias")
         store = [held([P, T2], F32, "store%d" % m) for m in range(N_TILES)]
 
@@ -62,16 +63,16 @@ def tile_list_mesh_convective_terms_kernel(
             return planes[:].rearrange("p a n -> p (a n)").bitcast(I32)
 
         nc.vector.memset(words_of(table_planes), 0)
-        nc.gpsimd.memset(bias_rows[:], 0.0)
+        nc.gpsimd.memset(bias_rows, 0.0)
         for b in range(R_PASSES):
             nc.gpsimd.dma_start(
                 out=bias_rows[PACK * b : PACK * (b + 1), :].rearrange("t (q i) -> t q i", i=8),
                 in_=bv[b * PASS : (b + 1) * PASS].rearrange("(q t i) -> t q i", t=PACK, i=8),
             )
-        make_identity(nc, identity[:])
+        make_identity(nc, identity)
         nc.gpsimd.memset(words_of(wg_planes_raw), 0)
         bias_ps = psum.tile([P, CHUNK], F32, name="bias_ps", tag="y", bufs=2)
-        nc.tensor.transpose(bias_ps[:, 0:P], bias_rows[:], identity[:])
+        nc.tensor.transpose(bias_ps[:, 0:P], bias_rows, identity)
         nc.scalar.activation(out=bias[:], in_=bias_ps[:, 0 : R_PASSES * PACK], func=IDENTITY)
 
         def load_planes(queue, planes, scales):
@@ -86,11 +87,9 @@ def tile_list_mesh_convective_terms_kernel(
 
         def load_wv(b, a):
             rows = wv[a * PASS : (a + 1) * PASS, b * PASS : (b + 1) * PASS]
-            wv_raw[b, a] = staged([P, PACK, PASS], "wv_raw%d%d" % (b, a))
-            nc.sync.dma_start(out=wv_raw[b, a][:], in_=rows.rearrange("(p j) c -> p j c", j=PACK))
+            nc.sync.dma_start(out=wv_raw[b, a], in_=rows.rearrange("(p j) c -> p j c", j=PACK))
 
         def load_wp(b):
-            wp_raw[b] = staged([P, PACK, N], "wp_raw%d" % b)
             rows = wp[b * PASS : (b + 1) * PASS, :].rearrange("(q t i) n -> t q i n", t=PACK, i=8)
             for t in range(PACK):
                 nc.sync.dma_start(out=wp_raw[b][:, t, :], in_=rows[t])
@@ -100,19 +99,14 @@ def tile_list_mesh_convective_terms_kernel(
         load_table(0)
         load_planes(nc.scalar, table_planes, tab_scales)
         load_wv(0, 0)
-        load_table(1)
         load_wv(0, 1)
+        load_table(1)
         nc.sync.dma_start(out=wg_raw[:].bitcast(I32), in_=wg_words.rearrange("a p n -> p a n").bitcast(I32))
         load_planes(nc.gpsimd, wg_planes_raw, wg_scales)
         load_wv(1, 0)
-        load_wv(1, 1)
-        load_wp(0)
-        load_wp(1)
-        masses = staged([P, S], "masses")
-        nc.sync.dma_start(out=masses[:], in_=wgo)
 
-        for m in range(N_TILES):
-            (nc.vector if m < 2 else nc.gpsimd).memset(store[m][:], 0.0)
+        for m in range(N_TILES - 1):
+            nc.vector.memset(store[m][:], 0.0)
 
         v_codes, v_scales = {}, {}
 
@@ -121,8 +115,8 @@ def tile_list_mesh_convective_terms_kernel(
             for a in range(K_PASSES):
                 v_codes[c, a] = held([P, CHUNK], U32, "v_codes%d%d" % (c, a))
                 v_scales[c, a] = held([P, CHUNK], U8, "v_scales%d%d" % (c, a))
-                nc.vector.tensor_copy(out=v_scales[c, a][:], in_=table_planes[:, a, :].indirect(picks))
                 nc.vector.tensor_copy(out=v_codes[c, a][:], in_=table[a][:].bitcast(U32).indirect(picks))
+                nc.vector.tensor_copy(out=v_scales[c, a][:], in_=table_planes[:, a, :].indirect(picks))
 
         def cast(key, dst, src):
             if key in ON_VECTOR:
@@ -138,22 +132,20 @@ def tile_list_mesh_convective_terms_kernel(
 
         wv_q, wp_q, h_q = {}, {}, {}
 
-        def prepare_wv(b):
-            for a in range(K_PASSES):
-                grouped = ring.tile([P, PASS * PACK], BF16, name="grouped", bufs=3, align_bytes=64)
-                cast(
-                    ("wv", b, a),
-                    grouped[:].rearrange("p (t q i j) -> p t q j i", t=PACK, i=8, j=PACK),
-                    wv_raw[b, a][:].rearrange("p j (q t i) -> p t q j i", t=PACK, i=8),
-                )
-                wv_q[b, a] = quantize(grouped, "wv%d%d" % (b, a))
+        def prepare_wv(b, a):
+            grouped = ring.tile([P, PASS * PACK], BF16, name="grouped", bufs=3, align_bytes=64)
+            dst = grouped[:].rearrange("p (t q u i j) -> p t q u j i", t=PACK, u=2, i=4, j=PACK)
+            src = wv_raw[b, a].rearrange("p j (q t u i) -> p t q u j i", t=PACK, u=2, i=4)
+            for t in range(PACK):
+                cast(("wv", b, a), dst[:, t], src[:, t])
+            wv_q[b, a] = quantize(grouped, "wv%d%d" % (b, a))
 
         def prepare_wp(b):
             grouped = ring.tile([P, PASS * PACK], BF16, name="grouped", bufs=3, align_bytes=64)
             cast(
                 ("wp", b),
                 grouped[:].rearrange("p (c i t) -> p c t i", t=PACK, i=4),
-                wp_raw[b][:].rearrange("p t (c i) -> p c t i", i=4),
+                wp_raw[b].rearrange("p t (c i) -> p c t i", i=4),
             )
             wp_q[b] = quantize(grouped, "wp%d" % b)
 
@@ -212,11 +204,12 @@ def tile_list_mesh_convective_terms_kernel(
                     op=MULT,
                 )
             h_q[c, b] = quantize(h, "h%d%d" % (c, b))
+            return vel
 
         y = {}
 
-        def project(c):
-            for m in range(N_TILES):
+        def project(c, tiles, into=None):
+            for m in tiles:
                 y_ps = psum.tile([P, CHUNK], F32, name="y_ps", tag="y", bufs=2)
                 cols = slice(m * P, (m + 1) * P)
                 for b in range(R_PASSES):
@@ -229,30 +222,38 @@ def tile_list_mesh_convective_terms_kernel(
                         start=(b == 0),
                         stop=(b == R_PASSES - 1),
                     )
-                y[c, m] = held([P, CHUNK], F32, "y%d%d" % (c, m))
-                nc.scalar.copy(out=y[c, m][:], in_=y_ps[:])
+                y[c, m] = held([P, CHUNK], F32, "y%d%d" % (c, m))[:] if into is None else into
+                nc.scalar.copy(out=y[c, m], in_=y_ps[:])
 
         def scatter(c):
             places = scatter_list[:, c * LIST_COLS : (c + 1) * LIST_COLS]
             for m in range(N_TILES):
                 nc.vector.tensor_tensor(
-                    out=store[m][:].indirect(places), in0=y[c, m][:], in1=masses[:, c * CHUNK : (c + 1) * CHUNK], op=MULT
+                    out=store[m][:].indirect(places), in0=y[c, m], in1=masses[:, c * CHUNK : (c + 1) * CHUNK], op=MULT
                 )
                 if c == CHUNKS - 1:
                     nc.sync.dma_start(out=out[m * P : (m + 1) * P, :], in_=store[m][:])
 
         gather(0)
-        prepare_wv(0)
+        prepare_wv(0, 0)
+        load_wv(1, 1)
+        prepare_wv(0, 1)
+        load_wp(0)
         permute_wg()
         convective(0, 0)
-        prepare_wv(1)
+        gather(1)
+        convective(1, 0)
+        prepare_wv(1, 0)
+        load_wp(1)
+        prepare_wv(1, 1)
+        nc.sync.dma_start(out=masses, in_=wgo)
         convective(0, 1)
         prepare_wp(0)
         prepare_wp(1)
-        project(0)
-        gather(1)
-        convective(1, 0)
-        convective(1, 1)
-        project(1)
+        project(0, range(N_TILES - 1))
+        last_vel = convective(1, 1)
+        project(0, [N_TILES - 1], last_vel[:, 0, :])
+        project(1, range(N_TILES))
+        nc.vector.memset(store[N_TILES - 1][:], 0.0)
         scatter(0)
         scatter(1)

@@ -15,6 +15,7 @@ U8 = mybir.dt.uint8
 FP8X4 = mybir.dt.float8_e4m3fn_x4
 FP4X4 = mybir.dt.float4_e2m1fn_x4
 MULT = mybir.AluOpType.mult
+ADD = mybir.AluOpType.add
 IDENTITY = mybir.ActivationFunctionType.Identity
 
 P = 128
@@ -27,7 +28,6 @@ CHUNKS = S // CHUNK
 LIST_COLS = CHUNK // 16
 SUB = 128
 N_TILES = N // P
-ON_VECTOR = (("wp", 0), ("wp", 1))
 
 
 def tile_list_mesh_convective_terms_kernel(
@@ -37,14 +37,18 @@ def tile_list_mesh_convective_terms_kernel(
     with ExitStack() as ctx:
         keep = ctx.enter_context(tc.tile_pool(name="keep", bufs=1))
         ring = ctx.enter_context(tc.tile_pool(name="ring", bufs=2))
+        shared = ctx.enter_context(tc.tile_pool(name="shared", bufs=1))
         psum = ctx.enter_context(tc.psum_pool(name="psum", bufs=1))
 
         def held(shape, dtype, name):
             return keep.tile(shape, dtype, name=name, align_bytes=64)
 
+        def placed(shape, dtype, name, offset):
+            return shared.tile(shape, dtype, name=name, align_bytes=64, offset=offset)
+
         gather_list = held([P, S // 16], U16, "gather_list")
         scatter_list = held([P, S // 16], U16, "scatter_list")
-        table = [held([P, T], I32, "table%d" % a) for a in range(K_PASSES)]
+        table = [held([P, T], I32, "table0"), placed([P, T], I32, "table1", 8192)]
         table_planes = held([P, K_PASSES, T], U8, "table_planes")
         wg_raw = held([P, K_PASSES, 2 * H], U8, "wg_raw")
         wg_planes_raw = held([P, K_PASSES, H], U8, "wg_planes_raw")
@@ -57,12 +61,13 @@ def tile_list_mesh_convective_terms_kernel(
         identity = held([P, P], F32, "identity")[:]
         bias_rows = stage[2][:, 0:P]
         bias = held([P, R_PASSES * PACK], F32, "bias")
-        store = [held([P, T2], F32, "store%d" % m) for m in range(N_TILES)]
+        store = [held([P, T2], F32, "store%d" % m) for m in range(N_TILES - 1)] + [placed([P, T2], F32, "store3", 8192)]
 
         def words_of(planes):
             return planes[:].rearrange("p a n -> p (a n)").bitcast(I32)
 
-        nc.vector.memset(words_of(table_planes), 0)
+        nc.vector.memset(table_planes[:, 0, :].bitcast(I32), 0)
+        nc.gpsimd.memset(table_planes[:, 1, :].bitcast(I32), 0)
         nc.gpsimd.memset(bias_rows, 0.0)
         for b in range(R_PASSES):
             nc.gpsimd.dma_start(
@@ -71,7 +76,7 @@ def tile_list_mesh_convective_terms_kernel(
             )
         make_identity(nc, identity)
         nc.gpsimd.memset(words_of(wg_planes_raw), 0)
-        bias_ps = psum.tile([P, CHUNK], F32, name="bias_ps", tag="y", bufs=2)
+        bias_ps = psum.tile([P, CHUNK], F32, name="bias_ps", tag="y", bufs=1)
         nc.tensor.transpose(bias_ps[:, 0:P], bias_rows, identity)
         nc.scalar.activation(out=bias[:], in_=bias_ps[:, 0 : R_PASSES * PACK], func=IDENTITY)
 
@@ -110,46 +115,65 @@ def tile_list_mesh_convective_terms_kernel(
 
         v_codes, v_scales = {}, {}
 
-        def gather(c):
-            picks = gather_list[:, c * LIST_COLS : (c + 1) * LIST_COLS]
-            for a in range(K_PASSES):
-                v_codes[c, a] = held([P, CHUNK], U32, "v_codes%d%d" % (c, a))
-                v_scales[c, a] = held([P, CHUNK], U8, "v_scales%d%d" % (c, a))
-                nc.vector.tensor_copy(out=v_codes[c, a][:], in_=table[a][:].bitcast(U32).indirect(picks))
-                nc.vector.tensor_copy(out=v_scales[c, a][:], in_=table_planes[:, a, :].indirect(picks))
+        def picks_of(c):
+            return gather_list[:, c * LIST_COLS : (c + 1) * LIST_COLS]
 
-        def cast(key, dst, src):
-            if key in ON_VECTOR:
-                nc.vector.tensor_copy(out=dst, in_=src)
+        def gather_codes(c, a):
+            name = "v_codes%d%d" % (c, a)
+            v_codes[c, a] = placed([P, CHUNK], U32, name, 4 * CHUNK * c) if a == 1 else held([P, CHUNK], U32, name)
+            nc.vector.tensor_copy(out=v_codes[c, a][:], in_=table[a][:].bitcast(U32).indirect(picks_of(c)))
+
+        def gather_scales(c, a):
+            v_scales[c, a] = held([P, CHUNK], U8, "v_scales%d%d" % (c, a))
+            nc.vector.tensor_copy(out=v_scales[c, a][:], in_=table_planes[:, a, :].indirect(picks_of(c)))
+
+        def quantize(grouped, codes, scales):
+            nc.vector.quantize_mx(out=codes[:].bitcast(FP8X4), scales=scales[:], in_=grouped)
+            return codes[:], scales[:]
+
+        def quantize_held(grouped, name):
+            return quantize(grouped, held([P, PASS], U32, name + "_codes"), held([P, PASS], U8, name + "_scales"))
+
+        def quantize_wv(b):
+            width = K_PASSES * PASS
+            if b == 0:
+                tiles = held([P, width], U32, "wv0_codes"), held([P, width], U8, "wv0_scales")
             else:
-                nc.scalar.copy(out=dst, in_=src)
-
-        def quantize(grouped, name):
-            codes = held([P, PASS], U32, name + "_codes")
-            scales = held([P, PASS], U8, name + "_scales")
-            nc.vector.quantize_mx(out=codes[:].bitcast(FP8X4), scales=scales[:], in_=grouped[:])
-            return codes, scales
+                tiles = placed([P, width], U32, "wv1_codes", 16384), placed([P, width], U8, "wv1_scales", 16384 + 4 * width)
+            codes, scales = quantize(wv_half[b][:], *tiles)
+            for a in range(K_PASSES):
+                wv_q[b, a] = codes[:, a * PASS : (a + 1) * PASS], scales[:, a * PASS : (a + 1) * PASS]
 
         wv_q, wp_q, h_q = {}, {}, {}
 
-        def prepare_wv(b, a):
-            grouped = ring.tile([P, PASS * PACK], BF16, name="grouped", bufs=3, align_bytes=64)
-            dst = grouped[:].rearrange("p (t q u i j) -> p t q u j i", t=PACK, u=2, i=4, j=PACK)
+        wv_half = [
+            placed([P, K_PASSES * PASS * PACK], BF16, "wv_bf0", 0),
+            held([P, K_PASSES * PASS * PACK], BF16, "wv_bf1"),
+        ]
+        wv_bf = {(b, a): wv_half[b][:, a * PASS * PACK : (a + 1) * PASS * PACK] for b in range(R_PASSES) for a in range(K_PASSES)}
+        h_bf = {(c, b): held([P, CHUNK * PACK], BF16, "h%d%d" % (c, b)) for c in range(CHUNKS) for b in range(R_PASSES)}
+        wp_bf = [h_bf[b, 0] for b in range(R_PASSES)]
+
+        def cast_wv(b, a):
+            dst = wv_bf[b, a].rearrange("p (t q u i j) -> p t q u j i", t=PACK, u=2, i=4, j=PACK)
             src = wv_raw[b, a].rearrange("p j (q t u i) -> p t q u j i", t=PACK, u=2, i=4)
             for t in range(PACK):
-                cast(("wv", b, a), dst[:, t], src[:, t])
-            wv_q[b, a] = quantize(grouped, "wv%d%d" % (b, a))
+                nc.scalar.copy(out=dst[:, t], in_=src[:, t])
+
+        def cast_wv_gpsimd(b, a):
+            dst = wv_bf[b, a].rearrange("p (t q i j) -> p t q i j", t=PACK, i=8, j=PACK)
+            src = wv_raw[b, a].rearrange("p j (q t i) -> p t q i j", t=PACK, i=8)
+            for t in range(PACK):
+                nc.gpsimd.tensor_scalar(out=dst[:, t], in0=src[:, t], scalar1=1.0, scalar2=0.0, op0=MULT, op1=ADD)
 
         def prepare_wp(b):
-            grouped = ring.tile([P, PASS * PACK], BF16, name="grouped", bufs=3, align_bytes=64)
-            cast(
-                ("wp", b),
-                grouped[:].rearrange("p (c i t) -> p c t i", t=PACK, i=4),
-                wp_raw[b].rearrange("p t (c i) -> p c t i", i=4),
-            )
-            wp_q[b] = quantize(grouped, "wp%d" % b)
+            dst = wp_bf[b][:].rearrange("p (u c i t) -> p u c t i", u=PACK, t=PACK, i=4)
+            src = wp_raw[b].rearrange("p t (u c i) -> p u c t i", u=PACK, i=4)
+            for u in range(PACK):
+                nc.scalar.copy(out=dst[:, u], in_=src[:, u])
+            wp_q[b] = quantize_held(wp_bf[b][:], "wp%d" % b)
 
-        wg_codes = held([P, K_PASSES * 2 * H], U8, "wg_codes")
+        wg_codes = placed([P, K_PASSES * 2 * H], U8, "wg_codes", 4096)
         wg_planes = held([P, K_PASSES * H], U8, "wg_planes")
 
         def permute_wg():
@@ -163,7 +187,10 @@ def tile_list_mesh_convective_terms_kernel(
             )
 
         def convective(c, b):
-            vel = ring.tile([P, PACK, CHUNK], F32, name="vel")
+            if (c, b) == (0, 0):
+                vel = placed([P, PACK, CHUNK], F32, "vel_first", 16384)
+            else:
+                vel = ring.tile([P, PACK, CHUNK], F32, name="vel")
             for t in range(PACK):
                 vel_ps = psum.tile([P, CHUNK], F32, name="vel_ps", bufs=3)
                 cols = slice(t * P, (t + 1) * P)
@@ -181,9 +208,9 @@ def tile_list_mesh_convective_terms_kernel(
                 nc.scalar.activation(
                     out=vel[:, t, :], in_=vel_ps[:], func=IDENTITY, bias=bias[:, PACK * b + t : PACK * b + t + 1], scale=1.0
                 )
-            h = ring.tile([P, CHUNK * PACK], BF16, name="h", align_bytes=64)
+            h = h_bf[c, b]
             for s in range(CHUNK // SUB):
-                grad_ps = psum.tile([P, PACK, SUB], F32, name="grad_ps", bufs=3)
+                grad_ps = psum.tile([P, PACK, SUB], F32, name="grad_ps", bufs=4)
                 picks = slice(s * SUB, (s + 1) * SUB)
                 for t in range(PACK):
                     for a in range(K_PASSES):
@@ -203,22 +230,22 @@ def tile_list_mesh_convective_terms_kernel(
                     in1=vel[:, :, picks].rearrange("p t (e i) -> p e t i", i=4),
                     op=MULT,
                 )
-            h_q[c, b] = quantize(h, "h%d%d" % (c, b))
+            h_q[c, b] = quantize_held(h[:], "h%d%d" % (c, b))
             return vel
 
         y = {}
 
         def project(c, tiles, into=None):
             for m in tiles:
-                y_ps = psum.tile([P, CHUNK], F32, name="y_ps", tag="y", bufs=2)
+                y_ps = psum.tile([P, CHUNK], F32, name="y_ps", tag="y", bufs=1)
                 cols = slice(m * P, (m + 1) * P)
                 for b in range(R_PASSES):
                     nc.tensor.matmul_mx(
                         out=y_ps[:],
                         lhsT=wp_q[b][0][:, cols].bitcast(FP8X4),
                         lhsT_scale=wp_q[b][1][:, cols],
-                        rhs=h_q[c, b][0][:].bitcast(FP8X4),
-                        rhs_scale=h_q[c, b][1][:],
+                        rhs=h_q[c, b][0].bitcast(FP8X4),
+                        rhs_scale=h_q[c, b][1],
                         start=(b == 0),
                         stop=(b == R_PASSES - 1),
                     )
@@ -234,19 +261,27 @@ def tile_list_mesh_convective_terms_kernel(
                 if c == CHUNKS - 1:
                     nc.sync.dma_start(out=out[m * P : (m + 1) * P, :], in_=store[m][:])
 
-        gather(0)
-        prepare_wv(0, 0)
+        gather_codes(0, 0)
+        gather_codes(1, 0)
+        gather_scales(0, 0)
+        gather_scales(0, 1)
+        gather_scales(1, 0)
+        gather_scales(1, 1)
+        cast_wv(0, 0)
         load_wv(1, 1)
-        prepare_wv(0, 1)
+        cast_wv(0, 1)
         load_wp(0)
+        quantize_wv(0)
+        gather_codes(0, 1)
         permute_wg()
+        gather_codes(1, 1)
         convective(0, 0)
-        gather(1)
-        convective(1, 0)
-        prepare_wv(1, 0)
+        cast_wv_gpsimd(1, 0)
         load_wp(1)
-        prepare_wv(1, 1)
+        cast_wv_gpsimd(1, 1)
         nc.sync.dma_start(out=masses, in_=wgo)
+        quantize_wv(1)
+        convective(1, 0)
         convective(0, 1)
         prepare_wp(0)
         prepare_wp(1)

@@ -15,7 +15,6 @@ U8 = mybir.dt.uint8
 FP8X4 = mybir.dt.float8_e4m3fn_x4
 FP4X4 = mybir.dt.float4_e2m1fn_x4
 MULT = mybir.AluOpType.mult
-ADD = mybir.AluOpType.add
 IDENTITY = mybir.ActivationFunctionType.Identity
 
 P = 128
@@ -51,7 +50,7 @@ def tile_list_mesh_convective_terms_kernel(
         table = [held([P, T], I32, "table0"), placed([P, T], I32, "table1", 8192)]
         table_planes = held([P, K_PASSES, T], U8, "table_planes")
         wg_raw = held([P, K_PASSES, 2 * H], U8, "wg_raw")
-        wg_planes_raw = held([P, K_PASSES, H], U8, "wg_planes_raw")
+        wg_planes_raw = placed([P, K_PASSES, H], U8, "wg_planes_raw", 24576)
 
         stage = [held([P, PACK * PASS], F32, "stage%d" % i) for i in range(3)]
         planes_of = [x[:].rearrange("p (j c) -> p j c", j=PACK) for x in stage]
@@ -120,7 +119,7 @@ def tile_list_mesh_convective_terms_kernel(
 
         def gather_codes(c, a):
             name = "v_codes%d%d" % (c, a)
-            v_codes[c, a] = placed([P, CHUNK], U32, name, 4 * CHUNK * c) if a == 1 else held([P, CHUNK], U32, name)
+            v_codes[c, a] = placed([P, CHUNK], U32, name, 24576 * c) if a == 1 else held([P, CHUNK], U32, name)
             nc.vector.tensor_copy(out=v_codes[c, a][:], in_=table[a][:].bitcast(U32).indirect(picks_of(c)))
 
         def gather_scales(c, a):
@@ -134,23 +133,22 @@ def tile_list_mesh_convective_terms_kernel(
         def quantize_held(grouped, name):
             return quantize(grouped, held([P, PASS], U32, name + "_codes"), held([P, PASS], U8, name + "_scales"))
 
-        def quantize_wv(b):
+        def quantize_first_half():
             width = K_PASSES * PASS
-            if b == 0:
-                tiles = held([P, width], U32, "wv0_codes"), held([P, width], U8, "wv0_scales")
-            else:
-                tiles = placed([P, width], U32, "wv1_codes", 16384), placed([P, width], U8, "wv1_scales", 16384 + 4 * width)
-            codes, scales = quantize(wv_half[b][:], *tiles)
+            codes, scales = quantize(first_half[:], held([P, width], U32, "wv0_codes"), held([P, width], U8, "wv0_scales"))
             for a in range(K_PASSES):
-                wv_q[b, a] = codes[:, a * PASS : (a + 1) * PASS], scales[:, a * PASS : (a + 1) * PASS]
+                wv_q[0, a] = codes[:, a * PASS : (a + 1) * PASS], scales[:, a * PASS : (a + 1) * PASS]
+
+        def quantize_second_half():
+            tiles = placed([P, PASS], U32, "wv10_codes", 20480), placed([P, PASS], U8, "wv10_scales", 22528)
+            wv_q[1, 0] = quantize(wv_bf[1, 0], *tiles)
 
         wv_q, wp_q, h_q = {}, {}, {}
 
-        wv_half = [
-            placed([P, K_PASSES * PASS * PACK], BF16, "wv_bf0", 0),
-            held([P, K_PASSES * PASS * PACK], BF16, "wv_bf1"),
-        ]
-        wv_bf = {(b, a): wv_half[b][:, a * PASS * PACK : (a + 1) * PASS * PACK] for b in range(R_PASSES) for a in range(K_PASSES)}
+        first_half = placed([P, K_PASSES * PASS * PACK], BF16, "wv_bf0", 0)
+        wv_bf = {(0, a): first_half[:, a * PASS * PACK : (a + 1) * PASS * PACK] for a in range(K_PASSES)}
+        wv_bf[1, 0] = placed([P, PASS * PACK], BF16, "wv_bf10", 8192)[:]
+        wv_bf[1, 1] = placed([P, PASS * PACK], BF16, "wv_bf11", 16384)[:]
         h_bf = {(c, b): held([P, CHUNK * PACK], BF16, "h%d%d" % (c, b)) for c in range(CHUNKS) for b in range(R_PASSES)}
         wp_bf = [h_bf[b, 0] for b in range(R_PASSES)]
 
@@ -160,11 +158,11 @@ def tile_list_mesh_convective_terms_kernel(
             for t in range(PACK):
                 nc.scalar.copy(out=dst[:, t], in_=src[:, t])
 
-        def cast_wv_gpsimd(b, a):
-            dst = wv_bf[b, a].rearrange("p (t q i j) -> p t q i j", t=PACK, i=8, j=PACK)
-            src = wv_raw[b, a].rearrange("p j (q t i) -> p t q i j", t=PACK, i=8)
-            for t in range(PACK):
-                nc.gpsimd.tensor_scalar(out=dst[:, t], in0=src[:, t], scalar1=1.0, scalar2=0.0, op0=MULT, op1=ADD)
+        def cast_wv_vector(b, a):
+            nc.vector.tensor_copy(
+                out=wv_bf[b, a].rearrange("p (t q i j) -> p t q j i", t=PACK, i=8, j=PACK),
+                in_=wv_raw[b, a].rearrange("p j (q t i) -> p t q j i", t=PACK, i=8),
+            )
 
         def prepare_wp(b):
             dst = wp_bf[b][:].rearrange("p (u c i t) -> p u c t i", u=PACK, t=PACK, i=4)
@@ -174,7 +172,7 @@ def tile_list_mesh_convective_terms_kernel(
             wp_q[b] = quantize_held(wp_bf[b][:], "wp%d" % b)
 
         wg_codes = placed([P, K_PASSES * 2 * H], U8, "wg_codes", 4096)
-        wg_planes = held([P, K_PASSES * H], U8, "wg_planes")
+        wg_planes = placed([P, K_PASSES * H], U8, "wg_planes", 2048)
 
         def permute_wg():
             nc.vector.tensor_copy(
@@ -271,17 +269,18 @@ def tile_list_mesh_convective_terms_kernel(
         load_wv(1, 1)
         cast_wv(0, 1)
         load_wp(0)
-        quantize_wv(0)
+        quantize_first_half()
         gather_codes(0, 1)
         permute_wg()
         gather_codes(1, 1)
         convective(0, 0)
-        cast_wv_gpsimd(1, 0)
+        cast_wv_vector(1, 0)
         load_wp(1)
-        cast_wv_gpsimd(1, 1)
+        cast_wv_vector(1, 1)
         nc.sync.dma_start(out=masses, in_=wgo)
-        quantize_wv(1)
+        quantize_second_half()
         convective(1, 0)
+        wv_q[1, 1] = quantize_held(wv_bf[1, 1], "wv11")
         convective(0, 1)
         prepare_wp(0)
         prepare_wp(1)

@@ -22,11 +22,11 @@ PACK = 4
 PASS = P * PACK
 K_PASSES = K // PASS
 R_PASSES = H // PASS
-CHUNK = 512
+CHUNK = 256
 CHUNKS = S // CHUNK
-LIST_COLS = CHUNK // 16
 SUB = 128
 N_TILES = N // P
+BANK = 512
 
 
 def tile_list_mesh_convective_terms_kernel(
@@ -35,7 +35,6 @@ def tile_list_mesh_convective_terms_kernel(
     nc = tc.nc
     with ExitStack() as ctx:
         keep = ctx.enter_context(tc.tile_pool(name="keep", bufs=1))
-        ring = ctx.enter_context(tc.tile_pool(name="ring", bufs=2))
         shared = ctx.enter_context(tc.tile_pool(name="shared", bufs=1))
         psum = ctx.enter_context(tc.psum_pool(name="psum", bufs=1))
 
@@ -48,246 +47,273 @@ def tile_list_mesh_convective_terms_kernel(
         gather_list = held([P, S // 16], U16, "gather_list")
         scatter_list = held([P, S // 16], U16, "scatter_list")
         table = [held([P, T], I32, "table0"), placed([P, T], I32, "table1", 8192)]
-        table_planes = held([P, K_PASSES, T], U8, "table_planes")
+        table_planes = held([P, T], U8, "table_planes")
         wg_raw = held([P, K_PASSES, 2 * H], U8, "wg_raw")
-        wg_planes_raw = placed([P, K_PASSES, H], U8, "wg_planes_raw", 24576)
-
-        stage = [held([P, PACK * PASS], F32, "stage%d" % i) for i in range(3)]
-        planes_of = [x[:].rearrange("p (j c) -> p j c", j=PACK) for x in stage]
-        wv_raw = {(b, a): planes_of[(K_PASSES * b + a) % 3] for b in range(R_PASSES) for a in range(K_PASSES)}
-        wp_raw = [planes_of[1 + b] for b in range(R_PASSES)]
-        masses = stage[0][:, 0:S]
+        wg_planes_raw = held([P, K_PASSES, H], U8, "wg_planes_raw")
+        masses = placed([P, S], F32, "masses", 26624)
         identity = held([P, P], F32, "identity")[:]
-        bias_rows = stage[2][:, 0:P]
+        bias_rows = placed([P, R_PASSES * P], F32, "bias_rows", 26112)
         bias = held([P, R_PASSES * PACK], F32, "bias")
-        store = [held([P, T2], F32, "store%d" % m) for m in range(N_TILES - 1)] + [placed([P, T2], F32, "store3", 8192)]
+        store = [held([P, T2], F32, "store%d" % m) for m in range(N_TILES)]
+        v_codes = [held([P, S], U32, "v_codes%d" % a) for a in range(K_PASSES)]
+        v_planes = held([P, S], U8, "v_planes")
+        v_plane1 = held([P, S], U8, "v_plane1")
+
+        scalar_banks = [psum.tile([P, BANK], F32, name="scalar_bank%d" % i) for i in range(4)]
+        vector_banks = [psum.tile([P, PACK, SUB], F32, name="vector_bank%d" % i) for i in range(4)]
+        turns = {"scalar": 0, "vector": 0, "vel": 0, "h": 0, "y": 0}
+
+        def in_turn(kind, tiles):
+            turns[kind] = turns[kind] + 1
+            return tiles[(turns[kind] - 1) % len(tiles)]
 
         def words_of(planes):
             return planes[:].rearrange("p a n -> p (a n)").bitcast(I32)
 
-        nc.vector.memset(table_planes[:, 0, :].bitcast(I32), 0)
-        nc.gpsimd.memset(table_planes[:, 1, :].bitcast(I32), 0)
-        nc.gpsimd.memset(bias_rows, 0.0)
-        for b in range(R_PASSES):
-            nc.gpsimd.dma_start(
-                out=bias_rows[PACK * b : PACK * (b + 1), :].rearrange("t (q i) -> t q i", i=8),
-                in_=bv[b * PASS : (b + 1) * PASS].rearrange("(q t i) -> t q i", t=PACK, i=8),
-            )
+        nc.gpsimd.memset(table_planes[:].bitcast(I32), 0)
+        nc.vector.memset(words_of(wg_planes_raw), 0)
+        nc.vector.memset(v_plane1[:].bitcast(I32), 0)
+        for rows in (slice(0, 28), slice(32, 64), slice(64, P)):
+            nc.gpsimd.memset(bias_rows[rows, :], 0.0)
         make_identity(nc, identity)
-        nc.gpsimd.memset(words_of(wg_planes_raw), 0)
-        bias_ps = psum.tile([P, CHUNK], F32, name="bias_ps", tag="y", bufs=1)
-        nc.tensor.transpose(bias_ps[:, 0:P], bias_rows, identity)
-        nc.scalar.activation(out=bias[:], in_=bias_ps[:, 0 : R_PASSES * PACK], func=IDENTITY)
-
-        def load_planes(queue, planes, scales):
-            for q in range(4):
-                queue.dma_start(
-                    out=planes[32 * q : 32 * q + 4, :, :].bitcast(I32),
-                    in_=scales[:, 4 * q : 4 * q + 4, :].rearrange("a r n -> r a n").bitcast(I32),
-                )
 
         def load_table(a):
             nc.sync.dma_start(out=table[a][:], in_=tab_words[a].rearrange("p t i -> p (t i)").bitcast(I32))
 
-        def load_wv(b, a):
-            rows = wv[a * PASS : (a + 1) * PASS, b * PASS : (b + 1) * PASS]
-            nc.sync.dma_start(out=wv_raw[b, a], in_=rows.rearrange("(p j) c -> p j c", j=PACK))
+        wv_raw = {}
 
-        def load_wp(b):
-            rows = wp[b * PASS : (b + 1) * PASS, :].rearrange("(q t i) n -> t q i n", t=PACK, i=8)
-            for t in range(PACK):
-                nc.sync.dma_start(out=wp_raw[b][:, t, :], in_=rows[t])
+        def load_wv(b, a, first, width, offset):
+            wv_raw[b, a, first] = placed([P, PACK, width], F32, "wv_raw%d%d%d" % (b, a, first), offset)
+            rows = wv[a * PASS : (a + 1) * PASS, b * PASS + first : b * PASS + first + width]
+            nc.sync.dma_start(out=wv_raw[b, a, first][:], in_=rows.rearrange("(p j) c -> p j c", j=PACK))
+
+        wp_raw = {}
+
+        def load_wp(half, offset):
+            width = N // 2
+            for b in range(R_PASSES):
+                wp_raw[b, half] = placed([P, PACK, width], F32, "wp_raw%d%d" % (b, half), offset + 4096 * b)
+                rows = wp[b * PASS : (b + 1) * PASS, half * width : (half + 1) * width]
+                rows = rows.rearrange("(q t i) n -> t q i n", t=PACK, i=8)
+                for t in range(PACK):
+                    nc.sync.dma_start(out=wp_raw[b, half][:, t, :], in_=rows[t])
 
         nc.sync.dma_start(gather_list[:], offs)
-        nc.sync.dma_start(scatter_list[:], offs2)
+        nc.sync.dma_start(
+            out=bias_rows[28:32, :].rearrange("t (g i) -> t g i", i=8),
+            in_=bv.rearrange("(g t i) -> t g i", t=PACK, i=8),
+        )
         load_table(0)
-        load_planes(nc.scalar, table_planes, tab_scales)
-        load_wv(0, 0)
-        load_wv(0, 1)
         load_table(1)
         nc.sync.dma_start(out=wg_raw[:].bitcast(I32), in_=wg_words.rearrange("a p n -> p a n").bitcast(I32))
-        load_planes(nc.gpsimd, wg_planes_raw, wg_scales)
-        load_wv(1, 0)
+        nc.sync.dma_start(scatter_list[:], offs2)
+        for q in range(4):
+            nc.sync.dma_start(
+                out=table_planes[32 * q : 32 * q + 8, :].bitcast(I32),
+                in_=tab_scales[:, 4 * q : 4 * q + 4, :].bitcast(I32),
+            )
+        for q in range(4):
+            nc.gpsimd.dma_start(
+                out=wg_planes_raw[32 * q : 32 * q + 4, :, :].bitcast(I32),
+                in_=wg_scales[:, 4 * q : 4 * q + 4, :].rearrange("a r n -> r a n").bitcast(I32),
+            )
+        for m in range(N_TILES // 2, N_TILES):
+            nc.gpsimd.memset(store[m][:], 0.0)
+        bias_ps = in_turn("scalar", scalar_banks)
+        for b in range(R_PASSES):
+            nc.tensor.transpose(bias_ps[:, b * P : (b + 1) * P], bias_rows[:, b * P : (b + 1) * P], identity)
+        nc.scalar.activation(
+            out=bias[:].rearrange("p (b t) -> p b t", t=PACK),
+            in_=bias_ps[:, 0 : R_PASSES * P].rearrange("p (b c) -> p b c", c=P)[:, :, 28:32],
+            func=IDENTITY,
+        )
+        load_wv(0, 0, 0, PASS, 18432)
+        load_wv(0, 1, 0, PASS, 26624)
 
-        for m in range(N_TILES - 1):
-            nc.vector.memset(store[m][:], 0.0)
+        def gather(dst, window, first, count):
+            picks = gather_list[:, first // 16 : (first + count) // 16]
+            nc.vector.tensor_copy(out=dst[:, first : first + count], in_=window.indirect(picks))
 
-        v_codes, v_scales = {}, {}
+        def gather_codes(a, first, count):
+            gather(v_codes[a], table[a][:].bitcast(U32), first, count)
 
-        def picks_of(c):
-            return gather_list[:, c * LIST_COLS : (c + 1) * LIST_COLS]
-
-        def gather_codes(c, a):
-            name = "v_codes%d%d" % (c, a)
-            v_codes[c, a] = placed([P, CHUNK], U32, name, 24576 * c) if a == 1 else held([P, CHUNK], U32, name)
-            nc.vector.tensor_copy(out=v_codes[c, a][:], in_=table[a][:].bitcast(U32).indirect(picks_of(c)))
-
-        def gather_scales(c, a):
-            v_scales[c, a] = held([P, CHUNK], U8, "v_scales%d%d" % (c, a))
-            nc.vector.tensor_copy(out=v_scales[c, a][:], in_=table_planes[:, a, :].indirect(picks_of(c)))
+        def gather_planes(first, count, queue):
+            gather(v_planes, table_planes[:], first, count)
+            for q in range(4):
+                queue.dma_start(
+                    out=v_plane1[32 * q : 32 * q + 4, first : first + count].bitcast(I32),
+                    in_=v_planes[32 * q + 4 : 32 * q + 8, first : first + count].bitcast(I32),
+                )
 
         def quantize(grouped, codes, scales):
-            nc.vector.quantize_mx(out=codes[:].bitcast(FP8X4), scales=scales[:], in_=grouped)
-            return codes[:], scales[:]
+            nc.vector.quantize_mx(out=codes.bitcast(FP8X4), scales=scales, in_=grouped)
 
-        def quantize_held(grouped, name):
-            return quantize(grouped, held([P, PASS], U32, name + "_codes"), held([P, PASS], U8, name + "_scales"))
+        def quantized(width, name):
+            return held([P, width], U32, name + "_codes"), held([P, width], U8, name + "_scales")
 
-        def quantize_first_half():
-            width = K_PASSES * PASS
-            codes, scales = quantize(first_half[:], held([P, width], U32, "wv0_codes"), held([P, width], U8, "wv0_scales"))
-            for a in range(K_PASSES):
-                wv_q[0, a] = codes[:, a * PASS : (a + 1) * PASS], scales[:, a * PASS : (a + 1) * PASS]
+        wv_bf = {(b, a): held([P, PASS * PACK], BF16, "wv_bf%d%d" % (b, a)) for b in range(R_PASSES) for a in range(K_PASSES)}
+        wv_q = {(b, a): quantized(PASS, "wv%d%d" % (b, a)) for b in range(R_PASSES) for a in range(K_PASSES)}
+        wp_q = [quantized(R_PASSES * P, "wp%d" % m) for m in range(N_TILES)]
+        h_q = {(c, b): quantized(CHUNK, "h%d%d" % (c, b)) for c in range(CHUNKS) for b in range(R_PASSES)}
+        vel_tiles = [held([P, PACK, CHUNK], F32, "vel%d" % i) for i in range(3)]
+        h_tiles = [held([P, CHUNK * PACK], BF16, "h_bf%d" % i) for i in range(3)]
+        y_tiles = [held([P, BANK], F32, "y%d" % i) for i in range(3)]
 
-        def quantize_second_half():
-            tiles = placed([P, PASS], U32, "wv10_codes", 20480), placed([P, PASS], U8, "wv10_scales", 22528)
-            wv_q[1, 0] = quantize(wv_bf[1, 0], *tiles)
-
-        wv_q, wp_q, h_q = {}, {}, {}
-
-        first_half = placed([P, K_PASSES * PASS * PACK], BF16, "wv_bf0", 0)
-        wv_bf = {(0, a): first_half[:, a * PASS * PACK : (a + 1) * PASS * PACK] for a in range(K_PASSES)}
-        wv_bf[1, 0] = placed([P, PASS * PACK], BF16, "wv_bf10", 8192)[:]
-        wv_bf[1, 1] = placed([P, PASS * PACK], BF16, "wv_bf11", 16384)[:]
-        h_bf = {(c, b): held([P, CHUNK * PACK], BF16, "h%d%d" % (c, b)) for c in range(CHUNKS) for b in range(R_PASSES)}
-        wp_bf = [h_bf[b, 0] for b in range(R_PASSES)]
-
-        def cast_wv(b, a):
-            dst = wv_bf[b, a].rearrange("p (t q u i j) -> p t q u j i", t=PACK, u=2, i=4, j=PACK)
-            src = wv_raw[b, a].rearrange("p j (q t u i) -> p t q u j i", t=PACK, u=2, i=4)
+        def cast_wv_scalar(b, a, first, width):
+            blocks = slice(first // 32, (first + width) // 32)
+            dst = wv_bf[b, a][:].rearrange("p (t q u i j) -> p t q u j i", t=PACK, u=2, i=4, j=PACK)
+            src = wv_raw[b, a, first][:].rearrange("p j (q t u i) -> p t q u j i", t=PACK, u=2, i=4)
             for t in range(PACK):
-                nc.scalar.copy(out=dst[:, t], in_=src[:, t])
+                nc.scalar.copy(out=dst[:, t, blocks], in_=src[:, t])
 
-        def cast_wv_vector(b, a):
+        def cast_wv_vector(b, a, first, width):
+            blocks = slice(first // 32, (first + width) // 32)
             nc.vector.tensor_copy(
-                out=wv_bf[b, a].rearrange("p (t q i j) -> p t q j i", t=PACK, i=8, j=PACK),
-                in_=wv_raw[b, a].rearrange("p j (q t i) -> p t q j i", t=PACK, i=8),
+                out=wv_bf[b, a][:].rearrange("p (t q i j) -> p t q j i", t=PACK, i=8, j=PACK)[:, :, blocks],
+                in_=wv_raw[b, a, first][:].rearrange("p j (q t i) -> p t q j i", t=PACK, i=8),
             )
 
-        def prepare_wp(b):
-            dst = wp_bf[b][:].rearrange("p (u c i t) -> p u c t i", u=PACK, t=PACK, i=4)
-            src = wp_raw[b].rearrange("p t (u c i) -> p u c t i", u=PACK, i=4)
-            for u in range(PACK):
-                nc.scalar.copy(out=dst[:, u], in_=src[:, u])
-            wp_q[b] = quantize_held(wp_bf[b][:], "wp%d" % b)
+        def quantize_wv(b, a):
+            quantize(wv_bf[b, a][:], wv_q[b, a][0][:], wv_q[b, a][1][:])
 
-        wg_codes = placed([P, K_PASSES * 2 * H], U8, "wg_codes", 4096)
-        wg_planes = placed([P, K_PASSES * H], U8, "wg_planes", 2048)
+        def prepare_wp(m):
+            grouped = in_turn("h", h_tiles)
+            for b in range(R_PASSES):
+                nc.scalar.copy(
+                    out=grouped[:, b * PASS : (b + 1) * PASS].rearrange("p (c i t) -> p c t i", t=PACK, i=4),
+                    in_=wp_raw[b, m // 2][:, :, (m % 2) * P : (m % 2 + 1) * P].rearrange("p t (c i) -> p c t i", i=4),
+                )
+            quantize(grouped[:], wp_q[m][0][:], wp_q[m][1][:])
+
+        wg_codes = held([P, K_PASSES * 2 * H], U8, "wg_codes")
+        wg_planes = held([P, K_PASSES * H], U8, "wg_planes")
 
         def permute_wg():
-            nc.vector.tensor_copy(
-                out=wg_codes[:].bitcast(I32).rearrange("p (g t q w) -> p g t q w", t=PACK, q=16, w=4),
-                in_=words_of(wg_raw).rearrange("p (g q t w) -> p g t q w", t=PACK, q=16, w=4),
-            )
             nc.vector.tensor_copy(
                 out=wg_planes[:].bitcast(I32).rearrange("p (g t q w) -> p g t q w", t=PACK, q=16, w=2),
                 in_=words_of(wg_planes_raw).rearrange("p (g q t w) -> p g t q w", t=PACK, q=16, w=2),
             )
+            nc.vector.tensor_copy(
+                out=wg_codes[:].bitcast(I32).rearrange("p (g t q w) -> p g t q w", t=PACK, q=16, w=4),
+                in_=words_of(wg_raw).rearrange("p (g q t w) -> p g t q w", t=PACK, q=16, w=4),
+            )
 
         def convective(c, b):
-            if (c, b) == (0, 0):
-                vel = placed([P, PACK, CHUNK], F32, "vel_first", 16384)
-            else:
-                vel = ring.tile([P, PACK, CHUNK], F32, name="vel")
-            for t in range(PACK):
-                vel_ps = psum.tile([P, CHUNK], F32, name="vel_ps", bufs=3)
-                cols = slice(t * P, (t + 1) * P)
-                for a in range(K_PASSES):
-                    codes, scales = wv_q[b, a]
-                    nc.tensor.matmul_mx(
-                        out=vel_ps[:],
-                        lhsT=codes[:, cols].bitcast(FP8X4),
-                        lhsT_scale=scales[:, cols],
-                        rhs=v_codes[c, a][:].bitcast(FP8X4),
-                        rhs_scale=v_scales[c, a][:],
-                        start=(a == 0),
-                        stop=(a == K_PASSES - 1),
+            vel = in_turn("vel", vel_tiles)
+            picks = slice(c * CHUNK, (c + 1) * CHUNK)
+            for pair in range(PACK // 2):
+                bank = in_turn("scalar", scalar_banks)
+                for u in range(2):
+                    cols = slice((2 * pair + u) * P, (2 * pair + u + 1) * P)
+                    for a in range(K_PASSES):
+                        nc.tensor.matmul_mx(
+                            out=bank[:, u * CHUNK : (u + 1) * CHUNK],
+                            lhsT=wv_q[b, a][0][:, cols].bitcast(FP8X4),
+                            lhsT_scale=wv_q[b, a][1][:, cols],
+                            rhs=v_codes[a][:, picks].bitcast(FP8X4),
+                            rhs_scale=v_planes[4 * a : P, picks],
+                            start=(a == 0),
+                            stop=(a == K_PASSES - 1),
+                        )
+                for u in range(2):
+                    t = 2 * pair + u
+                    nc.scalar.activation(
+                        out=vel[:, t, :],
+                        in_=bank[:, u * CHUNK : (u + 1) * CHUNK],
+                        func=IDENTITY,
+                        bias=bias[:, PACK * b + t : PACK * b + t + 1],
+                        scale=1.0,
                     )
-                nc.scalar.activation(
-                    out=vel[:, t, :], in_=vel_ps[:], func=IDENTITY, bias=bias[:, PACK * b + t : PACK * b + t + 1], scale=1.0
-                )
-            h = h_bf[c, b]
+            h = in_turn("h", h_tiles)
             for s in range(CHUNK // SUB):
-                grad_ps = psum.tile([P, PACK, SUB], F32, name="grad_ps", bufs=4)
-                picks = slice(s * SUB, (s + 1) * SUB)
+                bank = in_turn("vector", vector_banks)
+                few = slice(c * CHUNK + s * SUB, c * CHUNK + (s + 1) * SUB)
                 for t in range(PACK):
                     for a in range(K_PASSES):
                         col = a * H + b * PASS + t * P
                         nc.tensor.matmul_mx(
-                            out=grad_ps[:, t, :],
+                            out=bank[:, t, :],
                             lhsT=wg_codes[:, 2 * col : 2 * (col + P)].bitcast(FP4X4),
                             lhsT_scale=wg_planes[:, col : col + P],
-                            rhs=v_codes[c, a][:, picks].bitcast(FP8X4),
-                            rhs_scale=v_scales[c, a][:, picks],
+                            rhs=v_codes[a][:, few].bitcast(FP8X4),
+                            rhs_scale=(v_planes, v_plane1)[a][:, few],
                             start=(a == 0),
                             stop=(a == K_PASSES - 1),
                         )
                 nc.vector.tensor_tensor(
                     out=h[:, s * SUB * PACK : (s + 1) * SUB * PACK].rearrange("p (e i t) -> p e t i", t=PACK, i=4),
-                    in0=grad_ps[:].rearrange("p t (e i) -> p e t i", i=4),
-                    in1=vel[:, :, picks].rearrange("p t (e i) -> p e t i", i=4),
+                    in0=bank[:].rearrange("p t (e i) -> p e t i", i=4),
+                    in1=vel[:, :, s * SUB : (s + 1) * SUB].rearrange("p t (e i) -> p e t i", i=4),
                     op=MULT,
                 )
-            h_q[c, b] = quantize_held(h[:], "h%d%d" % (c, b))
-            return vel
+            quantize(h[:], h_q[c, b][0][:], h_q[c, b][1][:])
 
-        y = {}
-
-        def project(c, tiles, into=None):
-            for m in tiles:
-                y_ps = psum.tile([P, CHUNK], F32, name="y_ps", tag="y", bufs=1)
-                cols = slice(m * P, (m + 1) * P)
+        def project(chunks, m):
+            bank = in_turn("scalar", scalar_banks)
+            width = len(chunks) * CHUNK
+            for u, c in enumerate(chunks):
                 for b in range(R_PASSES):
                     nc.tensor.matmul_mx(
-                        out=y_ps[:],
-                        lhsT=wp_q[b][0][:, cols].bitcast(FP8X4),
-                        lhsT_scale=wp_q[b][1][:, cols],
-                        rhs=h_q[c, b][0].bitcast(FP8X4),
-                        rhs_scale=h_q[c, b][1],
+                        out=bank[:, u * CHUNK : (u + 1) * CHUNK],
+                        lhsT=wp_q[m][0][:, b * P : (b + 1) * P].bitcast(FP8X4),
+                        lhsT_scale=wp_q[m][1][:, b * P : (b + 1) * P],
+                        rhs=h_q[c, b][0][:].bitcast(FP8X4),
+                        rhs_scale=h_q[c, b][1][:],
                         start=(b == 0),
                         stop=(b == R_PASSES - 1),
                     )
-                y[c, m] = held([P, CHUNK], F32, "y%d%d" % (c, m))[:] if into is None else into
-                nc.scalar.copy(out=y[c, m], in_=y_ps[:])
+            y = in_turn("y", y_tiles)
+            nc.scalar.copy(out=y[:, 0:width], in_=bank[:, 0:width])
+            first = chunks[0] * CHUNK
+            places = scatter_list[:, first // 16 : (first + width) // 16]
+            nc.vector.tensor_tensor(
+                out=store[m][:].indirect(places), in0=y[:, 0:width], in1=masses[:, first : first + width], op=MULT
+            )
+            if chunks[-1] == CHUNKS - 1:
+                nc.sync.dma_start(out=out[m * P : (m + 1) * P, :], in_=store[m][:])
 
-        def scatter(c):
-            places = scatter_list[:, c * LIST_COLS : (c + 1) * LIST_COLS]
-            for m in range(N_TILES):
-                nc.vector.tensor_tensor(
-                    out=store[m][:].indirect(places), in0=y[c, m], in1=masses[:, c * CHUNK : (c + 1) * CHUNK], op=MULT
-                )
-                if c == CHUNKS - 1:
-                    nc.sync.dma_start(out=out[m * P : (m + 1) * P, :], in_=store[m][:])
-
-        gather_codes(0, 0)
-        gather_codes(1, 0)
-        gather_scales(0, 0)
-        gather_scales(0, 1)
-        gather_scales(1, 0)
-        gather_scales(1, 1)
-        cast_wv(0, 0)
-        load_wv(1, 1)
-        cast_wv(0, 1)
-        load_wp(0)
-        quantize_first_half()
-        gather_codes(0, 1)
+        for m in range(N_TILES // 2):
+            nc.vector.memset(store[m][:], 0.0)
+        gather_codes(0, 0, S)
+        gather_codes(1, 0, S // 2)
+        gather_planes(0, S // 2, nc.scalar)
         permute_wg()
-        gather_codes(1, 1)
+        gather_codes(1, S // 2, S // 2)
+        load_wv(1, 0, 0, PASS, 2048)
+        load_wv(1, 1, 0, PASS // 2, 10240)
+        load_wv(1, 1, PASS // 2, PASS // 2, 14336)
+        gather_planes(S // 2, S // 2, nc.gpsimd)
+        cast_wv_scalar(0, 0, 0, PASS)
+        load_wp(0, 18432)
+        cast_wv_vector(0, 1, 0, PASS)
+        nc.sync.dma_start(out=masses[:], in_=wgo)
+        quantize_wv(0, 0)
+        quantize_wv(0, 1)
         convective(0, 0)
-        cast_wv_vector(1, 0)
-        load_wp(1)
-        cast_wv_vector(1, 1)
-        nc.sync.dma_start(out=masses, in_=wgo)
-        quantize_second_half()
+        cast_wv_scalar(1, 0, 0, PASS)
+        load_wp(1, 2048)
+        cast_wv_vector(1, 1, 0, PASS // 2)
+        cast_wv_vector(1, 1, PASS // 2, PASS // 2)
         convective(1, 0)
-        wv_q[1, 1] = quantize_held(wv_bf[1, 1], "wv11")
+        quantize_wv(1, 0)
+        quantize_wv(1, 1)
         convective(0, 1)
         prepare_wp(0)
+        project([0], 0)
+        convective(1, 1)
         prepare_wp(1)
-        project(0, range(N_TILES - 1))
-        last_vel = convective(1, 1)
-        project(0, [N_TILES - 1], last_vel[:, 0, :])
-        project(1, range(N_TILES))
-        nc.vector.memset(store[N_TILES - 1][:], 0.0)
-        scatter(0)
-        scatter(1)
+        project([0], 1)
+        prepare_wp(2)
+        project([0], 2)
+        convective(2, 0)
+        prepare_wp(3)
+        project([0], 3)
+        convective(3, 0)
+        project([1], 0)
+        convective(2, 1)
+        project([1], 1)
+        convective(3, 1)
+        project([1], 2)
+        project([1], 3)
+        for m in range(N_TILES):
+            project([2, 3], m)

@@ -46,13 +46,13 @@ def tile_list_mesh_convective_terms_kernel(
 
         gather_list = held([P, S // 16], U16, "gather_list")
         scatter_list = held([P, S // 16], U16, "scatter_list")
-        table = [held([P, T], I32, "table0"), placed([P, T], I32, "table1", 8192)]
+        table = [placed([P, T], I32, "table0", 22528), placed([P, T], I32, "table1", 8192)]
         table_planes = held([P, T], U8, "table_planes")
         wg_raw = held([P, K_PASSES, 2 * H], U8, "wg_raw")
         wg_planes_raw = held([P, K_PASSES, H], U8, "wg_planes_raw")
-        masses = placed([P, S], F32, "masses", 26624)
+        masses = placed([P, S], F32, "masses", 4096)
         identity = held([P, P], F32, "identity")[:]
-        bias_rows = placed([P, R_PASSES * P], F32, "bias_rows", 26112)
+        bias_rows = held([P, R_PASSES * P], F32, "bias_rows")
         bias = held([P, R_PASSES * PACK], F32, "bias")
         store = [held([P, T2], F32, "store%d" % m) for m in range(N_TILES)]
         v_codes = [held([P, S], U32, "v_codes%d" % a) for a in range(K_PASSES)]
@@ -71,10 +71,13 @@ def tile_list_mesh_convective_terms_kernel(
             return planes[:].rearrange("p a n -> p (a n)").bitcast(I32)
 
         nc.gpsimd.memset(table_planes[:].bitcast(I32), 0)
-        nc.vector.memset(words_of(wg_planes_raw), 0)
-        nc.vector.memset(v_plane1[:].bitcast(I32), 0)
-        for rows in (slice(0, 28), slice(32, 64), slice(64, P)):
-            nc.gpsimd.memset(bias_rows[rows, :], 0.0)
+        nc.gpsimd.memset(words_of(wg_planes_raw), 0)
+        nc.gpsimd.memset(v_plane1[:].bitcast(I32), 0)
+        nc.gpsimd.memset(bias_rows[:], 0.0)
+        nc.gpsimd.dma_start(
+            out=bias_rows[0:PACK, :].rearrange("t (g i) -> t g i", i=8),
+            in_=bv.rearrange("(g t i) -> t g i", t=PACK, i=8),
+        )
         make_identity(nc, identity)
 
         def load_table(a):
@@ -99,36 +102,29 @@ def tile_list_mesh_convective_terms_kernel(
                     nc.sync.dma_start(out=wp_raw[b, half][:, t, :], in_=rows[t])
 
         nc.sync.dma_start(gather_list[:], offs)
-        nc.sync.dma_start(
-            out=bias_rows[28:32, :].rearrange("t (g i) -> t g i", i=8),
-            in_=bv.rearrange("(g t i) -> t g i", t=PACK, i=8),
-        )
+        nc.sync.dma_start(scatter_list[:], offs2)
         load_table(0)
         load_table(1)
         nc.sync.dma_start(out=wg_raw[:].bitcast(I32), in_=wg_words.rearrange("a p n -> p a n").bitcast(I32))
-        nc.sync.dma_start(scatter_list[:], offs2)
         for q in range(4):
-            nc.sync.dma_start(
+            nc.scalar.dma_start(
                 out=table_planes[32 * q : 32 * q + 8, :].bitcast(I32),
                 in_=tab_scales[:, 4 * q : 4 * q + 4, :].bitcast(I32),
             )
         for q in range(4):
-            nc.gpsimd.dma_start(
+            nc.scalar.dma_start(
                 out=wg_planes_raw[32 * q : 32 * q + 4, :, :].bitcast(I32),
                 in_=wg_scales[:, 4 * q : 4 * q + 4, :].rearrange("a r n -> r a n").bitcast(I32),
             )
-        for m in range(N_TILES // 2, N_TILES):
-            nc.gpsimd.memset(store[m][:], 0.0)
+        nc.gpsimd.memset(store[N_TILES - 1][:], 0.0)
         bias_ps = in_turn("scalar", scalar_banks)
         for b in range(R_PASSES):
             nc.tensor.transpose(bias_ps[:, b * P : (b + 1) * P], bias_rows[:, b * P : (b + 1) * P], identity)
         nc.scalar.activation(
             out=bias[:].rearrange("p (b t) -> p b t", t=PACK),
-            in_=bias_ps[:, 0 : R_PASSES * P].rearrange("p (b c) -> p b c", c=P)[:, :, 28:32],
+            in_=bias_ps[:, 0 : R_PASSES * P].rearrange("p (b c) -> p b c", c=P)[:, :, 0:PACK],
             func=IDENTITY,
         )
-        load_wv(0, 0, 0, PASS, 18432)
-        load_wv(0, 1, 0, PASS, 26624)
 
         def gather(dst, window, first, count):
             picks = gather_list[:, first // 16 : (first + count) // 16]
@@ -151,7 +147,9 @@ def tile_list_mesh_convective_terms_kernel(
         def quantized(width, name):
             return held([P, width], U32, name + "_codes"), held([P, width], U8, name + "_scales")
 
-        wv_bf = {(b, a): held([P, PASS * PACK], BF16, "wv_bf%d%d" % (b, a)) for b in range(R_PASSES) for a in range(K_PASSES)}
+        wv_bf = {(0, a): placed([P, PASS * PACK], BF16, "wv_bf0%d" % a, 36864 + 4096 * a) for a in range(K_PASSES)}
+        for a in range(K_PASSES):
+            wv_bf[1, a] = held([P, PASS * PACK], BF16, "wv_bf1%d" % a)
         wv_q = {(b, a): quantized(PASS, "wv%d%d" % (b, a)) for b in range(R_PASSES) for a in range(K_PASSES)}
         wp_q = [quantized(R_PASSES * P, "wp%d" % m) for m in range(N_TILES)]
         h_q = {(c, b): quantized(CHUNK, "h%d%d" % (c, b)) for c in range(CHUNKS) for b in range(R_PASSES)}
@@ -190,12 +188,12 @@ def tile_list_mesh_convective_terms_kernel(
 
         def permute_wg():
             nc.vector.tensor_copy(
-                out=wg_planes[:].bitcast(I32).rearrange("p (g t q w) -> p g t q w", t=PACK, q=16, w=2),
-                in_=words_of(wg_planes_raw).rearrange("p (g q t w) -> p g t q w", t=PACK, q=16, w=2),
-            )
-            nc.vector.tensor_copy(
                 out=wg_codes[:].bitcast(I32).rearrange("p (g t q w) -> p g t q w", t=PACK, q=16, w=4),
                 in_=words_of(wg_raw).rearrange("p (g q t w) -> p g t q w", t=PACK, q=16, w=4),
+            )
+            nc.vector.tensor_copy(
+                out=wg_planes[:].bitcast(I32).rearrange("p (g t q w) -> p g t q w", t=PACK, q=16, w=2),
+                in_=words_of(wg_planes_raw).rearrange("p (g q t w) -> p g t q w", t=PACK, q=16, w=2),
             )
 
         def convective(c, b):
@@ -272,28 +270,30 @@ def tile_list_mesh_convective_terms_kernel(
             if chunks[-1] == CHUNKS - 1:
                 nc.sync.dma_start(out=out[m * P : (m + 1) * P, :], in_=store[m][:])
 
-        for m in range(N_TILES // 2):
+        for m in range(N_TILES - 1):
             nc.vector.memset(store[m][:], 0.0)
         gather_codes(0, 0, S)
+        load_wv(0, 0, 0, PASS, 18432)
+        load_wv(0, 1, 0, PASS, 26624)
         gather_codes(1, 0, S // 2)
         gather_planes(0, S // 2, nc.scalar)
-        permute_wg()
         gather_codes(1, S // 2, S // 2)
-        load_wv(1, 0, 0, PASS, 2048)
-        load_wv(1, 1, 0, PASS // 2, 10240)
-        load_wv(1, 1, PASS // 2, PASS // 2, 14336)
-        gather_planes(S // 2, S // 2, nc.gpsimd)
+        load_wv(1, 0, 0, PASS, 4096)
+        gather_planes(S // 2, S // 2, nc.sync)
+        permute_wg()
         cast_wv_scalar(0, 0, 0, PASS)
-        load_wp(0, 18432)
+        load_wv(1, 1, 0, PASS // 2, 18432)
+        load_wv(1, 1, PASS // 2, PASS // 2, 22528)
         cast_wv_vector(0, 1, 0, PASS)
-        nc.sync.dma_start(out=masses[:], in_=wgo)
         quantize_wv(0, 0)
         quantize_wv(0, 1)
+        load_wp(0, 36864)
         convective(0, 0)
         cast_wv_scalar(1, 0, 0, PASS)
-        load_wp(1, 2048)
+        nc.sync.dma_start(out=masses[:], in_=wgo)
         cast_wv_vector(1, 1, 0, PASS // 2)
         cast_wv_vector(1, 1, PASS // 2, PASS // 2)
+        load_wp(1, 18432)
         convective(1, 0)
         quantize_wv(1, 0)
         quantize_wv(1, 1)

@@ -46,18 +46,18 @@ def tile_list_mesh_convective_terms_kernel(
 
         gather_list = held([P, S // 16], U16, "gather_list")
         scatter_list = held([P, S // 16], U16, "scatter_list")
-        table = [placed([P, T], I32, "table0", 22528), placed([P, T], I32, "table1", 8192)]
+        table = [placed([P, T], I32, "table0", 7680), placed([P, T], I32, "table1", 0)]
         table_planes = held([P, T], U8, "table_planes")
-        wg_raw = held([P, K_PASSES, 2 * H], U8, "wg_raw")
-        wg_planes_raw = held([P, K_PASSES, H], U8, "wg_planes_raw")
-        masses = placed([P, S], F32, "masses", 4096)
+        wg_raw = placed([P, K_PASSES, 2 * H], U8, "wg_raw", 8192)
+        wg_planes_raw = placed([P, K_PASSES, H], U8, "wg_planes_raw", 12288)
+        masses = placed([P, S], F32, "masses", 24576)
         identity = held([P, P], F32, "identity")[:]
         bias_rows = held([P, R_PASSES * P], F32, "bias_rows")
         bias = held([P, R_PASSES * PACK], F32, "bias")
-        store = [held([P, T2], F32, "store%d" % m) for m in range(N_TILES)]
+        store = [held([P, T2], F32, "store0"), held([P, T2], F32, "store1"), placed([P, T2], F32, "store2", 15360)]
         v_codes = [held([P, S], U32, "v_codes%d" % a) for a in range(K_PASSES)]
-        v_planes = held([P, S], U8, "v_planes")
-        v_plane1 = held([P, S], U8, "v_plane1")
+        v_planes = placed([P, S], U8, "v_planes", 14336)
+        v_plane1 = placed([P, S], U8, "v_plane1", 32768)
 
         scalar_banks = [psum.tile([P, BANK], F32, name="scalar_bank%d" % i) for i in range(4)]
         vector_banks = [psum.tile([P, PACK, SUB], F32, name="vector_bank%d" % i) for i in range(4)]
@@ -71,8 +71,6 @@ def tile_list_mesh_convective_terms_kernel(
             return planes[:].rearrange("p a n -> p (a n)").bitcast(I32)
 
         nc.gpsimd.memset(table_planes[:].bitcast(I32), 0)
-        nc.gpsimd.memset(words_of(wg_planes_raw), 0)
-        nc.gpsimd.memset(v_plane1[:].bitcast(I32), 0)
         nc.gpsimd.memset(bias_rows[:], 0.0)
         nc.gpsimd.dma_start(
             out=bias_rows[0:PACK, :].rearrange("t (g i) -> t g i", i=8),
@@ -104,27 +102,13 @@ def tile_list_mesh_convective_terms_kernel(
         nc.sync.dma_start(gather_list[:], offs)
         nc.sync.dma_start(scatter_list[:], offs2)
         load_table(0)
-        load_table(1)
-        nc.sync.dma_start(out=wg_raw[:].bitcast(I32), in_=wg_words.rearrange("a p n -> p a n").bitcast(I32))
+        load_wv(0, 0, 0, PASS, 31744)
+        load_wv(0, 1, 0, PASS, 40960)
         for q in range(4):
             nc.scalar.dma_start(
                 out=table_planes[32 * q : 32 * q + 8, :].bitcast(I32),
                 in_=tab_scales[:, 4 * q : 4 * q + 4, :].bitcast(I32),
             )
-        for q in range(4):
-            nc.scalar.dma_start(
-                out=wg_planes_raw[32 * q : 32 * q + 4, :, :].bitcast(I32),
-                in_=wg_scales[:, 4 * q : 4 * q + 4, :].rearrange("a r n -> r a n").bitcast(I32),
-            )
-        nc.gpsimd.memset(store[N_TILES - 1][:], 0.0)
-        bias_ps = in_turn("scalar", scalar_banks)
-        for b in range(R_PASSES):
-            nc.tensor.transpose(bias_ps[:, b * P : (b + 1) * P], bias_rows[:, b * P : (b + 1) * P], identity)
-        nc.scalar.activation(
-            out=bias[:].rearrange("p (b t) -> p b t", t=PACK),
-            in_=bias_ps[:, 0 : R_PASSES * P].rearrange("p (b c) -> p b c", c=P)[:, :, 0:PACK],
-            func=IDENTITY,
-        )
 
         def gather(dst, window, first, count):
             picks = gather_list[:, first // 16 : (first + count) // 16]
@@ -133,12 +117,12 @@ def tile_list_mesh_convective_terms_kernel(
         def gather_codes(a, first, count):
             gather(v_codes[a], table[a][:].bitcast(U32), first, count)
 
-        def gather_planes(first, count, queue):
-            gather(v_planes, table_planes[:], first, count)
+        def move_second_plane():
+            nc.gpsimd.memset(v_plane1[:].bitcast(I32), 0)
             for q in range(4):
-                queue.dma_start(
-                    out=v_plane1[32 * q : 32 * q + 4, first : first + count].bitcast(I32),
-                    in_=v_planes[32 * q + 4 : 32 * q + 8, first : first + count].bitcast(I32),
+                nc.sync.dma_start(
+                    out=v_plane1[32 * q : 32 * q + 4, :].bitcast(I32),
+                    in_=v_planes[32 * q + 4 : 32 * q + 8, :].bitcast(I32),
                 )
 
         def quantize(grouped, codes, scales):
@@ -147,14 +131,14 @@ def tile_list_mesh_convective_terms_kernel(
         def quantized(width, name):
             return held([P, width], U32, name + "_codes"), held([P, width], U8, name + "_scales")
 
-        wv_bf = {(0, a): placed([P, PASS * PACK], BF16, "wv_bf0%d" % a, 36864 + 4096 * a) for a in range(K_PASSES)}
+        wv_bf = {(0, a): placed([P, PASS * PACK], BF16, "wv_bf0%d" % a, 49152 + 4096 * a) for a in range(K_PASSES)}
         for a in range(K_PASSES):
-            wv_bf[1, a] = held([P, PASS * PACK], BF16, "wv_bf1%d" % a)
+            wv_bf[1, a] = placed([P, PASS * PACK], BF16, "wv_bf1%d" % a, 57344 + 4096 * a)
         wv_q = {(b, a): quantized(PASS, "wv%d%d" % (b, a)) for b in range(R_PASSES) for a in range(K_PASSES)}
         wp_q = [quantized(R_PASSES * P, "wp%d" % m) for m in range(N_TILES)]
         h_q = {(c, b): quantized(CHUNK, "h%d%d" % (c, b)) for c in range(CHUNKS) for b in range(R_PASSES)}
-        vel_tiles = [held([P, PACK, CHUNK], F32, "vel%d" % i) for i in range(3)]
-        h_tiles = [held([P, CHUNK * PACK], BF16, "h_bf%d" % i) for i in range(3)]
+        vel_tiles = [placed([P, PACK, CHUNK], F32, "vel0", 28672)] + [held([P, PACK, CHUNK], F32, "vel%d" % i) for i in (1, 2)]
+        h_tiles = [placed([P, CHUNK * PACK], BF16, "h_bf0", 47104)] + [held([P, CHUNK * PACK], BF16, "h_bf%d" % i) for i in (1, 2)]
         y_tiles = [held([P, BANK], F32, "y%d" % i) for i in range(3)]
 
         def cast_wv_scalar(b, a, first, width):
@@ -270,34 +254,53 @@ def tile_list_mesh_convective_terms_kernel(
             if chunks[-1] == CHUNKS - 1:
                 nc.sync.dma_start(out=out[m * P : (m + 1) * P, :], in_=store[m][:])
 
-        for m in range(N_TILES - 1):
+        for m in range(2):
             nc.vector.memset(store[m][:], 0.0)
         gather_codes(0, 0, S)
-        load_wv(0, 0, 0, PASS, 18432)
-        load_wv(0, 1, 0, PASS, 26624)
-        gather_codes(1, 0, S // 2)
-        gather_planes(0, S // 2, nc.scalar)
-        gather_codes(1, S // 2, S // 2)
-        load_wv(1, 0, 0, PASS, 4096)
-        gather_planes(S // 2, S // 2, nc.sync)
-        permute_wg()
+        load_table(1)
+        nc.sync.dma_start(out=wg_raw[:].bitcast(I32), in_=wg_words.rearrange("a p n -> p a n").bitcast(I32))
+        nc.gpsimd.memset(words_of(wg_planes_raw), 0)
+        for q in range(4):
+            nc.sync.dma_start(
+                out=wg_planes_raw[32 * q : 32 * q + 4, :, :].bitcast(I32),
+                in_=wg_scales[:, 4 * q : 4 * q + 4, :].rearrange("a r n -> r a n").bitcast(I32),
+            )
+        nc.vector.memset(store[2][:], 0.0)
+        gather(v_planes, table_planes[:], 0, S)
         cast_wv_scalar(0, 0, 0, PASS)
-        load_wv(1, 1, 0, PASS // 2, 18432)
-        load_wv(1, 1, PASS // 2, PASS // 2, 22528)
-        cast_wv_vector(0, 1, 0, PASS)
+        load_wv(1, 0, 0, PASS, 24576)
+        move_second_plane()
+        cast_wv_scalar(0, 1, 0, PASS)
+        load_wv(1, 1, 0, PASS // 2, 40960)
+        load_wv(1, 1, PASS // 2, PASS // 2, 45056)
+        bias_ps = in_turn("scalar", scalar_banks)
+        for b in range(R_PASSES):
+            nc.tensor.transpose(bias_ps[:, b * P : (b + 1) * P], bias_rows[:, b * P : (b + 1) * P], identity)
+        nc.scalar.activation(
+            out=bias[:].rearrange("p (b t) -> p b t", t=PACK),
+            in_=bias_ps[:, 0 : R_PASSES * P].rearrange("p (b c) -> p b c", c=P)[:, :, 0:PACK],
+            func=IDENTITY,
+        )
+        gather_codes(1, 0, CHUNK)
         quantize_wv(0, 0)
         quantize_wv(0, 1)
-        load_wp(0, 36864)
-        convective(0, 0)
+        load_wp(0, 49152)
+        permute_wg()
+        gather_codes(1, CHUNK, CHUNK)
+        gather_codes(1, 2 * CHUNK, 2 * CHUNK)
         cast_wv_scalar(1, 0, 0, PASS)
         nc.sync.dma_start(out=masses[:], in_=wgo)
         cast_wv_vector(1, 1, 0, PASS // 2)
         cast_wv_vector(1, 1, PASS // 2, PASS // 2)
-        load_wp(1, 18432)
-        convective(1, 0)
+        load_wp(1, 38912)
         quantize_wv(1, 0)
         quantize_wv(1, 1)
+        convective(0, 0)
+        store.append(placed([P, T2], F32, "store3", 49152 + 12288))
+        for piece in range(4):
+            nc.gpsimd.memset(store[3][:, piece * BANK : (piece + 1) * BANK], 0.0)
         convective(0, 1)
+        convective(1, 0)
         prepare_wp(0)
         project([0], 0)
         convective(1, 1)

@@ -44,20 +44,29 @@ def tile_list_mesh_convective_terms_kernel(
         def placed(shape, dtype, name, offset):
             return shared.tile(shape, dtype, name=name, align_bytes=64, offset=offset)
 
+        KB = 1024
+        at_raw10, at_planes, at_raw11, at_bf00, at_bf01, at_table1, at_bf11, at_raw01 = 0, 8 * KB - 64, 16 * KB, 24 * KB - 64, 33 * KB, 41 * KB, 50 * KB, 54 * KB
         gather_list = held([P, S // 16], U16, "gather_list")
         scatter_list = held([P, S // 16], U16, "scatter_list")
-        table = [placed([P, T], I32, "table0", 7680), placed([P, T], I32, "table1", 0)]
-        table_planes = held([P, T], U8, "table_planes")
-        wg_raw = placed([P, K_PASSES, 2 * H], U8, "wg_raw", 8192)
-        wg_planes_raw = placed([P, K_PASSES, H], U8, "wg_planes_raw", 12288)
-        masses = placed([P, S], F32, "masses", 24576)
+        table = [held([P, T], I32, "table0"), placed([P, T], I32, "table1", at_table1)]
+        table_planes = placed([P, T], U8, "table_planes", at_planes)
+        wg_raw = [held([P, K_PASSES, H], U8, "wg_raw0"), placed([P, K_PASSES, H], U8, "wg_raw1", at_bf00 + 64 + 2 * KB)]
+        wg_planes_raw = held([P, K_PASSES, H], U8, "wg_planes_raw")
+        masses = placed([P, S], F32, "masses", at_table1 - 4 * KB + 64)
         identity = held([P, P], F32, "identity")[:]
         bias_rows = held([P, R_PASSES * P], F32, "bias_rows")
-        bias = held([P, R_PASSES * PACK], F32, "bias")
-        store = [held([P, T2], F32, "store0"), held([P, T2], F32, "store1"), placed([P, T2], F32, "store2", 15360)]
-        v_codes = [held([P, S], U32, "v_codes%d" % a) for a in range(K_PASSES)]
-        v_planes = placed([P, S], U8, "v_planes", 14336)
-        v_plane1 = placed([P, S], U8, "v_plane1", 32768)
+        bias = placed([P, R_PASSES * PACK], F32, "bias", at_raw01)
+        store = [held([P, T2], F32, "store%d" % m) for m in range(3)]
+        store.append(placed([P, T2], F32, "store3", at_planes + 64))
+        v_codes0 = held([P, S], U32, "v_codes0")
+        v_codes1 = [placed([P, BANK], U32, "v_codes10", at_bf00 + 64), placed([P, BANK], U32, "v_codes11", at_bf01)]
+        v_planes = held([P, S], U8, "v_planes")
+        v_plane1 = held([P, S], U8, "v_plane1")
+
+        def codes_of(a, first, count):
+            if a == 0:
+                return v_codes0[:, first : first + count]
+            return v_codes1[first // BANK][:, first % BANK : first % BANK + count]
 
         scalar_banks = [psum.tile([P, BANK], F32, name="scalar_bank%d" % i) for i in range(4)]
         vector_banks = [psum.tile([P, PACK, SUB], F32, name="vector_bank%d" % i) for i in range(4)]
@@ -70,55 +79,42 @@ def tile_list_mesh_convective_terms_kernel(
         def words_of(planes):
             return planes[:].rearrange("p a n -> p (a n)").bitcast(I32)
 
-        nc.gpsimd.memset(table_planes[:].bitcast(I32), 0)
-        nc.gpsimd.memset(bias_rows[:], 0.0)
-        nc.gpsimd.dma_start(
-            out=bias_rows[0:PACK, :].rearrange("t (g i) -> t g i", i=8),
-            in_=bv.rearrange("(g t i) -> t g i", t=PACK, i=8),
-        )
-        make_identity(nc, identity)
-
-        def load_table(a):
-            nc.sync.dma_start(out=table[a][:], in_=tab_words[a].rearrange("p t i -> p (t i)").bitcast(I32))
+        def load_table(a, pieces):
+            words = tab_words[a].rearrange("p t i -> p (t i)").bitcast(I32)
+            width = T // pieces
+            for piece in range(pieces):
+                cols = slice(piece * width, (piece + 1) * width)
+                nc.sync.dma_start(out=table[a][:, cols], in_=words[:, cols])
 
         wv_raw = {}
 
-        def load_wv(b, a, first, width, offset):
-            wv_raw[b, a, first] = placed([P, PACK, width], F32, "wv_raw%d%d%d" % (b, a, first), offset)
-            rows = wv[a * PASS : (a + 1) * PASS, b * PASS + first : b * PASS + first + width]
-            nc.sync.dma_start(out=wv_raw[b, a, first][:], in_=rows.rearrange("(p j) c -> p j c", j=PACK))
+        def load_wv(b, a, pieces, offset):
+            name = "wv_raw%d%d" % (b, a)
+            wv_raw[b, a] = held([P, PACK, PASS], F32, name) if offset is None else placed([P, PACK, PASS], F32, name, offset)
+            rows = wv[a * PASS : (a + 1) * PASS, b * PASS : (b + 1) * PASS].rearrange("(p j) c -> p j c", j=PACK)
+            step = PACK // pieces
+            for j in range(0, PACK, step):
+                nc.sync.dma_start(out=wv_raw[b, a][:, j : j + step, :], in_=rows[:, j : j + step, :])
 
         wp_raw = {}
 
         def load_wp(half, offset):
             width = N // 2
             for b in range(R_PASSES):
-                wp_raw[b, half] = placed([P, PACK, width], F32, "wp_raw%d%d" % (b, half), offset + 4096 * b)
+                wp_raw[b, half] = placed([P, PACK, width], F32, "wp_raw%d%d" % (b, half), offset + 4 * KB * b)
                 rows = wp[b * PASS : (b + 1) * PASS, half * width : (half + 1) * width]
                 rows = rows.rearrange("(q t i) n -> t q i n", t=PACK, i=8)
                 for t in range(PACK):
                     nc.sync.dma_start(out=wp_raw[b, half][:, t, :], in_=rows[t])
 
-        nc.sync.dma_start(gather_list[:], offs)
-        nc.sync.dma_start(scatter_list[:], offs2)
-        load_table(0)
-        load_wv(0, 0, 0, PASS, 31744)
-        load_wv(0, 1, 0, PASS, 40960)
-        for q in range(4):
-            nc.scalar.dma_start(
-                out=table_planes[32 * q : 32 * q + 8, :].bitcast(I32),
-                in_=tab_scales[:, 4 * q : 4 * q + 4, :].bitcast(I32),
-            )
-
         def gather(dst, window, first, count):
             picks = gather_list[:, first // 16 : (first + count) // 16]
-            nc.vector.tensor_copy(out=dst[:, first : first + count], in_=window.indirect(picks))
+            nc.vector.tensor_copy(out=dst, in_=window.indirect(picks))
 
         def gather_codes(a, first, count):
-            gather(v_codes[a], table[a][:].bitcast(U32), first, count)
+            gather(codes_of(a, first, count), table[a][:].bitcast(U32), first, count)
 
         def move_second_plane():
-            nc.gpsimd.memset(v_plane1[:].bitcast(I32), 0)
             for q in range(4):
                 nc.sync.dma_start(
                     out=v_plane1[32 * q : 32 * q + 4, :].bitcast(I32),
@@ -131,28 +127,30 @@ def tile_list_mesh_convective_terms_kernel(
         def quantized(width, name):
             return held([P, width], U32, name + "_codes"), held([P, width], U8, name + "_scales")
 
-        wv_bf = {(0, a): placed([P, PASS * PACK], BF16, "wv_bf0%d" % a, 49152 + 4096 * a) for a in range(K_PASSES)}
-        for a in range(K_PASSES):
-            wv_bf[1, a] = placed([P, PASS * PACK], BF16, "wv_bf1%d" % a, 57344 + 4096 * a)
+        wv_bf = {
+            (0, 0): placed([P, PASS * PACK], BF16, "wv_bf00", at_bf00),
+            (0, 1): placed([P, PASS * PACK], BF16, "wv_bf01", at_bf01),
+            (1, 0): held([P, PASS * PACK], BF16, "wv_bf10"),
+            (1, 1): placed([P, PASS * PACK], BF16, "wv_bf11", at_bf11),
+        }
         wv_q = {(b, a): quantized(PASS, "wv%d%d" % (b, a)) for b in range(R_PASSES) for a in range(K_PASSES)}
-        wp_q = [quantized(R_PASSES * P, "wp%d" % m) for m in range(N_TILES)]
-        h_q = {(c, b): quantized(CHUNK, "h%d%d" % (c, b)) for c in range(CHUNKS) for b in range(R_PASSES)}
-        vel_tiles = [placed([P, PACK, CHUNK], F32, "vel0", 28672)] + [held([P, PACK, CHUNK], F32, "vel%d" % i) for i in (1, 2)]
-        h_tiles = [placed([P, CHUNK * PACK], BF16, "h_bf0", 47104)] + [held([P, CHUNK * PACK], BF16, "h_bf%d" % i) for i in (1, 2)]
+        wp_q = [(placed([P, R_PASSES * P], U32, "wp0_codes", at_bf11), held([P, R_PASSES * P], U8, "wp0_scales"))]
+        wp_q = wp_q + [quantized(R_PASSES * P, "wp%d" % m) for m in range(1, N_TILES)]
+        h_q = [quantized(S, "h%d" % b) for b in range(R_PASSES)]
+        vel_tiles = [held([P, PACK, BANK], F32, "vel%d" % i) for i in range(2)]
+        h_tiles = [held([P, CHUNK * PACK], BF16, "h_bf%d" % i) for i in range(3)]
         y_tiles = [held([P, BANK], F32, "y%d" % i) for i in range(3)]
 
-        def cast_wv_scalar(b, a, first, width):
-            blocks = slice(first // 32, (first + width) // 32)
+        def cast_wv_scalar(b, a):
             dst = wv_bf[b, a][:].rearrange("p (t q u i j) -> p t q u j i", t=PACK, u=2, i=4, j=PACK)
-            src = wv_raw[b, a, first][:].rearrange("p j (q t u i) -> p t q u j i", t=PACK, u=2, i=4)
+            src = wv_raw[b, a][:].rearrange("p j (q t u i) -> p t q u j i", t=PACK, u=2, i=4)
             for t in range(PACK):
-                nc.scalar.copy(out=dst[:, t, blocks], in_=src[:, t])
+                nc.scalar.copy(out=dst[:, t], in_=src[:, t])
 
-        def cast_wv_vector(b, a, first, width):
-            blocks = slice(first // 32, (first + width) // 32)
+        def cast_wv_vector(b, a):
             nc.vector.tensor_copy(
-                out=wv_bf[b, a][:].rearrange("p (t q i j) -> p t q j i", t=PACK, i=8, j=PACK)[:, :, blocks],
-                in_=wv_raw[b, a, first][:].rearrange("p j (q t i) -> p t q j i", t=PACK, i=8),
+                out=wv_bf[b, a][:].rearrange("p (t q i j) -> p t q j i", t=PACK, i=8, j=PACK),
+                in_=wv_raw[b, a][:].rearrange("p j (q t i) -> p t q j i", t=PACK, i=8),
             )
 
         def quantize_wv(b, a):
@@ -167,86 +165,109 @@ def tile_list_mesh_convective_terms_kernel(
                 )
             quantize(grouped[:], wp_q[m][0][:], wp_q[m][1][:])
 
-        wg_codes = held([P, K_PASSES * 2 * H], U8, "wg_codes")
-        wg_planes = held([P, K_PASSES * H], U8, "wg_planes")
+        wg_codes = [held([P, K_PASSES * 2 * PASS], U8, "wg_codes%d" % b) for b in range(R_PASSES)]
+        wg_planes = [held([P, K_PASSES * PASS], U8, "wg_planes%d" % b) for b in range(R_PASSES)]
 
-        def permute_wg():
+        def load_wg(b):
+            words = wg_words[:, :, b * H : (b + 1) * H].rearrange("a p n -> p a n")
+            nc.sync.dma_start(out=wg_raw[b][:].bitcast(I32), in_=words.bitcast(I32))
+
+        def permute_wg(b):
             nc.vector.tensor_copy(
-                out=wg_codes[:].bitcast(I32).rearrange("p (g t q w) -> p g t q w", t=PACK, q=16, w=4),
-                in_=words_of(wg_raw).rearrange("p (g q t w) -> p g t q w", t=PACK, q=16, w=4),
+                out=wg_codes[b][:].bitcast(I32).rearrange("p (a t q w) -> p a t q w", t=PACK, q=16, w=4),
+                in_=words_of(wg_raw[b]).rearrange("p (a q t w) -> p a t q w", t=PACK, q=16, w=4),
             )
             nc.vector.tensor_copy(
-                out=wg_planes[:].bitcast(I32).rearrange("p (g t q w) -> p g t q w", t=PACK, q=16, w=2),
-                in_=words_of(wg_planes_raw).rearrange("p (g q t w) -> p g t q w", t=PACK, q=16, w=2),
+                out=wg_planes[b][:].bitcast(I32).rearrange("p (a t q w) -> p a t q w", t=PACK, q=16, w=2),
+                in_=words_of(wg_planes_raw).rearrange("p (a b q t w) -> p b a t q w", a=K_PASSES, t=PACK, q=16, w=2)[:, b],
             )
 
-        def convective(c, b):
+        def velocity_pass(banks, half, b, a):
+            for t in range(PACK):
+                cols = slice(t * P, (t + 1) * P)
+                nc.tensor.matmul_mx(
+                    out=banks[t][:],
+                    lhsT=wv_q[b, a][0][:, cols].bitcast(FP8X4),
+                    lhsT_scale=wv_q[b, a][1][:, cols],
+                    rhs=codes_of(a, half * BANK, BANK).bitcast(FP8X4),
+                    rhs_scale=v_planes[4 * a : P, half * BANK : (half + 1) * BANK],
+                    start=(a == 0),
+                    stop=(a == K_PASSES - 1),
+                )
+
+        def gradient_pass(bank, first, b, a):
+            for t in range(PACK):
+                col = a * PASS + t * P
+                nc.tensor.matmul_mx(
+                    out=bank[:, t, :],
+                    lhsT=wg_codes[b][:, 2 * col : 2 * (col + P)].bitcast(FP4X4),
+                    lhsT_scale=wg_planes[b][:, col : col + P],
+                    rhs=codes_of(a, first, SUB).bitcast(FP8X4),
+                    rhs_scale=(v_planes, v_plane1)[a][:, first : first + SUB],
+                    start=(a == 0 and t == 0),
+                    stop=(a == K_PASSES - 1 and t == PACK - 1),
+                )
+
+        sums = {}
+
+        def multiply(half, b, pass_by_pass=False):
+            vel_banks = [in_turn("scalar", scalar_banks) for t in range(PACK)]
+            subs = range(BANK // SUB)
+            if pass_by_pass:
+                for a in range(K_PASSES):
+                    velocity_pass(vel_banks, half, b, a)
+                    for s in subs:
+                        gradient_pass(vector_banks[s], half * BANK + s * SUB, b, a)
+            else:
+                for a in range(K_PASSES):
+                    velocity_pass(vel_banks, half, b, a)
             vel = in_turn("vel", vel_tiles)
-            picks = slice(c * CHUNK, (c + 1) * CHUNK)
-            for pair in range(PACK // 2):
-                bank = in_turn("scalar", scalar_banks)
-                for u in range(2):
-                    cols = slice((2 * pair + u) * P, (2 * pair + u + 1) * P)
-                    for a in range(K_PASSES):
-                        nc.tensor.matmul_mx(
-                            out=bank[:, u * CHUNK : (u + 1) * CHUNK],
-                            lhsT=wv_q[b, a][0][:, cols].bitcast(FP8X4),
-                            lhsT_scale=wv_q[b, a][1][:, cols],
-                            rhs=v_codes[a][:, picks].bitcast(FP8X4),
-                            rhs_scale=v_planes[4 * a : P, picks],
-                            start=(a == 0),
-                            stop=(a == K_PASSES - 1),
-                        )
-                for u in range(2):
-                    t = 2 * pair + u
+            for u in range(BANK // CHUNK):
+                for t in range(PACK):
                     nc.scalar.activation(
-                        out=vel[:, t, :],
-                        in_=bank[:, u * CHUNK : (u + 1) * CHUNK],
+                        out=vel[:, t, u * CHUNK : (u + 1) * CHUNK],
+                        in_=vel_banks[t][:, u * CHUNK : (u + 1) * CHUNK],
                         func=IDENTITY,
                         bias=bias[:, PACK * b + t : PACK * b + t + 1],
                         scale=1.0,
                     )
+            sums[half, b] = (vel, pass_by_pass)
+
+        def convective(c, b):
+            vel, have_gradients = sums[c // 2, b]
             h = in_turn("h", h_tiles)
             for s in range(CHUNK // SUB):
-                bank = in_turn("vector", vector_banks)
-                few = slice(c * CHUNK + s * SUB, c * CHUNK + (s + 1) * SUB)
-                for t in range(PACK):
+                within = (c % 2) * CHUNK + s * SUB
+                bank = vector_banks[within // SUB]
+                if not have_gradients:
                     for a in range(K_PASSES):
-                        col = a * H + b * PASS + t * P
-                        nc.tensor.matmul_mx(
-                            out=bank[:, t, :],
-                            lhsT=wg_codes[:, 2 * col : 2 * (col + P)].bitcast(FP4X4),
-                            lhsT_scale=wg_planes[:, col : col + P],
-                            rhs=v_codes[a][:, few].bitcast(FP8X4),
-                            rhs_scale=(v_planes, v_plane1)[a][:, few],
-                            start=(a == 0),
-                            stop=(a == K_PASSES - 1),
-                        )
+                        gradient_pass(bank, c * CHUNK + s * SUB, b, a)
                 nc.vector.tensor_tensor(
                     out=h[:, s * SUB * PACK : (s + 1) * SUB * PACK].rearrange("p (e i t) -> p e t i", t=PACK, i=4),
                     in0=bank[:].rearrange("p t (e i) -> p e t i", i=4),
-                    in1=vel[:, :, s * SUB : (s + 1) * SUB].rearrange("p t (e i) -> p e t i", i=4),
+                    in1=vel[:, :, within : within + SUB].rearrange("p t (e i) -> p e t i", i=4),
                     op=MULT,
                 )
-            quantize(h[:], h_q[c, b][0][:], h_q[c, b][1][:])
+            for s in range(CHUNK // SUB):
+                few = slice(c * CHUNK + s * SUB, c * CHUNK + (s + 1) * SUB)
+                quantize(h[:, s * SUB * PACK : (s + 1) * SUB * PACK], h_q[b][0][:, few], h_q[b][1][:, few])
 
         def project(chunks, m):
             bank = in_turn("scalar", scalar_banks)
             width = len(chunks) * CHUNK
-            for u, c in enumerate(chunks):
-                for b in range(R_PASSES):
-                    nc.tensor.matmul_mx(
-                        out=bank[:, u * CHUNK : (u + 1) * CHUNK],
-                        lhsT=wp_q[m][0][:, b * P : (b + 1) * P].bitcast(FP8X4),
-                        lhsT_scale=wp_q[m][1][:, b * P : (b + 1) * P],
-                        rhs=h_q[c, b][0][:].bitcast(FP8X4),
-                        rhs_scale=h_q[c, b][1][:],
-                        start=(b == 0),
-                        stop=(b == R_PASSES - 1),
-                    )
+            first = chunks[0] * CHUNK
+            for b in range(R_PASSES):
+                nc.tensor.matmul_mx(
+                    out=bank[:, 0:width],
+                    lhsT=wp_q[m][0][:, b * P : (b + 1) * P].bitcast(FP8X4),
+                    lhsT_scale=wp_q[m][1][:, b * P : (b + 1) * P],
+                    rhs=h_q[b][0][:, first : first + width].bitcast(FP8X4),
+                    rhs_scale=h_q[b][1][:, first : first + width],
+                    start=(b == 0),
+                    stop=(b == R_PASSES - 1),
+                )
             y = in_turn("y", y_tiles)
             nc.scalar.copy(out=y[:, 0:width], in_=bank[:, 0:width])
-            first = chunks[0] * CHUNK
             places = scatter_list[:, first // 16 : (first + width) // 16]
             nc.vector.tensor_tensor(
                 out=store[m][:].indirect(places), in0=y[:, 0:width], in1=masses[:, first : first + width], op=MULT
@@ -254,25 +275,40 @@ def tile_list_mesh_convective_terms_kernel(
             if chunks[-1] == CHUNKS - 1:
                 nc.sync.dma_start(out=out[m * P : (m + 1) * P, :], in_=store[m][:])
 
-        for m in range(2):
-            nc.vector.memset(store[m][:], 0.0)
-        gather_codes(0, 0, S)
-        load_table(1)
-        nc.sync.dma_start(out=wg_raw[:].bitcast(I32), in_=wg_words.rearrange("a p n -> p a n").bitcast(I32))
-        nc.gpsimd.memset(words_of(wg_planes_raw), 0)
+        nc.sync.dma_start(gather_list[:], offs)
+        nc.sync.dma_start(scatter_list[:], offs2)
+        load_table(0, 4)
+        load_wv(0, 0, 1, None)
+        load_wg(0)
+        nc.vector.memset(table_planes[:].bitcast(I32), 0)
+        for q in range(4):
+            nc.scalar.dma_start(
+                out=table_planes[32 * q : 32 * q + 8, :].bitcast(I32),
+                in_=tab_scales[:, 4 * q : 4 * q + 4, :].bitcast(I32),
+            )
+        nc.gpsimd.memset(bias_rows[:], 0.0)
+        nc.gpsimd.dma_start(
+            out=bias_rows[0:PACK, :].rearrange("t (g i) -> t g i", i=8),
+            in_=bv.rearrange("(g t i) -> t g i", t=PACK, i=8),
+        )
+        make_identity(nc, identity)
+        load_wv(0, 1, 1, at_raw01)
+        nc.vector.memset(words_of(wg_planes_raw), 0)
+        nc.vector.memset(v_plane1[:].bitcast(I32), 0)
         for q in range(4):
             nc.sync.dma_start(
                 out=wg_planes_raw[32 * q : 32 * q + 4, :, :].bitcast(I32),
                 in_=wg_scales[:, 4 * q : 4 * q + 4, :].rearrange("a r n -> r a n").bitcast(I32),
             )
-        nc.vector.memset(store[2][:], 0.0)
-        gather(v_planes, table_planes[:], 0, S)
-        cast_wv_scalar(0, 0, 0, PASS)
-        load_wv(1, 0, 0, PASS, 24576)
+        load_table(1, 1)
+        for m in range(3):
+            nc.vector.memset(store[m][:], 0.0)
+        gather_codes(0, 0, S)
+        gather(v_planes[:], table_planes[:], 0, S)
+        cast_wv_scalar(0, 0)
         move_second_plane()
-        cast_wv_scalar(0, 1, 0, PASS)
-        load_wv(1, 1, 0, PASS // 2, 40960)
-        load_wv(1, 1, PASS // 2, PASS // 2, 45056)
+        load_wv(1, 0, 1, at_raw10)
+        cast_wv_scalar(0, 1)
         bias_ps = in_turn("scalar", scalar_banks)
         for b in range(R_PASSES):
             nc.tensor.transpose(bias_ps[:, b * P : (b + 1) * P], bias_rows[:, b * P : (b + 1) * P], identity)
@@ -281,42 +317,42 @@ def tile_list_mesh_convective_terms_kernel(
             in_=bias_ps[:, 0 : R_PASSES * P].rearrange("p (b c) -> p b c", c=P)[:, :, 0:PACK],
             func=IDENTITY,
         )
-        gather_codes(1, 0, CHUNK)
         quantize_wv(0, 0)
+        load_wv(1, 1, 1, at_raw11)
+        load_wg(1)
+        nc.vector.memset(store[3][:], 0.0)
+        permute_wg(0)
+        gather_codes(1, 0, BANK)
         quantize_wv(0, 1)
-        load_wp(0, 49152)
-        permute_wg()
-        gather_codes(1, CHUNK, CHUNK)
-        gather_codes(1, 2 * CHUNK, 2 * CHUNK)
-        cast_wv_scalar(1, 0, 0, PASS)
+        gather_codes(1, BANK, BANK)
+        load_wp(0, at_table1 + 64)
         nc.sync.dma_start(out=masses[:], in_=wgo)
-        cast_wv_vector(1, 1, 0, PASS // 2)
-        cast_wv_vector(1, 1, PASS // 2, PASS // 2)
-        load_wp(1, 38912)
+        multiply(0, 0, pass_by_pass=True)
+        convective(0, 0)
+        cast_wv_scalar(1, 0)
+        load_wp(1, at_raw10)
+        convective(1, 0)
+        multiply(1, 0)
+        cast_wv_vector(1, 1)
+        permute_wg(1)
         quantize_wv(1, 0)
         quantize_wv(1, 1)
-        convective(0, 0)
-        store.append(placed([P, T2], F32, "store3", 49152 + 12288))
-        for piece in range(4):
-            nc.gpsimd.memset(store[3][:, piece * BANK : (piece + 1) * BANK], 0.0)
-        convective(0, 1)
-        convective(1, 0)
-        prepare_wp(0)
-        project([0], 0)
-        convective(1, 1)
-        prepare_wp(1)
-        project([0], 1)
-        prepare_wp(2)
-        project([0], 2)
         convective(2, 0)
-        prepare_wp(3)
-        project([0], 3)
         convective(3, 0)
+        prepare_wp(0)
+        multiply(0, 1)
+        convective(0, 1)
+        convective(1, 1)
+        project([0], 0)
+        prepare_wp(1)
+        multiply(1, 1)
         project([1], 0)
+        project([0, 1], 1)
         convective(2, 1)
-        project([1], 1)
+        prepare_wp(2)
+        project([0, 1], 2)
         convective(3, 1)
-        project([1], 2)
-        project([1], 3)
+        prepare_wp(3)
+        project([0, 1], 3)
         for m in range(N_TILES):
             project([2, 3], m)

@@ -45,21 +45,20 @@ def tile_list_mesh_convective_terms_kernel(
             return shared.tile(shape, dtype, name=name, align_bytes=64, offset=offset)
 
         KB = 1024
-        at_raw10, at_planes, at_raw11, at_bf00, at_bf01, at_table1, at_bf11, at_raw01 = 0, 8 * KB - 64, 16 * KB, 24 * KB - 64, 33 * KB, 41 * KB, 50 * KB, 54 * KB
+        at_raw01, at_raw10, at_bf11, at_wp_bf = 0, 8 * KB, 16 * KB, 24 * KB
         gather_list = held([P, S // 16], U16, "gather_list")
         scatter_list = held([P, S // 16], U16, "scatter_list")
-        table = [held([P, T], I32, "table0"), placed([P, T], I32, "table1", at_table1)]
-        table_planes = placed([P, T], U8, "table_planes", at_planes)
-        wg_raw = [held([P, K_PASSES, H], U8, "wg_raw0"), placed([P, K_PASSES, H], U8, "wg_raw1", at_bf00 + 64 + 2 * KB)]
+        table = [held([P, T], I32, "table%d" % a) for a in range(K_PASSES)]
+        table_planes = held([P, T], U8, "table_planes")
+        wg_raw = [held([P, K_PASSES, H], U8, "wg_raw%d" % b) for b in range(R_PASSES)]
         wg_planes_raw = held([P, K_PASSES, H], U8, "wg_planes_raw")
-        masses = placed([P, S], F32, "masses", at_table1 - 4 * KB + 64)
+        masses = held([P, S], F32, "masses")
         identity = held([P, P], F32, "identity")[:]
         bias_rows = held([P, R_PASSES * P], F32, "bias_rows")
         bias = placed([P, R_PASSES * PACK], F32, "bias", at_raw01)
-        store = [held([P, T2], F32, "store%d" % m) for m in range(3)]
-        store.append(placed([P, T2], F32, "store3", at_planes + 64))
+        store = [held([P, T2], F32, "store0"), held([P, T2], F32, "store1")]
         v_codes0 = held([P, S], U32, "v_codes0")
-        v_codes1 = [placed([P, BANK], U32, "v_codes10", at_bf00 + 64), placed([P, BANK], U32, "v_codes11", at_bf01)]
+        v_codes1 = [held([P, BANK], U32, "v_codes1%d" % half) for half in range(2)]
         v_planes = held([P, S], U8, "v_planes")
         v_plane1 = held([P, S], U8, "v_plane1")
 
@@ -98,10 +97,10 @@ def tile_list_mesh_convective_terms_kernel(
 
         wp_raw = {}
 
-        def load_wp(half, offset):
+        def load_wp(half):
             width = N // 2
             for b in range(R_PASSES):
-                wp_raw[b, half] = placed([P, PACK, width], F32, "wp_raw%d%d" % (b, half), offset + 4 * KB * b)
+                wp_raw[b, half] = held([P, PACK, width], F32, "wp_raw%d%d" % (b, half))
                 rows = wp[b * PASS : (b + 1) * PASS, half * width : (half + 1) * width]
                 rows = rows.rearrange("(q t i) n -> t q i n", t=PACK, i=8)
                 for t in range(PACK):
@@ -127,37 +126,41 @@ def tile_list_mesh_convective_terms_kernel(
         def quantized(width, name):
             return held([P, width], U32, name + "_codes"), held([P, width], U8, name + "_scales")
 
-        wv_bf = {
-            (0, 0): placed([P, PASS * PACK], BF16, "wv_bf00", at_bf00),
-            (0, 1): placed([P, PASS * PACK], BF16, "wv_bf01", at_bf01),
-            (1, 0): held([P, PASS * PACK], BF16, "wv_bf10"),
-            (1, 1): placed([P, PASS * PACK], BF16, "wv_bf11", at_bf11),
-        }
+        wv_bf = {(b, a): held([P, PASS * PACK], BF16, "wv_bf%d%d" % (b, a)) for b, a in ((0, 0), (0, 1), (1, 0))}
+        wv_bf[1, 1] = placed([P, PASS * PACK], BF16, "wv_bf11", at_bf11)
         wv_q = {(b, a): quantized(PASS, "wv%d%d" % (b, a)) for b in range(R_PASSES) for a in range(K_PASSES)}
-        wp_q = [(placed([P, R_PASSES * P], U32, "wp0_codes", at_bf11), held([P, R_PASSES * P], U8, "wp0_scales"))]
-        wp_q = wp_q + [quantized(R_PASSES * P, "wp%d" % m) for m in range(1, N_TILES)]
+        wp_q = [quantized(R_PASSES * P, "wp%d" % m) for m in range(N_TILES)]
         h_q = [quantized(S, "h%d" % b) for b in range(R_PASSES)]
-        vel_tiles = [held([P, PACK, BANK], F32, "vel%d" % i) for i in range(2)]
-        h_tiles = [held([P, CHUNK * PACK], BF16, "h_bf%d" % i) for i in range(3)]
-        y_tiles = [held([P, BANK], F32, "y%d" % i) for i in range(3)]
+        vel_tiles = [held([P, PACK, CHUNK], F32, "vel%d" % i) for i in range(4)]
+        h_tiles = [held([P, CHUNK * PACK], BF16, "h_bf%d" % i) for i in range(2)]
+        vel_behind = {
+            (2, 0): placed([P, PACK, CHUNK], F32, "vel20", at_raw10),
+            (0, 1): placed([P, PACK, CHUNK], F32, "vel01", at_wp_bf + KB),
+        }
+        h_behind = {
+            (2, 0): placed([P, CHUNK * PACK], BF16, "h_bf20", at_bf11),
+            (3, 0): placed([P, CHUNK * PACK], BF16, "h_bf30", at_wp_bf - KB),
+        }
+        wp_first = placed([P, CHUNK * PACK], BF16, "wp_bf0", at_wp_bf)
+        y_tiles = [held([P, S], F32, "y%d" % i) for i in range(3)]
 
-        def cast_wv_scalar(b, a):
+        def cast_wv_scalar(b, a, codes=range(PACK)):
             dst = wv_bf[b, a][:].rearrange("p (t q u i j) -> p t q u j i", t=PACK, u=2, i=4, j=PACK)
             src = wv_raw[b, a][:].rearrange("p j (q t u i) -> p t q u j i", t=PACK, u=2, i=4)
-            for t in range(PACK):
+            for t in codes:
                 nc.scalar.copy(out=dst[:, t], in_=src[:, t])
 
-        def cast_wv_vector(b, a):
+        def cast_wv_vector(b, a, codes=slice(0, PACK)):
             nc.vector.tensor_copy(
-                out=wv_bf[b, a][:].rearrange("p (t q i j) -> p t q j i", t=PACK, i=8, j=PACK),
-                in_=wv_raw[b, a][:].rearrange("p j (q t i) -> p t q j i", t=PACK, i=8),
+                out=wv_bf[b, a][:].rearrange("p (t q i j) -> p t q j i", t=PACK, i=8, j=PACK)[:, codes],
+                in_=wv_raw[b, a][:].rearrange("p j (q t i) -> p t q j i", t=PACK, i=8)[:, codes],
             )
 
         def quantize_wv(b, a):
             quantize(wv_bf[b, a][:], wv_q[b, a][0][:], wv_q[b, a][1][:])
 
         def prepare_wp(m):
-            grouped = in_turn("h", h_tiles)
+            grouped = wp_first if m == 0 else in_turn("h", h_tiles)
             for b in range(R_PASSES):
                 nc.scalar.copy(
                     out=grouped[:, b * PASS : (b + 1) * PASS].rearrange("p (c i t) -> p c t i", t=PACK, i=4),
@@ -166,7 +169,7 @@ def tile_list_mesh_convective_terms_kernel(
             quantize(grouped[:], wp_q[m][0][:], wp_q[m][1][:])
 
         wg_codes = [held([P, K_PASSES * 2 * PASS], U8, "wg_codes%d" % b) for b in range(R_PASSES)]
-        wg_planes = [held([P, K_PASSES * PASS], U8, "wg_planes%d" % b) for b in range(R_PASSES)]
+        wg_planes = held([P, K_PASSES * H], U8, "wg_planes")
 
         def load_wg(b):
             words = wg_words[:, :, b * H : (b + 1) * H].rearrange("a p n -> p a n")
@@ -177,9 +180,11 @@ def tile_list_mesh_convective_terms_kernel(
                 out=wg_codes[b][:].bitcast(I32).rearrange("p (a t q w) -> p a t q w", t=PACK, q=16, w=4),
                 in_=words_of(wg_raw[b]).rearrange("p (a q t w) -> p a t q w", t=PACK, q=16, w=4),
             )
+
+        def permute_wg_planes():
             nc.vector.tensor_copy(
-                out=wg_planes[b][:].bitcast(I32).rearrange("p (a t q w) -> p a t q w", t=PACK, q=16, w=2),
-                in_=words_of(wg_planes_raw).rearrange("p (a b q t w) -> p b a t q w", a=K_PASSES, t=PACK, q=16, w=2)[:, b],
+                out=wg_planes[:].bitcast(I32).rearrange("p (g t q w) -> p g t q w", t=PACK, q=16, w=2),
+                in_=words_of(wg_planes_raw).rearrange("p (g q t w) -> p g t q w", t=PACK, q=16, w=2),
             )
 
         def velocity_pass(banks, half, b, a):
@@ -201,7 +206,7 @@ def tile_list_mesh_convective_terms_kernel(
                 nc.tensor.matmul_mx(
                     out=bank[:, t, :],
                     lhsT=wg_codes[b][:, 2 * col : 2 * (col + P)].bitcast(FP4X4),
-                    lhsT_scale=wg_planes[b][:, col : col + P],
+                    lhsT_scale=wg_planes[:, a * H + b * PASS + t * P : a * H + b * PASS + (t + 1) * P],
                     rhs=codes_of(a, first, SUB).bitcast(FP8X4),
                     rhs_scale=(v_planes, v_plane1)[a][:, first : first + SUB],
                     start=(a == 0 and t == 0),
@@ -221,21 +226,21 @@ def tile_list_mesh_convective_terms_kernel(
             else:
                 for a in range(K_PASSES):
                     velocity_pass(vel_banks, half, b, a)
-            vel = in_turn("vel", vel_tiles)
             for u in range(BANK // CHUNK):
+                vel = vel_behind[2 * half + u, b] if (2 * half + u, b) in vel_behind else in_turn("vel", vel_tiles)
+                sums[2 * half + u, b] = (vel, pass_by_pass)
                 for t in range(PACK):
                     nc.scalar.activation(
-                        out=vel[:, t, u * CHUNK : (u + 1) * CHUNK],
+                        out=vel[:, t, :],
                         in_=vel_banks[t][:, u * CHUNK : (u + 1) * CHUNK],
                         func=IDENTITY,
                         bias=bias[:, PACK * b + t : PACK * b + t + 1],
                         scale=1.0,
                     )
-            sums[half, b] = (vel, pass_by_pass)
 
         def convective(c, b):
-            vel, have_gradients = sums[c // 2, b]
-            h = in_turn("h", h_tiles)
+            vel, have_gradients = sums[c, b]
+            h = h_behind[c, b] if (c, b) in h_behind else in_turn("h", h_tiles)
             for s in range(CHUNK // SUB):
                 within = (c % 2) * CHUNK + s * SUB
                 bank = vector_banks[within // SUB]
@@ -245,70 +250,82 @@ def tile_list_mesh_convective_terms_kernel(
                 nc.vector.tensor_tensor(
                     out=h[:, s * SUB * PACK : (s + 1) * SUB * PACK].rearrange("p (e i t) -> p e t i", t=PACK, i=4),
                     in0=bank[:].rearrange("p t (e i) -> p e t i", i=4),
-                    in1=vel[:, :, within : within + SUB].rearrange("p t (e i) -> p e t i", i=4),
+                    in1=vel[:, :, s * SUB : (s + 1) * SUB].rearrange("p t (e i) -> p e t i", i=4),
                     op=MULT,
                 )
             for s in range(CHUNK // SUB):
                 few = slice(c * CHUNK + s * SUB, c * CHUNK + (s + 1) * SUB)
                 quantize(h[:, s * SUB * PACK : (s + 1) * SUB * PACK], h_q[b][0][:, few], h_q[b][1][:, few])
 
-        def project(chunks, m):
-            bank = in_turn("scalar", scalar_banks)
-            width = len(chunks) * CHUNK
-            first = chunks[0] * CHUNK
-            for b in range(R_PASSES):
-                nc.tensor.matmul_mx(
-                    out=bank[:, 0:width],
-                    lhsT=wp_q[m][0][:, b * P : (b + 1) * P].bitcast(FP8X4),
-                    lhsT_scale=wp_q[m][1][:, b * P : (b + 1) * P],
-                    rhs=h_q[b][0][:, first : first + width].bitcast(FP8X4),
-                    rhs_scale=h_q[b][1][:, first : first + width],
-                    start=(b == 0),
-                    stop=(b == R_PASSES - 1),
-                )
+        def project(m, first, count):
             y = in_turn("y", y_tiles)
-            nc.scalar.copy(out=y[:, 0:width], in_=bank[:, 0:width])
-            places = scatter_list[:, first // 16 : (first + width) // 16]
+            done = 0
+            while done < count:
+                width = min(BANK - (first + done) % BANK, count - done)
+                picks = slice(first + done, first + done + width)
+                bank = in_turn("scalar", scalar_banks)
+                for b in range(R_PASSES):
+                    nc.tensor.matmul_mx(
+                        out=bank[:, 0:width],
+                        lhsT=wp_q[m][0][:, b * P : (b + 1) * P].bitcast(FP8X4),
+                        lhsT_scale=wp_q[m][1][:, b * P : (b + 1) * P],
+                        rhs=h_q[b][0][:, picks].bitcast(FP8X4),
+                        rhs_scale=h_q[b][1][:, picks],
+                        start=(b == 0),
+                        stop=(b == R_PASSES - 1),
+                    )
+                nc.scalar.copy(out=y[:, done : done + width], in_=bank[:, 0:width])
+                done = done + width
+            places = scatter_list[:, first // 16 : (first + count) // 16]
             nc.vector.tensor_tensor(
-                out=store[m][:].indirect(places), in0=y[:, 0:width], in1=masses[:, first : first + width], op=MULT
+                out=store[m % 2][:].indirect(places), in0=y[:, 0:count], in1=masses[:, first : first + count], op=MULT
             )
-            if chunks[-1] == CHUNKS - 1:
-                nc.sync.dma_start(out=out[m * P : (m + 1) * P, :], in_=store[m][:])
+            if first + count == S:
+                nc.sync.dma_start(out=out[m * P : (m + 1) * P, :], in_=store[m % 2][:])
 
+        load_table(0, 1)
         nc.sync.dma_start(gather_list[:], offs)
-        nc.sync.dma_start(scatter_list[:], offs2)
-        load_table(0, 4)
-        load_wv(0, 0, 1, None)
-        load_wg(0)
         nc.vector.memset(table_planes[:].bitcast(I32), 0)
         for q in range(4):
-            nc.scalar.dma_start(
+            nc.sync.dma_start(
                 out=table_planes[32 * q : 32 * q + 8, :].bitcast(I32),
                 in_=tab_scales[:, 4 * q : 4 * q + 4, :].bitcast(I32),
             )
+        load_wv(0, 0, 1, None)
+        nc.sync.dma_start(scatter_list[:], offs2)
+        load_wg(0)
+        nc.vector.memset(words_of(wg_planes_raw), 0)
+        for q in range(4):
+            nc.sync.dma_start(
+                out=wg_planes_raw[32 * q : 32 * q + 4, :, :].bitcast(I32),
+                in_=wg_scales[:, 4 * q : 4 * q + 4, :].rearrange("a r n -> r a n").bitcast(I32),
+            )
+        load_wv(0, 1, 1, at_raw01)
+        load_table(1, 1)
+        nc.vector.memset(v_plane1[:].bitcast(I32), 0)
         nc.gpsimd.memset(bias_rows[:], 0.0)
         nc.gpsimd.dma_start(
             out=bias_rows[0:PACK, :].rearrange("t (g i) -> t g i", i=8),
             in_=bv.rearrange("(g t i) -> t g i", t=PACK, i=8),
         )
         make_identity(nc, identity)
-        load_wv(0, 1, 1, at_raw01)
-        nc.vector.memset(words_of(wg_planes_raw), 0)
-        nc.vector.memset(v_plane1[:].bitcast(I32), 0)
-        for q in range(4):
-            nc.sync.dma_start(
-                out=wg_planes_raw[32 * q : 32 * q + 4, :, :].bitcast(I32),
-                in_=wg_scales[:, 4 * q : 4 * q + 4, :].rearrange("a r n -> r a n").bitcast(I32),
-            )
-        load_table(1, 1)
-        for m in range(3):
-            nc.vector.memset(store[m][:], 0.0)
+        for tile in store:
+            nc.vector.memset(tile[:], 0.0)
         gather_codes(0, 0, S)
         gather(v_planes[:], table_planes[:], 0, S)
-        cast_wv_scalar(0, 0)
         move_second_plane()
         load_wv(1, 0, 1, at_raw10)
-        cast_wv_scalar(0, 1)
+        load_wv(1, 1, 1, None)
+        load_wg(1)
+        load_wp(0)
+        nc.sync.dma_start(out=masses[:], in_=wgo)
+        load_wp(1)
+        cast_wv_scalar(0, 0)
+        permute_wg(0)
+        quantize_wv(0, 0)
+        permute_wg_planes()
+        cast_wv_scalar(0, 1, range(0, 2))
+        cast_wv_vector(0, 1, slice(2, 4))
         bias_ps = in_turn("scalar", scalar_banks)
         for b in range(R_PASSES):
             nc.tensor.transpose(bias_ps[:, b * P : (b + 1) * P], bias_rows[:, b * P : (b + 1) * P], identity)
@@ -317,42 +334,33 @@ def tile_list_mesh_convective_terms_kernel(
             in_=bias_ps[:, 0 : R_PASSES * P].rearrange("p (b c) -> p b c", c=P)[:, :, 0:PACK],
             func=IDENTITY,
         )
-        quantize_wv(0, 0)
-        load_wv(1, 1, 1, at_raw11)
-        load_wg(1)
-        nc.vector.memset(store[3][:], 0.0)
-        permute_wg(0)
-        gather_codes(1, 0, BANK)
         quantize_wv(0, 1)
+        gather_codes(1, 0, BANK)
         gather_codes(1, BANK, BANK)
-        load_wp(0, at_table1 + 64)
-        nc.sync.dma_start(out=masses[:], in_=wgo)
         multiply(0, 0, pass_by_pass=True)
         convective(0, 0)
         cast_wv_scalar(1, 0)
-        load_wp(1, at_raw10)
         convective(1, 0)
-        multiply(1, 0)
         cast_wv_vector(1, 1)
         permute_wg(1)
         quantize_wv(1, 0)
         quantize_wv(1, 1)
+        multiply(1, 0)
         convective(2, 0)
-        convective(3, 0)
         prepare_wp(0)
+        convective(3, 0)
         multiply(0, 1)
         convective(0, 1)
         convective(1, 1)
-        project([0], 0)
+        project(0, 0, CHUNK)
         prepare_wp(1)
         multiply(1, 1)
-        project([1], 0)
-        project([0, 1], 1)
         convective(2, 1)
-        prepare_wp(2)
-        project([0, 1], 2)
+        project(0, CHUNK, CHUNK)
         convective(3, 1)
-        prepare_wp(3)
-        project([0, 1], 3)
-        for m in range(N_TILES):
-            project([2, 3], m)
+        project(1, 0, CHUNK)
+        project(0, BANK, BANK)
+        project(1, CHUNK, S - CHUNK)
+        for m in range(2, N_TILES):
+            prepare_wp(m)
+            project(m, 0, S)

@@ -45,27 +45,25 @@ def tile_list_mesh_convective_terms_kernel(
             return shared.tile(shape, dtype, name=name, align_bytes=64, offset=offset)
 
         KB = 1024
-        at_raw01, at_raw10, at_bf11, at_wp_bf = 0, 8 * KB, 16 * KB, 24 * KB
+        at_raw01, at_raw10, at_bf11, at_wp_bf, at_planes, at_y = 0, 8 * KB, 16 * KB, 24 * KB, 32 * KB, 44 * KB
         gather_list = held([P, S // 16], U16, "gather_list")
         scatter_list = held([P, S // 16], U16, "scatter_list")
         table = [held([P, T], I32, "table%d" % a) for a in range(K_PASSES)]
-        table_planes = held([P, T], U8, "table_planes")
+        table_planes = placed([P, T], U8, "table_planes", at_planes)
         wg_raw = [held([P, K_PASSES, H], U8, "wg_raw%d" % b) for b in range(R_PASSES)]
         wg_planes_raw = held([P, K_PASSES, H], U8, "wg_planes_raw")
         masses = held([P, S], F32, "masses")
         identity = held([P, P], F32, "identity")[:]
         bias_rows = held([P, R_PASSES * P], F32, "bias_rows")
         bias = placed([P, R_PASSES * PACK], F32, "bias", at_raw01)
-        store = [held([P, T2], F32, "store0"), held([P, T2], F32, "store1")]
+        store = [held([P, T2], F32, "store0"), held([P, T2], F32, "store1"), placed([P, T2], F32, "store2", at_planes)]
         v_codes0 = held([P, S], U32, "v_codes0")
-        v_codes1 = [held([P, BANK], U32, "v_codes1%d" % half) for half in range(2)]
+        v_codes1 = held([P, S], U32, "v_codes1")
         v_planes = held([P, S], U8, "v_planes")
         v_plane1 = held([P, S], U8, "v_plane1")
 
         def codes_of(a, first, count):
-            if a == 0:
-                return v_codes0[:, first : first + count]
-            return v_codes1[first // BANK][:, first % BANK : first % BANK + count]
+            return (v_codes0, v_codes1)[a][:, first : first + count]
 
         scalar_banks = [psum.tile([P, BANK], F32, name="scalar_bank%d" % i) for i in range(4)]
         vector_banks = [psum.tile([P, PACK, SUB], F32, name="vector_bank%d" % i) for i in range(4)]
@@ -78,12 +76,9 @@ def tile_list_mesh_convective_terms_kernel(
         def words_of(planes):
             return planes[:].rearrange("p a n -> p (a n)").bitcast(I32)
 
-        def load_table(a, pieces):
+        def load_table(a, cols=slice(0, T)):
             words = tab_words[a].rearrange("p t i -> p (t i)").bitcast(I32)
-            width = T // pieces
-            for piece in range(pieces):
-                cols = slice(piece * width, (piece + 1) * width)
-                nc.sync.dma_start(out=table[a][:, cols], in_=words[:, cols])
+            nc.sync.dma_start(out=table[a][:, cols], in_=words[:, cols])
 
         wv_raw = {}
 
@@ -129,19 +124,22 @@ def tile_list_mesh_convective_terms_kernel(
         wv_bf = {(b, a): held([P, PASS * PACK], BF16, "wv_bf%d%d" % (b, a)) for b, a in ((0, 0), (0, 1), (1, 0))}
         wv_bf[1, 1] = placed([P, PASS * PACK], BF16, "wv_bf11", at_bf11)
         wv_q = {(b, a): quantized(PASS, "wv%d%d" % (b, a)) for b in range(R_PASSES) for a in range(K_PASSES)}
-        wp_q = [quantized(R_PASSES * P, "wp%d" % m) for m in range(N_TILES)]
+        wp_q = quantized(N_TILES * R_PASSES * P, "wp")
         h_q = [quantized(S, "h%d" % b) for b in range(R_PASSES)]
         vel_tiles = [held([P, PACK, CHUNK], F32, "vel%d" % i) for i in range(4)]
-        h_tiles = [held([P, CHUNK * PACK], BF16, "h_bf%d" % i) for i in range(2)]
+        h_tiles = [held([P, CHUNK * PACK], BF16, "h_bf%d" % i) for i in range(3)]
         vel_behind = {
             (2, 0): placed([P, PACK, CHUNK], F32, "vel20", at_raw10),
-            (0, 1): placed([P, PACK, CHUNK], F32, "vel01", at_wp_bf + KB),
         }
         h_behind = {
             (2, 0): placed([P, CHUNK * PACK], BF16, "h_bf20", at_bf11),
-            (3, 0): placed([P, CHUNK * PACK], BF16, "h_bf30", at_wp_bf - KB),
+            (1, 1): placed([P, CHUNK * PACK], BF16, "h_bf11", at_wp_bf - KB),
+            (3, 0): placed([P, CHUNK * PACK], BF16, "h_bf30", at_y),
         }
         wp_first = placed([P, CHUNK * PACK], BF16, "wp_bf0", at_wp_bf)
+        wp_second = placed([P, CHUNK * PACK], BF16, "wp_bf1", at_wp_bf + KB)
+        wp_last = held([P, 2 * CHUNK * PACK], BF16, "wp_bf23")
+        y_first = placed([P, CHUNK], F32, "y_first", at_y)
         y_tiles = [held([P, S], F32, "y%d" % i) for i in range(3)]
 
         def cast_wv_scalar(b, a, codes=range(PACK)):
@@ -159,14 +157,16 @@ def tile_list_mesh_convective_terms_kernel(
         def quantize_wv(b, a):
             quantize(wv_bf[b, a][:], wv_q[b, a][0][:], wv_q[b, a][1][:])
 
-        def prepare_wp(m):
-            grouped = wp_first if m == 0 else in_turn("h", h_tiles)
-            for b in range(R_PASSES):
-                nc.scalar.copy(
-                    out=grouped[:, b * PASS : (b + 1) * PASS].rearrange("p (c i t) -> p c t i", t=PACK, i=4),
-                    in_=wp_raw[b, m // 2][:, :, (m % 2) * P : (m % 2 + 1) * P].rearrange("p t (c i) -> p c t i", i=4),
-                )
-            quantize(grouped[:], wp_q[m][0][:], wp_q[m][1][:])
+        def prepare_wp(tiles, grouped):
+            for u, m in enumerate(tiles):
+                for b in range(R_PASSES):
+                    first = (u * R_PASSES + b) * PASS
+                    nc.scalar.copy(
+                        out=grouped[:, first : first + PASS].rearrange("p (c i t) -> p c t i", t=PACK, i=4),
+                        in_=wp_raw[b, m // 2][:, :, (m % 2) * P : (m % 2 + 1) * P].rearrange("p t (c i) -> p c t i", i=4),
+                    )
+            cols = slice(tiles[0] * R_PASSES * P, (tiles[-1] + 1) * R_PASSES * P)
+            quantize(grouped[:], wp_q[0][:, cols], wp_q[1][:, cols])
 
         wg_codes = [held([P, K_PASSES * 2 * PASS], U8, "wg_codes%d" % b) for b in range(R_PASSES)]
         wg_planes = held([P, K_PASSES * H], U8, "wg_planes")
@@ -187,17 +187,17 @@ def tile_list_mesh_convective_terms_kernel(
                 in_=words_of(wg_planes_raw).rearrange("p (g q t w) -> p g t q w", t=PACK, q=16, w=2),
             )
 
-        def velocity_pass(banks, half, b, a):
+        def velocity_pass(banks, c, b, a):
             for t in range(PACK):
                 cols = slice(t * P, (t + 1) * P)
                 nc.tensor.matmul_mx(
-                    out=banks[t][:],
+                    out=banks[t // 2][:, (t % 2) * CHUNK : (t % 2 + 1) * CHUNK],
                     lhsT=wv_q[b, a][0][:, cols].bitcast(FP8X4),
                     lhsT_scale=wv_q[b, a][1][:, cols],
-                    rhs=codes_of(a, half * BANK, BANK).bitcast(FP8X4),
-                    rhs_scale=v_planes[4 * a : P, half * BANK : (half + 1) * BANK],
-                    start=(a == 0),
-                    stop=(a == K_PASSES - 1),
+                    rhs=codes_of(a, c * CHUNK, CHUNK).bitcast(FP8X4),
+                    rhs_scale=v_planes[4 * a : P, c * CHUNK : (c + 1) * CHUNK],
+                    start=(a == 0 and t % 2 == 0),
+                    stop=(a == K_PASSES - 1 and t % 2 == 1),
                 )
 
         def gradient_pass(bank, first, b, a):
@@ -213,77 +213,91 @@ def tile_list_mesh_convective_terms_kernel(
                     stop=(a == K_PASSES - 1 and t == PACK - 1),
                 )
 
-        sums = {}
+        banks_of = {}
+        rounded = {}
 
-        def multiply(half, b, pass_by_pass=False):
-            vel_banks = [in_turn("scalar", scalar_banks) for t in range(PACK)]
-            subs = range(BANK // SUB)
-            if pass_by_pass:
-                for a in range(K_PASSES):
-                    velocity_pass(vel_banks, half, b, a)
-                    for s in subs:
-                        gradient_pass(vector_banks[s], half * BANK + s * SUB, b, a)
-            else:
-                for a in range(K_PASSES):
-                    velocity_pass(vel_banks, half, b, a)
-            for u in range(BANK // CHUNK):
-                vel = vel_behind[2 * half + u, b] if (2 * half + u, b) in vel_behind else in_turn("vel", vel_tiles)
-                sums[2 * half + u, b] = (vel, pass_by_pass)
-                for t in range(PACK):
-                    nc.scalar.activation(
-                        out=vel[:, t, :],
-                        in_=vel_banks[t][:, u * CHUNK : (u + 1) * CHUNK],
-                        func=IDENTITY,
-                        bias=bias[:, PACK * b + t : PACK * b + t + 1],
-                        scale=1.0,
-                    )
+        def multiply(c, b, a):
+            if a == 0:
+                banks_of[c, b] = (
+                    [in_turn("scalar", scalar_banks) for pair in range(PACK // 2)],
+                    [in_turn("vector", vector_banks) for s in range(CHUNK // SUB)],
+                )
+            velocity_pass(banks_of[c, b][0], c, b, a)
+            for s, bank in enumerate(banks_of[c, b][1]):
+                gradient_pass(bank, c * CHUNK + s * SUB, b, a)
 
-        def convective(c, b):
-            vel, have_gradients = sums[c, b]
+        def gradients(c, b):
+            banks = [in_turn("vector", vector_banks) for s in range(CHUNK // SUB)]
+            for s, bank in enumerate(banks):
+                for a in range(K_PASSES):
+                    gradient_pass(bank, c * CHUNK + s * SUB, b, a)
+            return banks
+
+        def velocities(c, b):
+            banks = [in_turn("scalar", scalar_banks) for pair in range(PACK // 2)]
+            for a in range(K_PASSES):
+                velocity_pass(banks, c, b, a)
+            return banks
+
+        def convective(c, b, gradients_first=False):
+            if (c, b) not in banks_of:
+                if gradients_first:
+                    grad_banks = gradients(c, b)
+                    banks_of[c, b] = (velocities(c, b), grad_banks)
+                else:
+                    vel_banks = velocities(c, b)
+                    banks_of[c, b] = (vel_banks, gradients(c, b))
+            vel_banks, grad_banks = banks_of[c, b]
+            vel = vel_behind[c, b] if (c, b) in vel_behind else in_turn("vel", vel_tiles)
+            for t in range(PACK):
+                nc.scalar.activation(
+                    out=vel[:, t, :],
+                    in_=vel_banks[t // 2][:, (t % 2) * CHUNK : (t % 2 + 1) * CHUNK],
+                    func=IDENTITY,
+                    bias=bias[:, PACK * b + t : PACK * b + t + 1],
+                    scale=1.0,
+                )
             h = h_behind[c, b] if (c, b) in h_behind else in_turn("h", h_tiles)
-            for s in range(CHUNK // SUB):
-                within = (c % 2) * CHUNK + s * SUB
-                bank = vector_banks[within // SUB]
-                if not have_gradients:
-                    for a in range(K_PASSES):
-                        gradient_pass(bank, c * CHUNK + s * SUB, b, a)
+            for s, bank in enumerate(grad_banks):
                 nc.vector.tensor_tensor(
                     out=h[:, s * SUB * PACK : (s + 1) * SUB * PACK].rearrange("p (e i t) -> p e t i", t=PACK, i=4),
                     in0=bank[:].rearrange("p t (e i) -> p e t i", i=4),
                     in1=vel[:, :, s * SUB : (s + 1) * SUB].rearrange("p t (e i) -> p e t i", i=4),
                     op=MULT,
                 )
-            for s in range(CHUNK // SUB):
-                few = slice(c * CHUNK + s * SUB, c * CHUNK + (s + 1) * SUB)
-                quantize(h[:, s * SUB * PACK : (s + 1) * SUB * PACK], h_q[b][0][:, few], h_q[b][1][:, few])
+            rounded[c, b] = h
+
+        def quantize_h(c, b):
+            picks = slice(c * CHUNK, (c + 1) * CHUNK)
+            quantize(rounded[c, b][:], h_q[b][0][:, picks], h_q[b][1][:, picks])
 
         def project(m, first, count):
-            y = in_turn("y", y_tiles)
+            y = y_first if (m, first) == (0, 0) else in_turn("y", y_tiles)
             done = 0
             while done < count:
                 width = min(BANK - (first + done) % BANK, count - done)
                 picks = slice(first + done, first + done + width)
                 bank = in_turn("scalar", scalar_banks)
-                for b in range(R_PASSES):
+                for b in reversed(range(R_PASSES)):
                     nc.tensor.matmul_mx(
                         out=bank[:, 0:width],
-                        lhsT=wp_q[m][0][:, b * P : (b + 1) * P].bitcast(FP8X4),
-                        lhsT_scale=wp_q[m][1][:, b * P : (b + 1) * P],
+                        lhsT=wp_q[0][:, (m * R_PASSES + b) * P : (m * R_PASSES + b + 1) * P].bitcast(FP8X4),
+                        lhsT_scale=wp_q[1][:, (m * R_PASSES + b) * P : (m * R_PASSES + b + 1) * P],
                         rhs=h_q[b][0][:, picks].bitcast(FP8X4),
                         rhs_scale=h_q[b][1][:, picks],
-                        start=(b == 0),
-                        stop=(b == R_PASSES - 1),
+                        start=(b == R_PASSES - 1),
+                        stop=(b == 0),
                     )
                 nc.scalar.copy(out=y[:, done : done + width], in_=bank[:, 0:width])
                 done = done + width
             places = scatter_list[:, first // 16 : (first + count) // 16]
             nc.vector.tensor_tensor(
-                out=store[m % 2][:].indirect(places), in0=y[:, 0:count], in1=masses[:, first : first + count], op=MULT
+                out=store[m % 3][:].indirect(places), in0=y[:, 0:count], in1=masses[:, first : first + count], op=MULT
             )
             if first + count == S:
-                nc.sync.dma_start(out=out[m * P : (m + 1) * P, :], in_=store[m % 2][:])
+                nc.sync.dma_start(out=out[m * P : (m + 1) * P, :], in_=store[m % 3][:])
 
-        load_table(0, 1)
+        load_table(0)
         nc.sync.dma_start(gather_list[:], offs)
         nc.vector.memset(table_planes[:].bitcast(I32), 0)
         for q in range(4):
@@ -301,7 +315,7 @@ def tile_list_mesh_convective_terms_kernel(
                 in_=wg_scales[:, 4 * q : 4 * q + 4, :].rearrange("a r n -> r a n").bitcast(I32),
             )
         load_wv(0, 1, 1, at_raw01)
-        load_table(1, 1)
+        load_table(1, slice(0, T // 2))
         nc.vector.memset(v_plane1[:].bitcast(I32), 0)
         nc.gpsimd.memset(bias_rows[:], 0.0)
         nc.gpsimd.dma_start(
@@ -309,24 +323,26 @@ def tile_list_mesh_convective_terms_kernel(
             in_=bv.rearrange("(g t i) -> t g i", t=PACK, i=8),
         )
         make_identity(nc, identity)
-        for tile in store:
+        for tile in store[0:2]:
             nc.vector.memset(tile[:], 0.0)
         gather_codes(0, 0, S)
         gather(v_planes[:], table_planes[:], 0, S)
         move_second_plane()
+        load_table(1, slice(T // 2, T))
         load_wv(1, 0, 1, at_raw10)
-        load_wv(1, 1, 1, None)
         load_wg(1)
+        load_wv(1, 1, 1, None)
         load_wp(0)
         nc.sync.dma_start(out=masses[:], in_=wgo)
         load_wp(1)
+        nc.vector.memset(store[2][:], 0.0)
         cast_wv_scalar(0, 0)
         permute_wg(0)
-        quantize_wv(0, 0)
         permute_wg_planes()
+        quantize_wv(0, 0)
         cast_wv_scalar(0, 1, range(0, 2))
         cast_wv_vector(0, 1, slice(2, 4))
-        bias_ps = in_turn("scalar", scalar_banks)
+        bias_ps = vector_banks[3][:].rearrange("p t s -> p (t s)")
         for b in range(R_PASSES):
             nc.tensor.transpose(bias_ps[:, b * P : (b + 1) * P], bias_rows[:, b * P : (b + 1) * P], identity)
         nc.scalar.activation(
@@ -335,32 +351,42 @@ def tile_list_mesh_convective_terms_kernel(
             func=IDENTITY,
         )
         quantize_wv(0, 1)
-        gather_codes(1, 0, BANK)
+        for c in range(2):
+            multiply(c, 0, 0)
+        gather_codes(1, 0, CHUNK)
+        multiply(0, 0, 1)
+        gather_codes(1, CHUNK, CHUNK)
+        multiply(1, 0, 1)
         gather_codes(1, BANK, BANK)
-        multiply(0, 0, pass_by_pass=True)
         convective(0, 0)
-        cast_wv_scalar(1, 0)
         convective(1, 0)
-        cast_wv_vector(1, 1)
         permute_wg(1)
+        quantize_h(0, 0)
+        quantize_h(1, 0)
+        cast_wv_scalar(1, 0)
+        cast_wv_vector(1, 1)
         quantize_wv(1, 0)
         quantize_wv(1, 1)
-        multiply(1, 0)
         convective(2, 0)
-        prepare_wp(0)
-        convective(3, 0)
-        multiply(0, 1)
-        convective(0, 1)
-        convective(1, 1)
+        convective(0, 1, gradients_first=True)
+        quantize_h(2, 0)
+        prepare_wp([0], wp_first)
+        quantize_h(0, 1)
         project(0, 0, CHUNK)
-        prepare_wp(1)
-        multiply(1, 1)
+        convective(1, 1)
+        convective(3, 0)
+        quantize_h(1, 1)
+        prepare_wp([1], wp_second)
+        quantize_h(3, 0)
         convective(2, 1)
         project(0, CHUNK, CHUNK)
+        quantize_h(2, 1)
         convective(3, 1)
         project(1, 0, CHUNK)
+        quantize_h(3, 1)
+        project(1, CHUNK, CHUNK)
         project(0, BANK, BANK)
-        project(1, CHUNK, S - CHUNK)
+        project(1, BANK, BANK)
+        prepare_wp([2, 3], wp_last)
         for m in range(2, N_TILES):
-            prepare_wp(m)
             project(m, 0, S)

@@ -109,11 +109,8 @@ def tile_list_mesh_convective_terms_kernel(
             gather(codes_of(a, first, count), table[a][:].bitcast(U32), first, count)
 
         def move_second_plane():
-            for q in range(4):
-                nc.sync.dma_start(
-                    out=v_plane1[32 * q : 32 * q + 4, :].bitcast(I32),
-                    in_=v_planes[32 * q + 4 : 32 * q + 8, :].bitcast(I32),
-                )
+            for r in range(4):
+                nc.sync.dma_start(out=v_plane1[r:P:32, :].bitcast(I32), in_=v_planes[8 + r : 24 : 4, :].bitcast(I32))
 
         def quantize(grouped, codes, scales):
             nc.vector.quantize_mx(out=codes.bitcast(FP8X4), scales=scales, in_=grouped)
@@ -195,7 +192,7 @@ def tile_list_mesh_convective_terms_kernel(
                     lhsT=wv_q[b, a][0][:, cols].bitcast(FP8X4),
                     lhsT_scale=wv_q[b, a][1][:, cols],
                     rhs=codes_of(a, c * CHUNK, CHUNK).bitcast(FP8X4),
-                    rhs_scale=v_planes[4 * a : P, c * CHUNK : (c + 1) * CHUNK],
+                    rhs_scale=(v_planes, v_plane1)[a][:, c * CHUNK : (c + 1) * CHUNK],
                     start=(a == 0 and t % 2 == 0),
                     stop=(a == K_PASSES - 1 and t % 2 == 1),
                 )
@@ -300,19 +297,17 @@ def tile_list_mesh_convective_terms_kernel(
         load_table(0)
         nc.sync.dma_start(gather_list[:], offs)
         nc.vector.memset(table_planes[:].bitcast(I32), 0)
-        for q in range(4):
-            nc.sync.dma_start(
-                out=table_planes[32 * q : 32 * q + 8, :].bitcast(I32),
-                in_=tab_scales[:, 4 * q : 4 * q + 4, :].bitcast(I32),
-            )
+        for r in range(4):
+            nc.sync.dma_start(out=table_planes[r:P:32, :].bitcast(I32), in_=tab_scales[0, r:16:4, :].bitcast(I32))
+        nc.sync.dma_start(out=table_planes[8:24, :].bitcast(I32), in_=tab_scales[1].bitcast(I32))
         load_wv(0, 0, 1, None)
         nc.sync.dma_start(scatter_list[:], offs2)
         load_wg(0)
         nc.vector.memset(words_of(wg_planes_raw), 0)
-        for q in range(4):
+        for r in range(4):
             nc.sync.dma_start(
-                out=wg_planes_raw[32 * q : 32 * q + 4, :, :].bitcast(I32),
-                in_=wg_scales[:, 4 * q : 4 * q + 4, :].rearrange("a r n -> r a n").bitcast(I32),
+                out=wg_planes_raw[r:P:32, :, :].bitcast(I32),
+                in_=wg_scales[:, r:16:4, :].rearrange("a q n -> q a n").bitcast(I32),
             )
         load_wv(0, 1, 1, at_raw01)
         load_table(1, slice(0, T // 2))

@@ -45,18 +45,18 @@ def tile_list_mesh_convective_terms_kernel(
             return shared.tile(shape, dtype, name=name, align_bytes=64, offset=offset)
 
         KB = 1024
-        at_raw01, at_raw10, at_bf11, at_wp_bf, at_planes, at_y = 0, 8 * KB, 16 * KB, 24 * KB, 32 * KB, 44 * KB
+        at_raw01, at_raw10, at_bf10, at_wp_bf, at_bf00, at_y = 0, 8 * KB, 16 * KB, 24 * KB, 32 * KB, 44 * KB
         gather_list = held([P, S // 16], U16, "gather_list")
         scatter_list = held([P, S // 16], U16, "scatter_list")
         table = [held([P, T], I32, "table%d" % a) for a in range(K_PASSES)]
-        table_planes = placed([P, T], U8, "table_planes", at_planes)
+        table_planes = held([P, T], U8, "table_planes")
         wg_raw = [held([P, K_PASSES, H], U8, "wg_raw%d" % b) for b in range(R_PASSES)]
         wg_planes_raw = held([P, K_PASSES, H], U8, "wg_planes_raw")
         masses = held([P, S], F32, "masses")
         identity = held([P, P], F32, "identity")[:]
         bias_rows = held([P, R_PASSES * P], F32, "bias_rows")
         bias = placed([P, R_PASSES * PACK], F32, "bias", at_raw01)
-        store = [held([P, T2], F32, "store0"), held([P, T2], F32, "store1"), placed([P, T2], F32, "store2", at_planes)]
+        store = [held([P, T2], F32, "store0"), held([P, T2], F32, "store1"), placed([P, T2], F32, "store2", at_bf00)]
         v_codes0 = held([P, S], U32, "v_codes0")
         v_codes1 = held([P, S], U32, "v_codes1")
         v_planes = held([P, S], U8, "v_planes")
@@ -76,9 +76,9 @@ def tile_list_mesh_convective_terms_kernel(
         def words_of(planes):
             return planes[:].rearrange("p a n -> p (a n)").bitcast(I32)
 
-        def load_table(a, cols=slice(0, T)):
+        def load_table(a):
             words = tab_words[a].rearrange("p t i -> p (t i)").bitcast(I32)
-            nc.sync.dma_start(out=table[a][:, cols], in_=words[:, cols])
+            nc.sync.dma_start(out=table[a][:], in_=words)
 
         wv_raw = {}
 
@@ -118,8 +118,9 @@ def tile_list_mesh_convective_terms_kernel(
         def quantized(width, name):
             return held([P, width], U32, name + "_codes"), held([P, width], U8, name + "_scales")
 
-        wv_bf = {(b, a): held([P, PASS * PACK], BF16, "wv_bf%d%d" % (b, a)) for b, a in ((0, 0), (0, 1), (1, 0))}
-        wv_bf[1, 1] = placed([P, PASS * PACK], BF16, "wv_bf11", at_bf11)
+        wv_bf = {(b, a): held([P, PASS * PACK], BF16, "wv_bf%d%d" % (b, a)) for b, a in ((0, 1), (1, 1))}
+        wv_bf[0, 0] = placed([P, PASS * PACK], BF16, "wv_bf00", at_bf00)
+        wv_bf[1, 0] = placed([P, PASS * PACK], BF16, "wv_bf10", at_bf10)
         wv_q = {(b, a): quantized(PASS, "wv%d%d" % (b, a)) for b in range(R_PASSES) for a in range(K_PASSES)}
         wp_q = quantized(N_TILES * R_PASSES * P, "wp")
         h_q = [quantized(S, "h%d" % b) for b in range(R_PASSES)]
@@ -129,14 +130,12 @@ def tile_list_mesh_convective_terms_kernel(
             (2, 0): placed([P, PACK, CHUNK], F32, "vel20", at_raw10),
         }
         h_behind = {
-            (2, 0): placed([P, CHUNK * PACK], BF16, "h_bf20", at_bf11),
-            (1, 1): placed([P, CHUNK * PACK], BF16, "h_bf11", at_wp_bf - KB),
-            (3, 0): placed([P, CHUNK * PACK], BF16, "h_bf30", at_y),
+            (2, 0): placed([P, CHUNK * PACK], BF16, "h_bf20", at_bf10),
+            (3, 0): placed([P, CHUNK * PACK], BF16, "h_bf30", at_bf10 + 2 * KB),
         }
         wp_first = placed([P, CHUNK * PACK], BF16, "wp_bf0", at_wp_bf)
         wp_second = placed([P, CHUNK * PACK], BF16, "wp_bf1", at_wp_bf + KB)
         wp_last = held([P, 2 * CHUNK * PACK], BF16, "wp_bf23")
-        y_first = placed([P, CHUNK], F32, "y_first", at_y)
         y_tiles = [held([P, S], F32, "y%d" % i) for i in range(3)]
 
         def cast_wv_scalar(b, a, codes=range(PACK)):
@@ -269,7 +268,7 @@ def tile_list_mesh_convective_terms_kernel(
             quantize(rounded[c, b][:], h_q[b][0][:, picks], h_q[b][1][:, picks])
 
         def project(m, first, count):
-            y = y_first if (m, first) == (0, 0) else in_turn("y", y_tiles)
+            y = in_turn("y", y_tiles)
             done = 0
             while done < count:
                 width = min(BANK - (first + done) % BANK, count - done)
@@ -310,7 +309,7 @@ def tile_list_mesh_convective_terms_kernel(
                 in_=wg_scales[:, r:16:4, :].rearrange("a q n -> q a n").bitcast(I32),
             )
         load_wv(0, 1, 1, at_raw01)
-        load_table(1, slice(0, T // 2))
+        load_table(1)
         nc.vector.memset(v_plane1[:].bitcast(I32), 0)
         nc.gpsimd.memset(bias_rows[:], 0.0)
         nc.gpsimd.dma_start(
@@ -323,18 +322,18 @@ def tile_list_mesh_convective_terms_kernel(
         gather_codes(0, 0, S)
         gather(v_planes[:], table_planes[:], 0, S)
         move_second_plane()
-        load_table(1, slice(T // 2, T))
         load_wv(1, 0, 1, at_raw10)
-        load_wg(1)
         load_wv(1, 1, 1, None)
+        load_wg(1)
         load_wp(0)
         nc.sync.dma_start(out=masses[:], in_=wgo)
         load_wp(1)
-        nc.vector.memset(store[2][:], 0.0)
-        cast_wv_scalar(0, 0)
+        cast_wv_scalar(0, 0, range(0, 2))
+        cast_wv_vector(0, 0, slice(2, 4))
         permute_wg(0)
-        permute_wg_planes()
         quantize_wv(0, 0)
+        permute_wg_planes()
+        nc.vector.memset(store[2][:], 0.0)
         cast_wv_scalar(0, 1, range(0, 2))
         cast_wv_vector(0, 1, slice(2, 4))
         bias_ps = vector_banks[3][:].rearrange("p t s -> p (t s)")
@@ -355,26 +354,26 @@ def tile_list_mesh_convective_terms_kernel(
         gather_codes(1, BANK, BANK)
         convective(0, 0)
         convective(1, 0)
-        permute_wg(1)
         quantize_h(0, 0)
         quantize_h(1, 0)
         cast_wv_scalar(1, 0)
         cast_wv_vector(1, 1)
+        permute_wg(1)
         quantize_wv(1, 0)
         quantize_wv(1, 1)
         convective(2, 0)
-        convective(0, 1, gradients_first=True)
+        convective(3, 0)
         quantize_h(2, 0)
+        convective(0, 1)
+        quantize_h(3, 0)
         prepare_wp([0], wp_first)
         quantize_h(0, 1)
         project(0, 0, CHUNK)
         convective(1, 1)
-        convective(3, 0)
         quantize_h(1, 1)
-        prepare_wp([1], wp_second)
-        quantize_h(3, 0)
         convective(2, 1)
         project(0, CHUNK, CHUNK)
+        prepare_wp([1], wp_second)
         quantize_h(2, 1)
         convective(3, 1)
         project(1, 0, CHUNK)

@@ -56,7 +56,7 @@ def tile_list_mesh_convective_terms_kernel(
         identity = held([P, P], F32, "identity")[:]
         bias_rows = held([P, R_PASSES * P], F32, "bias_rows")
         bias = placed([P, R_PASSES * PACK], F32, "bias", at_raw01)
-        store = [held([P, T2], F32, "store0"), held([P, T2], F32, "store1"), placed([P, T2], F32, "store2", at_bf00)]
+        store = [held([P, T2], F32, "store0"), held([P, T2], F32, "store1")]
         v_codes0 = held([P, S], U32, "v_codes0")
         v_codes1 = held([P, S], U32, "v_codes1")
         v_planes = held([P, S], U8, "v_planes")
@@ -118,8 +118,7 @@ def tile_list_mesh_convective_terms_kernel(
         def quantized(width, name):
             return held([P, width], U32, name + "_codes"), held([P, width], U8, name + "_scales")
 
-        wv_bf = {(b, a): held([P, PASS * PACK], BF16, "wv_bf%d%d" % (b, a)) for b, a in ((0, 1), (1, 1))}
-        wv_bf[0, 0] = placed([P, PASS * PACK], BF16, "wv_bf00", at_bf00)
+        wv_bf = {(b, a): held([P, PASS * PACK], BF16, "wv_bf%d%d" % (b, a)) for b, a in ((0, 0), (0, 1), (1, 1))}
         wv_bf[1, 0] = placed([P, PASS * PACK], BF16, "wv_bf10", at_bf10)
         wv_q = {(b, a): quantized(PASS, "wv%d%d" % (b, a)) for b in range(R_PASSES) for a in range(K_PASSES)}
         wp_q = quantized(N_TILES * R_PASSES * P, "wp")
@@ -127,6 +126,7 @@ def tile_list_mesh_convective_terms_kernel(
         vel_tiles = [held([P, PACK, CHUNK], F32, "vel%d" % i) for i in range(4)]
         h_tiles = [held([P, CHUNK * PACK], BF16, "h_bf%d" % i) for i in range(3)]
         vel_behind = {
+            (3, 1): placed([P, PACK, CHUNK], F32, "vel31", at_y),
             (2, 0): placed([P, PACK, CHUNK], F32, "vel20", at_raw10),
         }
         h_behind = {
@@ -136,6 +136,10 @@ def tile_list_mesh_convective_terms_kernel(
         wp_first = placed([P, CHUNK * PACK], BF16, "wp_bf0", at_wp_bf)
         wp_second = placed([P, CHUNK * PACK], BF16, "wp_bf1", at_wp_bf + KB)
         wp_last = held([P, 2 * CHUNK * PACK], BF16, "wp_bf23")
+        y_behind = {
+            (0, CHUNK): placed([P, CHUNK], F32, "y_cover0", at_y),
+            (1, 0): placed([P, CHUNK], F32, "y_cover1", at_y + KB),
+        }
         y_tiles = [held([P, S], F32, "y%d" % i) for i in range(3)]
 
         def cast_wv_scalar(b, a, codes=range(PACK)):
@@ -268,7 +272,7 @@ def tile_list_mesh_convective_terms_kernel(
             quantize(rounded[c, b][:], h_q[b][0][:, picks], h_q[b][1][:, picks])
 
         def project(m, first, count):
-            y = in_turn("y", y_tiles)
+            y = y_behind[m, first] if (m, first) in y_behind else in_turn("y", y_tiles)
             done = 0
             while done < count:
                 width = min(BANK - (first + done) % BANK, count - done)
@@ -288,10 +292,10 @@ def tile_list_mesh_convective_terms_kernel(
                 done = done + width
             places = scatter_list[:, first // 16 : (first + count) // 16]
             nc.vector.tensor_tensor(
-                out=store[m % 3][:].indirect(places), in0=y[:, 0:count], in1=masses[:, first : first + count], op=MULT
+                out=store[m % 2][:].indirect(places), in0=y[:, 0:count], in1=masses[:, first : first + count], op=MULT
             )
             if first + count == S:
-                nc.sync.dma_start(out=out[m * P : (m + 1) * P, :], in_=store[m % 3][:])
+                nc.sync.dma_start(out=out[m * P : (m + 1) * P, :], in_=store[m % 2][:])
 
         load_table(0)
         nc.sync.dma_start(gather_list[:], offs)
@@ -317,9 +321,9 @@ def tile_list_mesh_convective_terms_kernel(
             in_=bv.rearrange("(g t i) -> t g i", t=PACK, i=8),
         )
         make_identity(nc, identity)
-        for tile in store[0:2]:
-            nc.vector.memset(tile[:], 0.0)
+        nc.vector.memset(store[0][:], 0.0)
         gather_codes(0, 0, S)
+        nc.vector.memset(store[1][:], 0.0)
         gather(v_planes[:], table_planes[:], 0, S)
         move_second_plane()
         load_wv(1, 0, 1, at_raw10)
@@ -333,7 +337,6 @@ def tile_list_mesh_convective_terms_kernel(
         permute_wg(0)
         quantize_wv(0, 0)
         permute_wg_planes()
-        nc.vector.memset(store[2][:], 0.0)
         cast_wv_scalar(0, 1, range(0, 2))
         cast_wv_vector(0, 1, slice(2, 4))
         bias_ps = vector_banks[3][:].rearrange("p t s -> p (t s)")
@@ -372,15 +375,14 @@ def tile_list_mesh_convective_terms_kernel(
         convective(1, 1)
         quantize_h(1, 1)
         convective(2, 1)
-        project(0, CHUNK, CHUNK)
         prepare_wp([1], wp_second)
-        quantize_h(2, 1)
         convective(3, 1)
-        project(1, 0, CHUNK)
+        quantize_h(2, 1)
         quantize_h(3, 1)
-        project(1, CHUNK, CHUNK)
+        project(0, CHUNK, CHUNK)
+        project(1, 0, CHUNK)
         project(0, BANK, BANK)
-        project(1, BANK, BANK)
+        project(1, CHUNK, S - CHUNK)
         prepare_wp([2, 3], wp_last)
         for m in range(2, N_TILES):
             project(m, 0, S)

@@ -148,11 +148,11 @@ def tile_list_mesh_convective_terms_kernel(
             for t in codes:
                 nc.scalar.copy(out=dst[:, t], in_=src[:, t])
 
-        def cast_wv_vector(b, a, codes=slice(0, PACK)):
-            nc.vector.tensor_copy(
-                out=wv_bf[b, a][:].rearrange("p (t q i j) -> p t q j i", t=PACK, i=8, j=PACK)[:, codes],
-                in_=wv_raw[b, a][:].rearrange("p j (q t i) -> p t q j i", t=PACK, i=8)[:, codes],
-            )
+        def cast_wv_vector(b, a, codes=range(PACK)):
+            dst = wv_bf[b, a][:].rearrange("p (t q u i j) -> p t q u j i", t=PACK, u=2, i=4, j=PACK)
+            src = wv_raw[b, a][:].rearrange("p j (q t u i) -> p t q u j i", t=PACK, u=2, i=4)
+            for t in codes:
+                nc.vector.tensor_copy(out=dst[:, t], in_=src[:, t])
 
         def quantize_wv(b, a):
             quantize(wv_bf[b, a][:], wv_q[b, a][0][:], wv_q[b, a][1][:])
@@ -333,12 +333,12 @@ def tile_list_mesh_convective_terms_kernel(
         nc.sync.dma_start(out=masses[:], in_=wgo)
         load_wp(1)
         cast_wv_scalar(0, 0, range(0, 2))
-        cast_wv_vector(0, 0, slice(2, 4))
+        cast_wv_vector(0, 0, range(2, 4))
         permute_wg(0)
         quantize_wv(0, 0)
         permute_wg_planes()
         cast_wv_scalar(0, 1, range(0, 2))
-        cast_wv_vector(0, 1, slice(2, 4))
+        cast_wv_vector(0, 1, range(2, 4))
         bias_ps = vector_banks[3][:].rearrange("p t s -> p (t s)")
         for b in range(R_PASSES):
             nc.tensor.transpose(bias_ps[:, b * P : (b + 1) * P], bias_rows[:, b * P : (b + 1) * P], identity)

@@ -44,8 +44,7 @@ def tile_list_mesh_convective_terms_kernel(
         def placed(shape, dtype, name, offset):
             return shared.tile(shape, dtype, name=name, align_bytes=64, offset=offset)
 
-        KB = 1024
-        at_raw01, at_raw10, at_bf10, at_wp_bf, at_bf00, at_y = 0, 8 * KB, 16 * KB, 24 * KB, 32 * KB, 44 * KB
+        at_raw00 = 0
         gather_list = held([P, S // 16], U16, "gather_list")
         scatter_list = held([P, S // 16], U16, "scatter_list")
         table = [held([P, T], I32, "table%d" % a) for a in range(K_PASSES)]
@@ -55,15 +54,17 @@ def tile_list_mesh_convective_terms_kernel(
         masses = held([P, S], F32, "masses")
         identity = held([P, P], F32, "identity")[:]
         bias_rows = held([P, R_PASSES * P], F32, "bias_rows")
-        bias = placed([P, R_PASSES * PACK], F32, "bias", at_raw01)
+        bias = held([P, R_PASSES * PACK], F32, "bias")
         store = [held([P, T2], F32, "store0"), held([P, T2], F32, "store1")]
-        v_codes0 = held([P, S], U32, "v_codes0")
+        v_codes0 = [placed([P, BANK], U32, "v_codes0_low", at_raw00), held([P, BANK], U32, "v_codes0_high")]
         v_codes1 = held([P, S], U32, "v_codes1")
         v_planes = held([P, S], U8, "v_planes")
         v_plane1 = held([P, S], U8, "v_plane1")
 
         def codes_of(a, first, count):
-            return (v_codes0, v_codes1)[a][:, first : first + count]
+            if a == 0:
+                return v_codes0[first // BANK][:, first % BANK : first % BANK + count]
+            return v_codes1[:, first : first + count]
 
         scalar_banks = [psum.tile([P, BANK], F32, name="scalar_bank%d" % i) for i in range(4)]
         vector_banks = [psum.tile([P, PACK, SUB], F32, name="vector_bank%d" % i) for i in range(4)]
@@ -118,29 +119,19 @@ def tile_list_mesh_convective_terms_kernel(
         def quantized(width, name):
             return held([P, width], U32, name + "_codes"), held([P, width], U8, name + "_scales")
 
-        wv_bf = {(b, a): held([P, PASS * PACK], BF16, "wv_bf%d%d" % (b, a)) for b, a in ((0, 0), (0, 1), (1, 1))}
-        wv_bf[1, 0] = placed([P, PASS * PACK], BF16, "wv_bf10", at_bf10)
+        wv_bf = {(b, a): held([P, PASS * PACK], BF16, "wv_bf%d%d" % (b, a)) for b in range(R_PASSES) for a in range(K_PASSES)}
         wv_q = {(b, a): quantized(PASS, "wv%d%d" % (b, a)) for b in range(R_PASSES) for a in range(K_PASSES)}
         wp_q = quantized(N_TILES * R_PASSES * P, "wp")
         h_q = [quantized(S, "h%d" % b) for b in range(R_PASSES)]
         vel_tiles = [held([P, PACK, CHUNK], F32, "vel%d" % i) for i in range(4)]
-        h_tiles = [held([P, CHUNK * PACK], BF16, "h_bf%d" % i) for i in range(3)]
-        vel_behind = {
-            (3, 1): placed([P, PACK, CHUNK], F32, "vel31", at_y),
-            (2, 0): placed([P, PACK, CHUNK], F32, "vel20", at_raw10),
-        }
-        h_behind = {
-            (2, 0): placed([P, CHUNK * PACK], BF16, "h_bf20", at_bf10),
-            (3, 0): placed([P, CHUNK * PACK], BF16, "h_bf30", at_bf10 + 2 * KB),
-        }
-        wp_first = placed([P, CHUNK * PACK], BF16, "wp_bf0", at_wp_bf)
-        wp_second = placed([P, CHUNK * PACK], BF16, "wp_bf1", at_wp_bf + KB)
+        h_tiles = [held([P, CHUNK * PACK], BF16, "h_bf%d" % i) for i in range(4)]
+        vel_behind = {}
+        h_behind = {}
+        wp_first = held([P, CHUNK * PACK], BF16, "wp_bf0")
+        wp_second = held([P, CHUNK * PACK], BF16, "wp_bf1")
         wp_last = held([P, 2 * CHUNK * PACK], BF16, "wp_bf23")
-        y_behind = {
-            (0, CHUNK): placed([P, CHUNK], F32, "y_cover0", at_y),
-            (1, 0): placed([P, CHUNK], F32, "y_cover1", at_y + KB),
-        }
-        y_tiles = [held([P, S], F32, "y%d" % i) for i in range(3)]
+        y_behind = {}
+        y_tiles = [held([P, S], F32, "y%d" % i) for i in range(4)]
 
         def cast_wv_scalar(b, a, codes=range(PACK)):
             dst = wv_bf[b, a][:].rearrange("p (t q u i j) -> p t q u j i", t=PACK, u=2, i=4, j=PACK)
@@ -157,14 +148,16 @@ def tile_list_mesh_convective_terms_kernel(
         def quantize_wv(b, a):
             quantize(wv_bf[b, a][:], wv_q[b, a][0][:], wv_q[b, a][1][:])
 
-        def prepare_wp(tiles, grouped):
+        def round_wp(tiles, grouped, halves=range(R_PASSES)):
             for u, m in enumerate(tiles):
-                for b in range(R_PASSES):
+                for b in halves:
                     first = (u * R_PASSES + b) * PASS
                     nc.scalar.copy(
                         out=grouped[:, first : first + PASS].rearrange("p (c i t) -> p c t i", t=PACK, i=4),
                         in_=wp_raw[b, m // 2][:, :, (m % 2) * P : (m % 2 + 1) * P].rearrange("p t (c i) -> p c t i", i=4),
                     )
+
+        def quantize_wp(tiles, grouped):
             cols = slice(tiles[0] * R_PASSES * P, (tiles[-1] + 1) * R_PASSES * P)
             quantize(grouped[:], wp_q[0][:, cols], wp_q[1][:, cols])
 
@@ -187,8 +180,8 @@ def tile_list_mesh_convective_terms_kernel(
                 in_=words_of(wg_planes_raw).rearrange("p (g q t w) -> p g t q w", t=PACK, q=16, w=2),
             )
 
-        def velocity_pass(banks, c, b, a):
-            for t in range(PACK):
+        def velocity_pass(banks, c, b, a, codes=range(PACK)):
+            for t in codes:
                 cols = slice(t * P, (t + 1) * P)
                 nc.tensor.matmul_mx(
                     out=banks[t // 2][:, (t % 2) * CHUNK : (t % 2 + 1) * CHUNK],
@@ -200,7 +193,7 @@ def tile_list_mesh_convective_terms_kernel(
                     stop=(a == K_PASSES - 1 and t % 2 == 1),
                 )
 
-        def gradient_pass(bank, first, b, a):
+        def gradient_pass(bank, first, b, a, opens=0):
             for t in range(PACK):
                 col = a * PASS + t * P
                 nc.tensor.matmul_mx(
@@ -209,45 +202,42 @@ def tile_list_mesh_convective_terms_kernel(
                     lhsT_scale=wg_planes[:, a * H + b * PASS + t * P : a * H + b * PASS + (t + 1) * P],
                     rhs=codes_of(a, first, SUB).bitcast(FP8X4),
                     rhs_scale=(v_planes, v_plane1)[a][:, first : first + SUB],
-                    start=(a == 0 and t == 0),
-                    stop=(a == K_PASSES - 1 and t == PACK - 1),
+                    start=(a == opens and t == 0),
+                    stop=(a != opens and t == PACK - 1),
                 )
 
-        banks_of = {}
-        rounded = {}
+        grad_of = {}
+        vel_of = {}
+        vels = {}
+        ys = {}
 
-        def multiply(c, b, a):
+        def grad(c, b, a):
+            if a == 1:
+                grad_of[c, b] = [in_turn("vector", vector_banks) for s in range(CHUNK // SUB)]
+            for s, bank in enumerate(grad_of[c, b]):
+                gradient_pass(bank, c * CHUNK + s * SUB, b, a, 1)
+
+        def velo(c, b, a):
             if a == 0:
-                banks_of[c, b] = (
-                    [in_turn("scalar", scalar_banks) for pair in range(PACK // 2)],
-                    [in_turn("vector", vector_banks) for s in range(CHUNK // SUB)],
-                )
-            velocity_pass(banks_of[c, b][0], c, b, a)
-            for s, bank in enumerate(banks_of[c, b][1]):
-                gradient_pass(bank, c * CHUNK + s * SUB, b, a)
+                vel_of[c, b] = [in_turn("scalar", scalar_banks) for pair in range(PACK // 2)]
+            velocity_pass(vel_of[c, b], c, b, a)
 
-        def gradients(c, b):
-            banks = [in_turn("vector", vector_banks) for s in range(CHUNK // SUB)]
-            for s, bank in enumerate(banks):
+        def velos(c, b):
+            vel_of[c, b] = [in_turn("scalar", scalar_banks) for pair in range(PACK // 2)]
+            for pair in range(PACK // 2):
+                for a in range(K_PASSES):
+                    velocity_pass(vel_of[c, b], c, b, a, range(2 * pair, 2 * pair + 2))
+
+        def grads(c, b):
+            grad_of[c, b] = [in_turn("vector", vector_banks) for s in range(CHUNK // SUB)]
+            for s, bank in enumerate(grad_of[c, b]):
                 for a in range(K_PASSES):
                     gradient_pass(bank, c * CHUNK + s * SUB, b, a)
-            return banks
 
-        def velocities(c, b):
-            banks = [in_turn("scalar", scalar_banks) for pair in range(PACK // 2)]
-            for a in range(K_PASSES):
-                velocity_pass(banks, c, b, a)
-            return banks
+        rounded = {}
 
-        def convective(c, b, gradients_first=False):
-            if (c, b) not in banks_of:
-                if gradients_first:
-                    grad_banks = gradients(c, b)
-                    banks_of[c, b] = (velocities(c, b), grad_banks)
-                else:
-                    vel_banks = velocities(c, b)
-                    banks_of[c, b] = (vel_banks, gradients(c, b))
-            vel_banks, grad_banks = banks_of[c, b]
+        def empty(c, b):
+            vel_banks = vel_of[c, b]
             vel = vel_behind[c, b] if (c, b) in vel_behind else in_turn("vel", vel_tiles)
             for t in range(PACK):
                 nc.scalar.activation(
@@ -257,7 +247,42 @@ def tile_list_mesh_convective_terms_kernel(
                     bias=bias[:, PACK * b + t : PACK * b + t + 1],
                     scale=1.0,
                 )
+            vels[c, b] = vel
+
+        early = held([P, PACK, BANK], F32, "early_grad")
+        early_banks = []
+
+        def early_gradients(a):
+            for t in range(PACK):
+                if a == 0:
+                    early_banks.append(in_turn("scalar", scalar_banks))
+                col = a * PASS + t * P
+                nc.tensor.matmul_mx(
+                    out=early_banks[t][:],
+                    lhsT=wg_codes[0][:, 2 * col : 2 * (col + P)].bitcast(FP4X4),
+                    lhsT_scale=wg_planes[:, a * H + t * P : a * H + (t + 1) * P],
+                    rhs=codes_of(a, BANK, BANK).bitcast(FP8X4),
+                    rhs_scale=(v_planes, v_plane1)[a][:, BANK:S],
+                    start=(a == 0),
+                    stop=(a == K_PASSES - 1),
+                )
+                if a == K_PASSES - 1:
+                    nc.scalar.copy(out=early[:, t, :], in_=early_banks[t][:])
+
+        def product(c, b):
+            vel = vels[c, b]
             h = h_behind[c, b] if (c, b) in h_behind else in_turn("h", h_tiles)
+            rounded[c, b] = h
+            if (c, b) not in grad_of:
+                first = c * CHUNK - BANK
+                nc.vector.tensor_tensor(
+                    out=h[:].rearrange("p (e i t) -> p e t i", t=PACK, i=4),
+                    in0=early[:, :, first : first + CHUNK].rearrange("p t (e i) -> p e t i", i=4),
+                    in1=vel[:].rearrange("p t (e i) -> p e t i", i=4),
+                    op=MULT,
+                )
+                return
+            grad_banks = grad_of[c, b]
             for s, bank in enumerate(grad_banks):
                 nc.vector.tensor_tensor(
                     out=h[:, s * SUB * PACK : (s + 1) * SUB * PACK].rearrange("p (e i t) -> p e t i", t=PACK, i=4),
@@ -271,7 +296,7 @@ def tile_list_mesh_convective_terms_kernel(
             picks = slice(c * CHUNK, (c + 1) * CHUNK)
             quantize(rounded[c, b][:], h_q[b][0][:, picks], h_q[b][1][:, picks])
 
-        def project(m, first, count):
+        def project(m, first, count, later=False):
             y = y_behind[m, first] if (m, first) in y_behind else in_turn("y", y_tiles)
             done = 0
             while done < count:
@@ -290,9 +315,16 @@ def tile_list_mesh_convective_terms_kernel(
                     )
                 nc.scalar.copy(out=y[:, done : done + width], in_=bank[:, 0:width])
                 done = done + width
+            ys[m, first] = y
+            if not later:
+                scatter(m, first, count)
+
+        def scatter(m, first, count, made=None):
+            made = first if made is None else made
+            y = ys[m, made][:, first - made : first - made + count]
             places = scatter_list[:, first // 16 : (first + count) // 16]
             nc.vector.tensor_tensor(
-                out=store[m % 2][:].indirect(places), in0=y[:, 0:count], in1=masses[:, first : first + count], op=MULT
+                out=store[m % 2][:].indirect(places), in0=y, in1=masses[:, first : first + count], op=MULT
             )
             if first + count == S:
                 nc.sync.dma_start(out=out[m * P : (m + 1) * P, :], in_=store[m % 2][:])
@@ -303,8 +335,6 @@ def tile_list_mesh_convective_terms_kernel(
         for r in range(4):
             nc.sync.dma_start(out=table_planes[r:P:32, :].bitcast(I32), in_=tab_scales[0, r:16:4, :].bitcast(I32))
         nc.sync.dma_start(out=table_planes[8:24, :].bitcast(I32), in_=tab_scales[1].bitcast(I32))
-        load_wv(0, 0, 1, None)
-        nc.sync.dma_start(scatter_list[:], offs2)
         load_wg(0)
         nc.vector.memset(words_of(wg_planes_raw), 0)
         for r in range(4):
@@ -312,8 +342,8 @@ def tile_list_mesh_convective_terms_kernel(
                 out=wg_planes_raw[r:P:32, :, :].bitcast(I32),
                 in_=wg_scales[:, r:16:4, :].rearrange("a q n -> q a n").bitcast(I32),
             )
-        load_wv(0, 1, 1, at_raw01)
         load_table(1)
+        load_wv(0, 0, 1, at_raw00)
         nc.vector.memset(v_plane1[:].bitcast(I32), 0)
         nc.gpsimd.memset(bias_rows[:], 0.0)
         nc.gpsimd.dma_start(
@@ -322,23 +352,18 @@ def tile_list_mesh_convective_terms_kernel(
         )
         make_identity(nc, identity)
         nc.vector.memset(store[0][:], 0.0)
-        gather_codes(0, 0, S)
         nc.vector.memset(store[1][:], 0.0)
+        gather_codes(0, BANK, BANK)
         gather(v_planes[:], table_planes[:], 0, S)
         move_second_plane()
-        load_wv(1, 0, 1, at_raw10)
-        load_wv(1, 1, 1, None)
+        load_wv(0, 1, 1, None)
+        load_wv(1, 0, 1, None)
         load_wg(1)
+        load_wv(1, 1, 1, None)
         load_wp(0)
+        nc.sync.dma_start(scatter_list[:], offs2)
         nc.sync.dma_start(out=masses[:], in_=wgo)
         load_wp(1)
-        cast_wv_scalar(0, 0, range(0, 2))
-        cast_wv_vector(0, 0, range(2, 4))
-        permute_wg(0)
-        quantize_wv(0, 0)
-        permute_wg_planes()
-        cast_wv_scalar(0, 1, range(0, 2))
-        cast_wv_vector(0, 1, range(2, 4))
         bias_ps = vector_banks[3][:].rearrange("p t s -> p (t s)")
         for b in range(R_PASSES):
             nc.tensor.transpose(bias_ps[:, b * P : (b + 1) * P], bias_rows[:, b * P : (b + 1) * P], identity)
@@ -347,42 +372,86 @@ def tile_list_mesh_convective_terms_kernel(
             in_=bias_ps[:, 0 : R_PASSES * P].rearrange("p (b c) -> p b c", c=P)[:, :, 0:PACK],
             func=IDENTITY,
         )
-        quantize_wv(0, 1)
-        for c in range(2):
-            multiply(c, 0, 0)
-        gather_codes(1, 0, CHUNK)
-        multiply(0, 0, 1)
-        gather_codes(1, CHUNK, CHUNK)
-        multiply(1, 0, 1)
+        permute_wg(0)
+        permute_wg_planes()
+        early_gradients(0)
         gather_codes(1, BANK, BANK)
-        convective(0, 0)
-        convective(1, 0)
-        quantize_h(0, 0)
-        quantize_h(1, 0)
-        cast_wv_scalar(1, 0)
-        cast_wv_vector(1, 1)
+        cast_wv_scalar(0, 0, range(0, 1))
+        early_gradients(1)
+        gather_codes(1, 0, BANK)
+        grad(0, 0, 1)
+        grad(1, 0, 1)
+        cast_wv_vector(0, 0, range(1, 4))
+        gather_codes(0, 0, BANK)
+        grad(0, 0, 0)
+        grad(1, 0, 0)
+        quantize_wv(0, 0)
+        cast_wv_scalar(0, 1, range(0, 1))
+        cast_wv_vector(0, 1, range(1, 4))
+        velo(0, 0, 0)
+        velo(1, 0, 0)
+        quantize_wv(0, 1)
+        velo(0, 0, 1)
+        velo(1, 0, 1)
+        cast_wv_scalar(1, 0, range(0, 1))
+        empty(0, 0)
+        empty(1, 0)
+        cast_wv_vector(1, 0, range(1, 4))
         permute_wg(1)
         quantize_wv(1, 0)
+        velos(2, 0)
+        product(0, 0)
+        grads(0, 1)
+        product(1, 0)
+        cast_wv_scalar(1, 1, range(0, 2))
+        cast_wv_vector(1, 1, range(2, 4))
+        empty(2, 0)
+        velos(3, 0)
+        quantize_h(0, 0)
         quantize_wv(1, 1)
-        convective(2, 0)
-        convective(3, 0)
+        velos(0, 1)
+        grads(1, 1)
+        round_wp([0], wp_first, [0])
+        empty(3, 0)
+        product(2, 0)
+        quantize_h(1, 0)
         quantize_h(2, 0)
-        convective(0, 1)
-        quantize_h(3, 0)
-        prepare_wp([0], wp_first)
+        empty(0, 1)
+        velos(1, 1)
+        round_wp([0], wp_first, [1])
+        product(3, 0)
+        product(0, 1)
+        empty(1, 1)
+        quantize_wp([0], wp_first)
         quantize_h(0, 1)
-        project(0, 0, CHUNK)
-        convective(1, 1)
+        velos(2, 1)
+        project(0, 0, CHUNK, True)
+        grads(2, 1)
+        quantize_h(3, 0)
+        product(1, 1)
+        empty(2, 1)
+        round_wp([1], wp_second)
+        scatter(0, 0, CHUNK)
         quantize_h(1, 1)
-        convective(2, 1)
-        prepare_wp([1], wp_second)
-        convective(3, 1)
+        velos(3, 1)
+        project(0, CHUNK, CHUNK, True)
+        grads(3, 1)
+        product(2, 1)
+        quantize_wp([1], wp_second)
+        empty(3, 1)
         quantize_h(2, 1)
+        project(0, BANK, CHUNK, True)
+        project(1, 0, CHUNK, True)
+        scatter(0, CHUNK, CHUNK)
+        product(3, 1)
+        round_wp([2, 3], wp_last)
+        scatter(0, BANK, CHUNK)
         quantize_h(3, 1)
-        project(0, CHUNK, CHUNK)
-        project(1, 0, CHUNK)
-        project(0, BANK, BANK)
-        project(1, CHUNK, S - CHUNK)
-        prepare_wp([2, 3], wp_last)
+        project(0, BANK + CHUNK, CHUNK, True)
+        scatter(1, 0, CHUNK)
+        project(1, CHUNK, S - CHUNK, True)
+        scatter(0, BANK + CHUNK, CHUNK)
+        quantize_wp([2, 3], wp_last)
+        scatter(1, CHUNK, S - CHUNK)
         for m in range(2, N_TILES):
             project(m, 0, S)

@@ -27,6 +27,7 @@ CHUNKS = S // CHUNK
 SUB = 128
 N_TILES = N // P
 BANK = 512
+SCALE_ROW = 96
 
 
 def tile_list_mesh_convective_terms_kernel(
@@ -44,7 +45,7 @@ def tile_list_mesh_convective_terms_kernel(
         def placed(shape, dtype, name, offset):
             return shared.tile(shape, dtype, name=name, align_bytes=64, offset=offset)
 
-        at_raw00 = 0
+        at_raw00, at_vel20, at_wp0 = 0, 8192, 12288
         gather_list = held([P, S // 16], U16, "gather_list")
         scatter_list = held([P, S // 16], U16, "scatter_list")
         table = [held([P, T], I32, "table%d" % a) for a in range(K_PASSES)]
@@ -56,10 +57,10 @@ def tile_list_mesh_convective_terms_kernel(
         bias_rows = held([P, R_PASSES * P], F32, "bias_rows")
         bias = held([P, R_PASSES * PACK], F32, "bias")
         store = [held([P, T2], F32, "store0"), held([P, T2], F32, "store1")]
-        v_codes0 = [placed([P, BANK], U32, "v_codes0_low", at_raw00), held([P, BANK], U32, "v_codes0_high")]
+        v_codes0 = [held([P, BANK], U32, "v_codes0_low"), held([P, BANK], U32, "v_codes0_high")]
         v_codes1 = held([P, S], U32, "v_codes1")
         v_planes = held([P, S], U8, "v_planes")
-        v_plane1 = held([P, S], U8, "v_plane1")
+        v_plane = [held([P, S], U8, "v_plane%d" % a) for a in range(K_PASSES)]
 
         def codes_of(a, first, count):
             if a == 0:
@@ -67,7 +68,7 @@ def tile_list_mesh_convective_terms_kernel(
             return v_codes1[:, first : first + count]
 
         scalar_banks = [psum.tile([P, BANK], F32, name="scalar_bank%d" % i) for i in range(4)]
-        vector_banks = [psum.tile([P, PACK, SUB], F32, name="vector_bank%d" % i) for i in range(4)]
+        vector_banks = [psum.tile([P, BANK], F32, name="vector_bank%d" % i) for i in range(4)]
         turns = {"scalar": 0, "vector": 0, "vel": 0, "h": 0, "y": 0}
 
         def in_turn(kind, tiles):
@@ -109,9 +110,12 @@ def tile_list_mesh_convective_terms_kernel(
         def gather_codes(a, first, count):
             gather(codes_of(a, first, count), table[a][:].bitcast(U32), first, count)
 
-        def move_second_plane():
+        def move_plane(a):
             for r in range(4):
-                nc.sync.dma_start(out=v_plane1[r:P:32, :].bitcast(I32), in_=v_planes[8 + r : 24 : 4, :].bitcast(I32))
+                first = SCALE_ROW + 16 * a + r
+                nc.sync.dma_start(
+                    out=v_plane[a][r:P:32, :].bitcast(I32), in_=v_planes[first : first + 13 : 4, :].bitcast(I32)
+                )
 
         def quantize(grouped, codes, scales):
             nc.vector.quantize_mx(out=codes.bitcast(FP8X4), scales=scales, in_=grouped)
@@ -122,12 +126,23 @@ def tile_list_mesh_convective_terms_kernel(
         wv_bf = {(b, a): held([P, PASS * PACK], BF16, "wv_bf%d%d" % (b, a)) for b in range(R_PASSES) for a in range(K_PASSES)}
         wv_q = {(b, a): quantized(PASS, "wv%d%d" % (b, a)) for b in range(R_PASSES) for a in range(K_PASSES)}
         wp_q = quantized(N_TILES * R_PASSES * P, "wp")
-        h_q = [quantized(S, "h%d" % b) for b in range(R_PASSES)]
+        h_codes = {
+            (0, 0): placed([P, BANK], U32, "h_codes00", at_vel20),
+            (0, 1): placed([P, BANK], U32, "h_codes01", at_wp0),
+            (1, 0): held([P, BANK], U32, "h_codes10"),
+            (1, 1): held([P, BANK], U32, "h_codes11"),
+        }
+        h_scales = [held([P, S], U8, "h_scales%d" % b) for b in range(R_PASSES)]
+        h_pairs = [held([P, BANK * PACK], BF16, "h_pair%d" % i) for i in range(2)]
+
+        def h_words(b, first, count):
+            return h_codes[b, first // BANK][:, first % BANK : first % BANK + count]
+
         vel_tiles = [held([P, PACK, CHUNK], F32, "vel%d" % i) for i in range(4)]
-        h_tiles = [held([P, CHUNK * PACK], BF16, "h_bf%d" % i) for i in range(4)]
-        vel_behind = {}
-        h_behind = {}
-        wp_first = held([P, CHUNK * PACK], BF16, "wp_bf0")
+        h_tiles = [held([P, CHUNK * PACK], BF16, "h_bf%d" % i) for i in range(3)]
+        vel_behind = {(2, 0): placed([P, PACK, CHUNK], F32, "vel20", at_vel20)}
+        h_behind = {(c, 0): h_pairs[c // 2][:, (c % 2) * CHUNK * PACK : (c % 2 + 1) * CHUNK * PACK] for c in range(CHUNKS)}
+        wp_first = placed([P, CHUNK * PACK], BF16, "wp_bf0", at_wp0)
         wp_second = held([P, CHUNK * PACK], BF16, "wp_bf1")
         wp_last = held([P, 2 * CHUNK * PACK], BF16, "wp_bf23")
         y_behind = {}
@@ -139,11 +154,11 @@ def tile_list_mesh_convective_terms_kernel(
             for t in codes:
                 nc.scalar.copy(out=dst[:, t], in_=src[:, t])
 
-        def cast_wv_vector(b, a, codes=range(PACK)):
-            dst = wv_bf[b, a][:].rearrange("p (t q u i j) -> p t q u j i", t=PACK, u=2, i=4, j=PACK)
-            src = wv_raw[b, a][:].rearrange("p j (q t u i) -> p t q u j i", t=PACK, u=2, i=4)
-            for t in codes:
-                nc.vector.tensor_copy(out=dst[:, t], in_=src[:, t])
+        def cast_wv_vector(b, a, codes):
+            nc.vector.tensor_copy(
+                out=wv_bf[b, a][:].rearrange("p (t q i j) -> p q t j i", t=PACK, i=8, j=PACK)[:, :, codes],
+                in_=wv_raw[b, a][:].rearrange("p j (q t i) -> p q t j i", t=PACK, i=8)[:, :, codes],
+            )
 
         def quantize_wv(b, a):
             quantize(wv_bf[b, a][:], wv_q[b, a][0][:], wv_q[b, a][1][:])
@@ -188,7 +203,7 @@ def tile_list_mesh_convective_terms_kernel(
                     lhsT=wv_q[b, a][0][:, cols].bitcast(FP8X4),
                     lhsT_scale=wv_q[b, a][1][:, cols],
                     rhs=codes_of(a, c * CHUNK, CHUNK).bitcast(FP8X4),
-                    rhs_scale=(v_planes, v_plane1)[a][:, c * CHUNK : (c + 1) * CHUNK],
+                    rhs_scale=v_plane[a][:, c * CHUNK : (c + 1) * CHUNK],
                     start=(a == 0 and t % 2 == 0),
                     stop=(a == K_PASSES - 1 and t % 2 == 1),
                 )
@@ -197,11 +212,11 @@ def tile_list_mesh_convective_terms_kernel(
             for t in range(PACK):
                 col = a * PASS + t * P
                 nc.tensor.matmul_mx(
-                    out=bank[:, t, :],
+                    out=bank[:, t * SUB : (t + 1) * SUB],
                     lhsT=wg_codes[b][:, 2 * col : 2 * (col + P)].bitcast(FP4X4),
                     lhsT_scale=wg_planes[:, a * H + b * PASS + t * P : a * H + b * PASS + (t + 1) * P],
                     rhs=codes_of(a, first, SUB).bitcast(FP8X4),
-                    rhs_scale=(v_planes, v_plane1)[a][:, first : first + SUB],
+                    rhs_scale=v_plane[a][:, first : first + SUB],
                     start=(a == opens and t == 0),
                     stop=(a != opens and t == PACK - 1),
                 )
@@ -262,7 +277,7 @@ def tile_list_mesh_convective_terms_kernel(
                     lhsT=wg_codes[0][:, 2 * col : 2 * (col + P)].bitcast(FP4X4),
                     lhsT_scale=wg_planes[:, a * H + t * P : a * H + (t + 1) * P],
                     rhs=codes_of(a, BANK, BANK).bitcast(FP8X4),
-                    rhs_scale=(v_planes, v_plane1)[a][:, BANK:S],
+                    rhs_scale=v_plane[a][:, BANK:S],
                     start=(a == 0),
                     stop=(a == K_PASSES - 1),
                 )
@@ -271,12 +286,12 @@ def tile_list_mesh_convective_terms_kernel(
 
         def product(c, b):
             vel = vels[c, b]
-            h = h_behind[c, b] if (c, b) in h_behind else in_turn("h", h_tiles)
+            h = h_behind[c, b] if (c, b) in h_behind else in_turn("h", h_tiles)[:]
             rounded[c, b] = h
             if (c, b) not in grad_of:
                 first = c * CHUNK - BANK
                 nc.vector.tensor_tensor(
-                    out=h[:].rearrange("p (e i t) -> p e t i", t=PACK, i=4),
+                    out=h.rearrange("p (e i t) -> p e t i", t=PACK, i=4),
                     in0=early[:, :, first : first + CHUNK].rearrange("p t (e i) -> p e t i", i=4),
                     in1=vel[:].rearrange("p t (e i) -> p e t i", i=4),
                     op=MULT,
@@ -286,7 +301,7 @@ def tile_list_mesh_convective_terms_kernel(
             for s, bank in enumerate(grad_banks):
                 nc.vector.tensor_tensor(
                     out=h[:, s * SUB * PACK : (s + 1) * SUB * PACK].rearrange("p (e i t) -> p e t i", t=PACK, i=4),
-                    in0=bank[:].rearrange("p t (e i) -> p e t i", i=4),
+                    in0=bank[:].rearrange("p (t e i) -> p e t i", t=PACK, i=4),
                     in1=vel[:, :, s * SUB : (s + 1) * SUB].rearrange("p t (e i) -> p e t i", i=4),
                     op=MULT,
                 )
@@ -294,7 +309,10 @@ def tile_list_mesh_convective_terms_kernel(
 
         def quantize_h(c, b):
             picks = slice(c * CHUNK, (c + 1) * CHUNK)
-            quantize(rounded[c, b][:], h_q[b][0][:, picks], h_q[b][1][:, picks])
+            quantize(rounded[c, b], h_words(b, c * CHUNK, CHUNK), h_scales[b][:, picks])
+
+        def quantize_pair(half):
+            quantize(h_pairs[half][:], h_words(0, half * BANK, BANK), h_scales[0][:, half * BANK : (half + 1) * BANK])
 
         def project(m, first, count, later=False):
             y = y_behind[m, first] if (m, first) in y_behind else in_turn("y", y_tiles)
@@ -308,8 +326,8 @@ def tile_list_mesh_convective_terms_kernel(
                         out=bank[:, 0:width],
                         lhsT=wp_q[0][:, (m * R_PASSES + b) * P : (m * R_PASSES + b + 1) * P].bitcast(FP8X4),
                         lhsT_scale=wp_q[1][:, (m * R_PASSES + b) * P : (m * R_PASSES + b + 1) * P],
-                        rhs=h_q[b][0][:, picks].bitcast(FP8X4),
-                        rhs_scale=h_q[b][1][:, picks],
+                        rhs=h_words(b, first + done, width).bitcast(FP8X4),
+                        rhs_scale=h_scales[b][:, picks],
                         start=(b == R_PASSES - 1),
                         stop=(b == 0),
                     )
@@ -329,12 +347,12 @@ def tile_list_mesh_convective_terms_kernel(
             if first + count == S:
                 nc.sync.dma_start(out=out[m * P : (m + 1) * P, :], in_=store[m % 2][:])
 
-        load_table(0)
         nc.sync.dma_start(gather_list[:], offs)
-        nc.vector.memset(table_planes[:].bitcast(I32), 0)
-        for r in range(4):
-            nc.sync.dma_start(out=table_planes[r:P:32, :].bitcast(I32), in_=tab_scales[0, r:16:4, :].bitcast(I32))
-        nc.sync.dma_start(out=table_planes[8:24, :].bitcast(I32), in_=tab_scales[1].bitcast(I32))
+        nc.sync.dma_start(
+            out=table_planes[SCALE_ROW:P, :].bitcast(I32), in_=tab_scales.rearrange("a q n -> (a q) n").bitcast(I32)
+        )
+        load_table(0)
+        nc.vector.memset(table_planes[0:SCALE_ROW, :].bitcast(I32), 0)
         load_wg(0)
         nc.vector.memset(words_of(wg_planes_raw), 0)
         for r in range(4):
@@ -343,19 +361,23 @@ def tile_list_mesh_convective_terms_kernel(
                 in_=wg_scales[:, r:16:4, :].rearrange("a q n -> q a n").bitcast(I32),
             )
         load_table(1)
-        load_wv(0, 0, 1, at_raw00)
-        nc.vector.memset(v_plane1[:].bitcast(I32), 0)
+        for a in range(K_PASSES):
+            nc.vector.memset(v_plane[a][:].bitcast(I32), 0)
         nc.gpsimd.memset(bias_rows[:], 0.0)
         nc.gpsimd.dma_start(
             out=bias_rows[0:PACK, :].rearrange("t (g i) -> t g i", i=8),
             in_=bv.rearrange("(g t i) -> t g i", t=PACK, i=8),
         )
         make_identity(nc, identity)
-        nc.vector.memset(store[0][:], 0.0)
-        nc.vector.memset(store[1][:], 0.0)
-        gather_codes(0, BANK, BANK)
+        for tile in store:
+            for first in range(0, T2, T2 // 2):
+                nc.gpsimd.memset(tile[:, first : first + T2 // 2], 0.0)
         gather(v_planes[:], table_planes[:], 0, S)
-        move_second_plane()
+        gather_codes(0, BANK, BANK)
+        gather_codes(0, 0, BANK)
+        move_plane(0)
+        load_wv(0, 0, 1, None)
+        move_plane(1)
         load_wv(0, 1, 1, None)
         load_wv(1, 0, 1, None)
         load_wg(1)
@@ -364,7 +386,7 @@ def tile_list_mesh_convective_terms_kernel(
         nc.sync.dma_start(scatter_list[:], offs2)
         nc.sync.dma_start(out=masses[:], in_=wgo)
         load_wp(1)
-        bias_ps = vector_banks[3][:].rearrange("p t s -> p (t s)")
+        bias_ps = vector_banks[3][:]
         for b in range(R_PASSES):
             nc.tensor.transpose(bias_ps[:, b * P : (b + 1) * P], bias_rows[:, b * P : (b + 1) * P], identity)
         nc.scalar.activation(
@@ -381,13 +403,12 @@ def tile_list_mesh_convective_terms_kernel(
         gather_codes(1, 0, BANK)
         grad(0, 0, 1)
         grad(1, 0, 1)
-        cast_wv_vector(0, 0, range(1, 4))
-        gather_codes(0, 0, BANK)
+        cast_wv_vector(0, 0, slice(1, 4))
         grad(0, 0, 0)
         grad(1, 0, 0)
         quantize_wv(0, 0)
         cast_wv_scalar(0, 1, range(0, 1))
-        cast_wv_vector(0, 1, range(1, 4))
+        cast_wv_vector(0, 1, slice(1, 4))
         velo(0, 0, 0)
         velo(1, 0, 0)
         quantize_wv(0, 1)
@@ -396,7 +417,7 @@ def tile_list_mesh_convective_terms_kernel(
         cast_wv_scalar(1, 0, range(0, 1))
         empty(0, 0)
         empty(1, 0)
-        cast_wv_vector(1, 0, range(1, 4))
+        cast_wv_vector(1, 0, slice(1, 4))
         permute_wg(1)
         quantize_wv(1, 0)
         velos(2, 0)
@@ -404,30 +425,30 @@ def tile_list_mesh_convective_terms_kernel(
         grads(0, 1)
         product(1, 0)
         cast_wv_scalar(1, 1, range(0, 2))
-        cast_wv_vector(1, 1, range(2, 4))
+        cast_wv_vector(1, 1, slice(2, 4))
         empty(2, 0)
         velos(3, 0)
-        quantize_h(0, 0)
         quantize_wv(1, 1)
         velos(0, 1)
-        grads(1, 1)
-        round_wp([0], wp_first, [0])
         empty(3, 0)
+        round_wp([0], wp_first, [0])
         product(2, 0)
-        quantize_h(1, 0)
-        quantize_h(2, 0)
         empty(0, 1)
+        scalar_banks[2:4], vector_banks[2:4] = vector_banks[2:4], scalar_banks[2:4]
         velos(1, 1)
+        grads(1, 1)
         round_wp([0], wp_first, [1])
         product(3, 0)
+        quantize_pair(0)
         product(0, 1)
         empty(1, 1)
         quantize_wp([0], wp_first)
         quantize_h(0, 1)
         velos(2, 1)
+        scalar_banks[2:4], vector_banks[0:2] = vector_banks[0:2], scalar_banks[2:4]
         project(0, 0, CHUNK, True)
         grads(2, 1)
-        quantize_h(3, 0)
+        quantize_pair(1)
         product(1, 1)
         empty(2, 1)
         round_wp([1], wp_second)

@@ -54,7 +54,8 @@ def tile_list_mesh_convective_terms_kernel(
         wg_planes_raw = held([P, K_PASSES, H], U8, "wg_planes_raw")
         masses = held([P, S], F32, "masses")
         identity = held([P, P], F32, "identity")[:]
-        bias_rows = held([P, R_PASSES * P], F32, "bias_rows")
+        bias_raw = held([P, PASS], F32, "bias_raw")
+        bias_rows = held([P, PASS], F32, "bias_rows")
         bias = held([P, R_PASSES * PACK], F32, "bias")
         store = [held([P, T2], F32, "store0"), held([P, T2], F32, "store1")]
         v_codes0 = [held([P, BANK], U32, "v_codes0_low"), held([P, BANK], U32, "v_codes0_high")]
@@ -363,10 +364,11 @@ def tile_list_mesh_convective_terms_kernel(
         load_table(1)
         for a in range(K_PASSES):
             nc.vector.memset(v_plane[a][:].bitcast(I32), 0)
+        nc.scalar.dma_start(out=bias_raw[0:R_PASSES, :], in_=bv.rearrange("(b c) -> b c", b=R_PASSES))
         nc.gpsimd.memset(bias_rows[:], 0.0)
-        nc.gpsimd.dma_start(
-            out=bias_rows[0:PACK, :].rearrange("t (g i) -> t g i", i=8),
-            in_=bv.rearrange("(g t i) -> t g i", t=PACK, i=8),
+        nc.scalar.copy(
+            out=bias_rows[0:R_PASSES, :].rearrange("b (t q i) -> b t q i", t=PACK, i=8),
+            in_=bias_raw[0:R_PASSES, :].rearrange("b (q t i) -> b t q i", t=PACK, i=8),
         )
         make_identity(nc, identity)
         for tile in store:
@@ -387,11 +389,11 @@ def tile_list_mesh_convective_terms_kernel(
         nc.sync.dma_start(out=masses[:], in_=wgo)
         load_wp(1)
         bias_ps = vector_banks[3][:]
-        for b in range(R_PASSES):
-            nc.tensor.transpose(bias_ps[:, b * P : (b + 1) * P], bias_rows[:, b * P : (b + 1) * P], identity)
+        for t in range(PACK):
+            nc.tensor.transpose(bias_ps[:, t * P : (t + 1) * P], bias_rows[:, t * P : (t + 1) * P], identity)
         nc.scalar.activation(
-            out=bias[:].rearrange("p (b t) -> p b t", t=PACK),
-            in_=bias_ps[:, 0 : R_PASSES * P].rearrange("p (b c) -> p b c", c=P)[:, :, 0:PACK],
+            out=bias[:].rearrange("p (b t) -> p t b", t=PACK),
+            in_=bias_ps[:].rearrange("p (t c) -> p t c", c=P)[:, :, 0:R_PASSES],
             func=IDENTITY,
         )
         permute_wg(0)

@@ -430,7 +430,9 @@ def tile_list_mesh_convective_terms_kernel(
         cast_wv_vector(1, 1, slice(2, 4))
         empty(2, 0)
         velos(3, 0)
-        quantize_wv(1, 1)
+        for u in range(2):
+            cols = slice(u * 2 * P, (u + 1) * 2 * P)
+            quantize(wv_bf[1, 1][:, u * 2 * PASS : (u + 1) * 2 * PASS], wv_q[1, 1][0][:, cols], wv_q[1, 1][1][:, cols])
         velos(0, 1)
         empty(3, 0)
         round_wp([0], wp_first, [0])

from contextlib import ExitStack

import concourse.mybir as mybir
from concourse.masks import make_identity

K, H, N, T, S, T2 = 1024, 1024, 512, 2048, 1024, 2048
FLOPS = 2 * S * (2 * K * H + H * N)

F32 = mybir.dt.float32
BF16 = mybir.dt.bfloat16
I32 = mybir.dt.int32
U32 = mybir.dt.uint32
U16 = mybir.dt.uint16
U8 = mybir.dt.uint8
FP8X4 = mybir.dt.float8_e4m3fn_x4
FP4X4 = mybir.dt.float4_e2m1fn_x4
MULT = mybir.AluOpType.mult
IDENTITY = mybir.ActivationFunctionType.Identity

P = 128
PACK = 4
PASS = P * PACK
K_PASSES = K // PASS
R_PASSES = H // PASS
CHUNK = 256
CHUNKS = S // CHUNK
SUB = 128
N_TILES = N // P
BANK = 512
SCALE_ROW = 96


def tile_list_mesh_convective_terms_kernel(
    tc, tab_words, tab_scales, offs, wv, bv, wg_words, wg_scales, wp, wgo, offs2, out
):
    nc = tc.nc
    with ExitStack() as ctx:
        keep = ctx.enter_context(tc.tile_pool(name="keep", bufs=1))
        shared = ctx.enter_context(tc.tile_pool(name="shared", bufs=1))
        psum = ctx.enter_context(tc.psum_pool(name="psum", bufs=1))

        def held(shape, dtype, name):
            return keep.tile(shape, dtype, name=name, align_bytes=64)

        def placed(shape, dtype, name, offset):
            return shared.tile(shape, dtype, name=name, align_bytes=64, offset=offset)

        at_raw00, at_vel20, at_wp0 = 0, 8192, 12288
        gather_list = held([P, S // 16], U16, "gather_list")
        scatter_list = held([P, S // 16], U16, "scatter_list")
        table = [held([P, T], I32, "table%d" % a) for a in range(K_PASSES)]
        table_planes = held([P, T], U8, "table_planes")
        wg_raw = [held([P, K_PASSES, H], U8, "wg_raw%d" % b) for b in range(R_PASSES)]
        wg_planes_raw = held([P, K_PASSES, H], U8, "wg_planes_raw")
        masses = held([P, S], F32, "masses")
        identity = held([P, P], F32, "identity")[:]
        bias_raw = held([P, PASS], F32, "bias_raw")
        bias_rows = held([P, PASS], F32, "bias_rows")
        bias = held([P, R_PASSES * PACK], F32, "bias")
        store = [held([P, T2], F32, "store0"), held([P, T2], F32, "store1")]
        v_codes0 = [held([P, BANK], U32, "v_codes0_low"), held([P, BANK], U32, "v_codes0_high")]
        v_codes1 = held([P, S], U32, "v_codes1")
        v_planes = held([P, S], U8, "v_planes")
        v_plane = [held([P, S], U8, "v_plane%d" % a) for a in range(K_PASSES)]

        def codes_of(a, first, count):
            if a == 0:
                return v_codes0[first // BANK][:, first % BANK : first % BANK + count]
            return v_codes1[:, first : first + count]

        scalar_banks = [psum.tile([P, BANK], F32, name="scalar_bank%d" % i) for i in range(4)]
        vector_banks = [psum.tile([P, BANK], F32, name="vector_bank%d" % i) for i in range(4)]
        turns = {"scalar": 0, "vector": 0, "vel": 0, "h": 0, "y": 0}

        def in_turn(kind, tiles):
            turns[kind] = turns[kind] + 1
            return tiles[(turns[kind] - 1) % len(tiles)]

        def words_of(planes):
            return planes[:].rearrange("p a n -> p (a n)").bitcast(I32)

        def load_table(a):
            words = tab_words[a].rearrange("p t i -> p (t i)").bitcast(I32)
            nc.sync.dma_start(out=table[a][:], in_=words)

        wv_raw = {}

        def load_wv(b, a, pieces, offset):
            name = "wv_raw%d%d" % (b, a)
            wv_raw[b, a] = held([P, PACK, PASS], F32, name) if offset is None else placed([P, PACK, PASS], F32, name, offset)
            rows = wv[a * PASS : (a + 1) * PASS, b * PASS : (b + 1) * PASS].rearrange("(p j) c -> p j c", j=PACK)
            step = PACK // pieces
            for j in range(0, PACK, step):
                nc.sync.dma_start(out=wv_raw[b, a][:, j : j + step, :], in_=rows[:, j : j + step, :])

        wp_raw = {}

        def load_wp(half):
            width = N // 2
            for b in range(R_PASSES):
                wp_raw[b, half] = held([P, PACK, width], F32, "wp_raw%d%d" % (b, half))
                rows = wp[b * PASS : (b + 1) * PASS, half * width : (half + 1) * width]
                rows = rows.rearrange("(q t i) n -> t q i n", t=PACK, i=8)
                for t in range(PACK):
                    nc.sync.dma_start(out=wp_raw[b, half][:, t, :], in_=rows[t])

        def gather(dst, window, first, count):
            picks = gather_list[:, first // 16 : (first + count) // 16]
            nc.vector.tensor_copy(out=dst, in_=window.indirect(picks))

        def gather_codes(a, first, count):
            gather(codes_of(a, first, count), table[a][:].bitcast(U32), first, count)

        def move_plane(a):
            for r in range(4):
                first = SCALE_ROW + 16 * a + r
                nc.sync.dma_start(
                    out=v_plane[a][r:P:32, :].bitcast(I32), in_=v_planes[first : first + 13 : 4, :].bitcast(I32)
                )

        def quantize(grouped, codes, scales):
            nc.vector.quantize_mx(out=codes.bitcast(FP8X4), scales=scales, in_=grouped)

        def quantized(width, name):
            return held([P, width], U32, name + "_codes"), held([P, width], U8, name + "_scales")

        wv_bf = {(b, a): held([P, PASS * PACK], BF16, "wv_bf%d%d" % (b, a)) for b in range(R_PASSES) for a in range(K_PASSES)}
        wv_q = {(b, a): quantized(PASS, "wv%d%d" % (b, a)) for b in range(R_PASSES) for a in range(K_PASSES)}
        wp_q = quantized(N_TILES * R_PASSES * P, "wp")
        h_codes = {
            (0, 0): placed([P, BANK], U32, "h_codes00", at_vel20),
            (0, 1): placed([P, BANK], U32, "h_codes01", at_wp0),
            (1, 0): held([P, BANK], U32, "h_codes10"),
            (1, 1): held([P, BANK], U32, "h_codes11"),
        }
        h_scales = [held([P, S], U8, "h_scales%d" % b) for b in range(R_PASSES)]
        h_pairs = [held([P, BANK * PACK], BF16, "h_pair%d" % i) for i in range(2)]

        def h_words(b, first, count):
            return h_codes[b, first // BANK][:, first % BANK : first % BANK + count]

        vel_tiles = [held([P, PACK, CHUNK], F32, "vel%d" % i) for i in range(4)]
        h_tiles = [held([P, CHUNK * PACK], BF16, "h_bf%d" % i) for i in range(3)]
        vel_behind = {(2, 0): placed([P, PACK, CHUNK], F32, "vel20", at_vel20)}
        h_behind = {(c, 0): h_pairs[c // 2][:, (c % 2) * CHUNK * PACK : (c % 2 + 1) * CHUNK * PACK] for c in range(CHUNKS)}
        wp_first = placed([P, CHUNK * PACK], BF16, "wp_bf0", at_wp0)
        wp_second = held([P, CHUNK * PACK], BF16, "wp_bf1")
        wp_last = held([P, 2 * CHUNK * PACK], BF16, "wp_bf23")
        y_behind = {}
        y_tiles = [held([P, S], F32, "y%d" % i) for i in range(4)]

        def cast_wv_scalar(b, a, codes=range(PACK)):
            dst = wv_bf[b, a][:].rearrange("p (t q u i j) -> p t q u j i", t=PACK, u=2, i=4, j=PACK)
            src = wv_raw[b, a][:].rearrange("p j (q t u i) -> p t q u j i", t=PACK, u=2, i=4)
            for t in codes:
                nc.scalar.copy(out=dst[:, t], in_=src[:, t])

        def cast_wv_vector(b, a, codes):
            nc.vector.tensor_copy(
                out=wv_bf[b, a][:].rearrange("p (t q i j) -> p q t j i", t=PACK, i=8, j=PACK)[:, :, codes],
                in_=wv_raw[b, a][:].rearrange("p j (q t i) -> p q t j i", t=PACK, i=8)[:, :, codes],
            )

        def quantize_wv(b, a):
            quantize(wv_bf[b, a][:], wv_q[b, a][0][:], wv_q[b, a][1][:])

        def round_wp(tiles, grouped, halves=range(R_PASSES)):
            for u, m in enumerate(tiles):
                for b in halves:
                    first = (u * R_PASSES + b) * PASS
                    nc.scalar.copy(
                        out=grouped[:, first : first + PASS].rearrange("p (c i t) -> p c t i", t=PACK, i=4),
                        in_=wp_raw[b, m // 2][:, :, (m % 2) * P : (m % 2 + 1) * P].rearrange("p t (c i) -> p c t i", i=4),
                    )

        def quantize_wp(tiles, grouped):
            cols = slice(tiles[0] * R_PASSES * P, (tiles[-1] + 1) * R_PASSES * P)
            quantize(grouped[:], wp_q[0][:, cols], wp_q[1][:, cols])

        wg_codes = [held([P, K_PASSES * 2 * PASS], U8, "wg_codes%d" % b) for b in range(R_PASSES)]
        wg_planes = held([P, K_PASSES * H], U8, "wg_planes")

        def load_wg(b):
            words = wg_words[:, :, b * H : (b + 1) * H].rearrange("a p n -> p a n")
            nc.sync.dma_start(out=wg_raw[b][:].bitcast(I32), in_=words.bitcast(I32))

        def permute_wg(b):
            nc.vector.tensor_copy(
                out=wg_codes[b][:].bitcast(I32).rearrange("p (a t q w) -> p a t q w", t=PACK, q=16, w=4),
                in_=words_of(wg_raw[b]).rearrange("p (a q t w) -> p a t q w", t=PACK, q=16, w=4),
            )

        def permute_wg_planes():
            nc.vector.tensor_copy(
                out=wg_planes[:].bitcast(I32).rearrange("p (g t q w) -> p g t q w", t=PACK, q=16, w=2),
                in_=words_of(wg_planes_raw).rearrange("p (g q t w) -> p g t q w", t=PACK, q=16, w=2),
            )

        def velocity_pass(banks, c, b, a, codes=range(PACK)):
            for t in codes:
                cols = slice(t * P, (t + 1) * P)
                nc.tensor.matmul_mx(
                    out=banks[t // 2][:, (t % 2) * CHUNK : (t % 2 + 1) * CHUNK],
                    lhsT=wv_q[b, a][0][:, cols].bitcast(FP8X4),
                    lhsT_scale=wv_q[b, a][1][:, cols],
                    rhs=codes_of(a, c * CHUNK, CHUNK).bitcast(FP8X4),
                    rhs_scale=v_plane[a][:, c * CHUNK : (c + 1) * CHUNK],
                    start=(a == 0 and t % 2 == 0),
                    stop=(a == K_PASSES - 1 and t % 2 == 1),
                )

        def gradient_pass(bank, first, b, a, opens=0):
            for t in range(PACK):
                col = a * PASS + t * P
                nc.tensor.matmul_mx(
                    out=bank[:, t * SUB : (t + 1) * SUB],
                    lhsT=wg_codes[b][:, 2 * col : 2 * (col + P)].bitcast(FP4X4),
                    lhsT_scale=wg_planes[:, a * H + b * PASS + t * P : a * H + b * PASS + (t + 1) * P],
                    rhs=codes_of(a, first, SUB).bitcast(FP8X4),
                    rhs_scale=v_plane[a][:, first : first + SUB],
                    start=(a == opens and t == 0),
                    stop=(a != opens and t == PACK - 1),
                )

        grad_of = {}
        vel_of = {}
        vels = {}
        ys = {}

        def grad(c, b, a):
            if a == 1:
                grad_of[c, b] = [in_turn("vector", vector_banks) for s in range(CHUNK // SUB)]
            for s, bank in enumerate(grad_of[c, b]):
                gradient_pass(bank, c * CHUNK + s * SUB, b, a, 1)

        def velo(c, b, a):
            if a == 0:
                vel_of[c, b] = [in_turn("scalar", scalar_banks) for pair in range(PACK // 2)]
            velocity_pass(vel_of[c, b], c, b, a)

        def velos(c, b):
            vel_of[c, b] = [in_turn("scalar", scalar_banks) for pair in range(PACK // 2)]
            for pair in range(PACK // 2):
                for a in range(K_PASSES):
                    velocity_pass(vel_of[c, b], c, b, a, range(2 * pair, 2 * pair + 2))

        def grads(c, b):
            grad_of[c, b] = [in_turn("vector", vector_banks) for s in range(CHUNK // SUB)]
            for s, bank in enumerate(grad_of[c, b]):
                for a in range(K_PASSES):
                    gradient_pass(bank, c * CHUNK + s * SUB, b, a)

        rounded = {}

        def empty(c, b):
            vel_banks = vel_of[c, b]
            vel = vel_behind[c, b] if (c, b) in vel_behind else in_turn("vel", vel_tiles)
            for t in range(PACK):
                nc.scalar.activation(
                    out=vel[:, t, :],
                    in_=vel_banks[t // 2][:, (t % 2) * CHUNK : (t % 2 + 1) * CHUNK],
                    func=IDENTITY,
                    bias=bias[:, PACK * b + t : PACK * b + t + 1],
                    scale=1.0,
                )
            vels[c, b] = vel

        early = held([P, PACK, BANK], F32, "early_grad")
        early_banks = []

        def early_gradients(a):
            for t in range(PACK):
                if a == 0:
                    early_banks.append(in_turn("scalar", scalar_banks))
                col = a * PASS + t * P
                nc.tensor.matmul_mx(
                    out=early_banks[t][:],
                    lhsT=wg_codes[0][:, 2 * col : 2 * (col + P)].bitcast(FP4X4),
                    lhsT_scale=wg_planes[:, a * H + t * P : a * H + (t + 1) * P],
                    rhs=codes_of(a, BANK, BANK).bitcast(FP8X4),
                    rhs_scale=v_plane[a][:, BANK:S],
                    start=(a == 0),
                    stop=(a == K_PASSES - 1),
                )
                if a == K_PASSES - 1:
                    nc.scalar.copy(out=early[:, t, :], in_=early_banks[t][:])

        def product(c, b):
            vel = vels[c, b]
            h = h_behind[c, b] if (c, b) in h_behind else in_turn("h", h_tiles)[:]
            rounded[c, b] = h
            if (c, b) not in grad_of:
                first = c * CHUNK - BANK
                nc.vector.tensor_tensor(
                    out=h.rearrange("p (e i t) -> p e t i", t=PACK, i=4),
                    in0=early[:, :, first : first + CHUNK].rearrange("p t (e i) -> p e t i", i=4),
                    in1=vel[:].rearrange("p t (e i) -> p e t i", i=4),
                    op=MULT,
                )
                return
            grad_banks = grad_of[c, b]
            for s, bank in enumerate(grad_banks):
                nc.vector.tensor_tensor(
                    out=h[:, s * SUB * PACK : (s + 1) * SUB * PACK].rearrange("p (e i t) -> p e t i", t=PACK, i=4),
                    in0=bank[:].rearrange("p (t e i) -> p e t i", t=PACK, i=4),
                    in1=vel[:, :, s * SUB : (s + 1) * SUB].rearrange("p t (e i) -> p e t i", i=4),
                    op=MULT,
                )
            rounded[c, b] = h

        def quantize_h(c, b):
            picks = slice(c * CHUNK, (c + 1) * CHUNK)
            quantize(rounded[c, b], h_words(b, c * CHUNK, CHUNK), h_scales[b][:, picks])

        def quantize_pair(half):
            quantize(h_pairs[half][:], h_words(0, half * BANK, BANK), h_scales[0][:, half * BANK : (half + 1) * BANK])

        def project(m, first, count, later=False):
            y = y_behind[m, first] if (m, first) in y_behind else in_turn("y", y_tiles)
            done = 0
            while done < count:
                width = min(BANK - (first + done) % BANK, count - done)
                picks = slice(first + done, first + done + width)
                bank = in_turn("scalar", scalar_banks)
                for b in reversed(range(R_PASSES)):
                    nc.tensor.matmul_mx(
                        out=bank[:, 0:width],
                        lhsT=wp_q[0][:, (m * R_PASSES + b) * P : (m * R_PASSES + b + 1) * P].bitcast(FP8X4),
                        lhsT_scale=wp_q[1][:, (m * R_PASSES + b) * P : (m * R_PASSES + b + 1) * P],
                        rhs=h_words(b, first + done, width).bitcast(FP8X4),
                        rhs_scale=h_scales[b][:, picks],
                        start=(b == R_PASSES - 1),
                        stop=(b == 0),
                    )
                nc.scalar.copy(out=y[:, done : done + width], in_=bank[:, 0:width])
                done = done + width
            ys[m, first] = y
            if not later:
                scatter(m, first, count)

        def scatter(m, first, count, made=None):
            made = first if made is None else made
            y = ys[m, made][:, first - made : first - made + count]
            places = scatter_list[:, first // 16 : (first + count) // 16]
            nc.vector.tensor_tensor(
                out=store[m % 2][:].indirect(places), in0=y, in1=masses[:, first : first + count], op=MULT
            )
            if first + count == S:
                nc.sync.dma_start(out=out[m * P : (m + 1) * P, :], in_=store[m % 2][:])

        nc.sync.dma_start(gather_list[:], offs)
        nc.sync.dma_start(
            out=table_planes[SCALE_ROW:P, :].bitcast(I32), in_=tab_scales.rearrange("a q n -> (a q) n").bitcast(I32)
        )
        load_table(0)
        nc.vector.memset(table_planes[0:SCALE_ROW, :].bitcast(I32), 0)
        load_wg(0)
        nc.vector.memset(words_of(wg_planes_raw), 0)
        for r in range(4):
            nc.sync.dma_start(
                out=wg_planes_raw[r:P:32, :, :].bitcast(I32),
                in_=wg_scales[:, r:16:4, :].rearrange("a q n -> q a n").bitcast(I32),
            )
        load_table(1)
        for a in range(K_PASSES):
            nc.vector.memset(v_plane[a][:].bitcast(I32), 0)
        nc.scalar.dma_start(out=bias_raw[0:R_PASSES, :], in_=bv.rearrange("(b c) -> b c", b=R_PASSES))
        nc.gpsimd.memset(bias_rows[:], 0.0)
        nc.scalar.copy(
            out=bias_rows[0:R_PASSES, :].rearrange("b (t q i) -> b t q i", t=PACK, i=8),
            in_=bias_raw[0:R_PASSES, :].rearrange("b (q t i) -> b t q i", t=PACK, i=8),
        )
        make_identity(nc, identity)
        for tile in store:
            for first in range(0, T2, T2 // 2):
                nc.gpsimd.memset(tile[:, first : first + T2 // 2], 0.0)
        gather(v_planes[:], table_planes[:], 0, S)
        gather_codes(0, BANK, BANK)
        gather_codes(0, 0, BANK)
        move_plane(0)
        load_wv(0, 0, 1, None)
        move_plane(1)
        load_wv(0, 1, 1, None)
        load_wv(1, 0, 1, None)
        load_wg(1)
        load_wv(1, 1, 1, None)
        load_wp(0)
        nc.sync.dma_start(scatter_list[:], offs2)
        nc.sync.dma_start(out=masses[:], in_=wgo)
        load_wp(1)
        bias_ps = vector_banks[3][:]
        for t in range(PACK):
            nc.tensor.transpose(bias_ps[:, t * P : (t + 1) * P], bias_rows[:, t * P : (t + 1) * P], identity)
        nc.scalar.activation(
            out=bias[:].rearrange("p (b t) -> p t b", t=PACK),
            in_=bias_ps[:].rearrange("p (t c) -> p t c", c=P)[:, :, 0:R_PASSES],
            func=IDENTITY,
        )
        permute_wg(0)
        permute_wg_planes()
        early_gradients(0)
        gather_codes(1, BANK, BANK)
        cast_wv_scalar(0, 0, range(0, 1))
        early_gradients(1)
        gather_codes(1, 0, BANK)
        grad(0, 0, 1)
        grad(1, 0, 1)
        cast_wv_vector(0, 0, slice(1, 4))
        grad(0, 0, 0)
        grad(1, 0, 0)
        quantize_wv(0, 0)
        cast_wv_scalar(0, 1, range(0, 1))
        cast_wv_vector(0, 1, slice(1, 4))
        velo(0, 0, 0)
        velo(1, 0, 0)
        quantize_wv(0, 1)
        velo(0, 0, 1)
        velo(1, 0, 1)
        cast_wv_scalar(1, 0, range(0, 1))
        empty(0, 0)
        empty(1, 0)
        cast_wv_vector(1, 0, slice(1, 4))
        permute_wg(1)
        quantize_wv(1, 0)
        velos(2, 0)
        product(0, 0)
        grads(0, 1)
        product(1, 0)
        cast_wv_scalar(1, 1, range(0, 2))
        cast_wv_vector(1, 1, slice(2, 4))
        empty(2, 0)
        velos(3, 0)
        for u in range(2):
            cols = slice(u * 2 * P, (u + 1) * 2 * P)
            quantize(wv_bf[1, 1][:, u * 2 * PASS : (u + 1) * 2 * PASS], wv_q[1, 1][0][:, cols], wv_q[1, 1][1][:, cols])
        velos(0, 1)
        empty(3, 0)
        round_wp([0], wp_first, [0])
        product(2, 0)
        empty(0, 1)
        scalar_banks[2:4], vector_banks[2:4] = vector_banks[2:4], scalar_banks[2:4]
        velos(1, 1)
        grads(1, 1)
        round_wp([0], wp_first, [1])
        product(3, 0)
        quantize_pair(0)
        product(0, 1)
        empty(1, 1)
        quantize_wp([0], wp_first)
        quantize_h(0, 1)
        velos(2, 1)
        scalar_banks[2:4], vector_banks[0:2] = vector_banks[0:2], scalar_banks[2:4]
        project(0, 0, CHUNK, True)
        grads(2, 1)
        quantize_pair(1)
        product(1, 1)
        empty(2, 1)
        round_wp([1], wp_second)
        scatter(0, 0, CHUNK)
        quantize_h(1, 1)
        velos(3, 1)
        project(0, CHUNK, CHUNK, True)
        grads(3, 1)
        product(2, 1)
        quantize_wp([1], wp_second)
        empty(3, 1)
        quantize_h(2, 1)
        project(0, BANK, CHUNK, True)
        project(1, 0, CHUNK, True)
        scatter(0, CHUNK, CHUNK)
        product(3, 1)
        round_wp([2, 3], wp_last)
        scatter(0, BANK, CHUNK)
        quantize_h(3, 1)
        project(0, BANK + CHUNK, CHUNK, True)
        scatter(1, 0, CHUNK)
        project(1, CHUNK, S - CHUNK, True)
        scatter(0, BANK + CHUNK, CHUNK)
        quantize_wp([2, 3], wp_last)
        scatter(1, CHUNK, S - CHUNK)
        for m in range(2, N_TILES):
            project(m, 0, S)
